import numpy as np, ml_dtypes
CORES = [5,29,101,125,133,157,229,253]
N = 8
BF = ml_dtypes.bfloat16
S, R, NF, PH, LB, RO = 1024, 4096, 256, 512, 9, 4
def place(s, p):
    return ((s * p >> 4) + s + 37 * p) & (R - 1)
def records(rng):
    st = ((np.arange(8)[None, :] + rng.integers(0, 3, (N, 1))) % 3)[:, :, None, None]
    lo = np.where(st == 0, 0, np.where(st == 1, 64 * rng.integers(0, 4, (N, 8, 1, R)), 200 * (rng.random((N, 8, 1, R)) < 0.35))).astype(np.int32)
    span = np.where(st == 0, 256, np.where(st == 1, 64, 56)).astype(np.float32)
    x = np.minimum(lo + (rng.random((N, 8, 16, R), dtype=np.float32) * span).astype(np.int32), 255)
    u = rng.random((N, 8, 16, 1))
    th = np.where(st == 0, 1000 + 700 * u, np.where(st == 1, 256 + 2000 * u, 450 + 1150 * u)).astype(np.int64)
    return x, th
def parts(rng):
    var = rng.choice(np.array([0.2, 0.35, 0.5]), (N, 8, 1, 1)); emp = rng.choice(np.array([0.2, 0.45, 0.7]), (N, 8, 1, 1))
    tk = rng.integers(0, S, (N, 8, 16, S)) + S * (rng.random((N, 8, 16, S)) < var)
    fr = np.where(rng.random((N, 8, 16, NF)) < emp, -1, rng.integers(0, S * PH, (N, 8, 16, NF)))
    return tk, fr, rng.integers(0, S, (N, 8, NF)), rng.integers(0, NF, (N, 8, NF)), rng.integers(0, S, (N, 8, NF))
def pack(x, tk, fr, th, s, f, c):
    return {"x": np.ascontiguousarray(x.reshape(N, 128, R)).astype(np.float32).astype(BF), "sk": np.ascontiguousarray(tk.reshape(N, 128, S)).astype(np.int32),
            "fr": np.ascontiguousarray(fr.reshape(N, 128, NF)).astype(np.int32), "th": np.ascontiguousarray(th.reshape(N, 128, 1)).astype(np.int32),
            "gs": s.astype(np.int32), "gf": f.astype(np.int32), "gcl": c.astype(np.int32)}
def setup_inputs(rng):
    x, th = records(rng); tk, fr, s, f, c = parts(rng)
    return pack(x, tk, fr, th, s, f, c)
def setup_inputs_spread(rng):
    amp = np.exp2(8 * rng.random((N, 8, 1, R))).astype(np.float32)
    x = np.minimum((rng.random((N, 8, 16, R), dtype=np.float32) * amp).astype(np.int32), 255)
    x = np.where(rng.random((N, 8, 1, R)) < 0.0625, 255 - x, x)
    th = np.minimum(np.exp2(12 * rng.random((N, 8, 16, 1))).astype(np.int64), 4080)
    u = rng.random((N, 8, 16, S)); tk = np.minimum((2 * S * u * np.sqrt(u)).astype(np.int64), 2 * S - 1)
    v = rng.random((N, 8, 16, NF)); fr = np.where(rng.random(v.shape) < 0.3 * rng.random((N, 8, 1, 1)) + 0.1, -1, np.minimum((S * PH * v * v).astype(np.int64), S * PH - 1))
    w = rng.random((3, N, 8, NF)); w = w * w
    return pack(x, tk, fr, th, np.minimum((S * w[0]).astype(np.int64), S - 1), np.minimum((NF * w[1]).astype(np.int64), NF - 1), np.minimum((S * w[2]).astype(np.int64), S - 1))
def setup_inputs_ends(rng):
    one = rng.random((N, 8, 1, R)) < 0.5; each = rng.random((N, 8, 16, R)) < 0.5
    x = 255 * np.where(rng.random((N, 8, 1, R)) < 0.25, each, one).astype(np.int64)
    tk = (2 * S - 1) * rng.integers(0, 2, (N, 8, 16, S)); fr = np.where(rng.integers(0, 2, (N, 8, 16, NF)) == 1, S * PH - 1, -1)
    s = (S - 1) * rng.integers(0, 2, (N, 8, NF)); f = (NF - 1) * rng.integers(0, 2, (N, 8, NF)); c = (S - 1) * rng.integers(0, 2, (N, 8, NF))
    th = np.full((N, 8, 16, 1), 4080, np.int64)
    for a in range(N):
        for g in range(8):
            if g == 7: z = rng.permutation(15)[:9 if a % 2 == 0 else 7]
            else: z = rng.permutation(16)[:16 if g == 6 else 8]
            th[a, g, z, 0] = 0
    s[:, :, NF - 1] = S - 1; f[:, :, NF - 1] = NF - 1; c[:, :, NF - 1] = 0
    tk[::2, :, :, S - 1] = 2 * S - 1; tk[::2, :, :, 0] = 0; tk[:, 7, :, S - 1] = 2 * S - 1; tk[:, 7, :, 0] = 0
    x[..., place(S - 1, PH - 1)] = 255; x[..., place(S - 1, NF - 1)] = 255; x[..., place(0, NF - 1)] = 0
    return pack(x, tk, fr, th, s, f, c)
def setup_inputs_corners(rng):
    x, th = records(rng); tk, fr, s, f, c = parts(rng); i = np.arange(NF); even = i % 2 == 0
    near = np.array([[3, 21], [21, 3], [5, 19], [19, 5], [7, 9], [9, 7]])
    for a in range(N):
        o = rng.permutation(8)
        tk[a, o[0]] = tk[a, o[0]] & (S - 1); fr[a, o[0]] = -1
        tk[a, o[1]] = (tk[a, o[1]] & (S - 1)) + S; fr[a, o[1]] = -1
        tk[a, o[2]] = (tk[a, o[2]] & (S - 1)) + S
        fr[a, o[2]] = PH * rng.integers(0, S, (16, NF)) + np.where(rng.random((16, NF)) < 0.5, i, NF + i)
        f[a, o[3]] = i; fr[a, o[3]] = np.where(i % 2 == 0, -1, rng.integers(0, S * PH, (16, NF)))
        f[a, o[4]] = rng.choice(np.array([0, NF - 1]), NF); s[a, o[4]] = rng.choice(np.array([0, S - 1]), NF); c[a, o[4]] = np.where(rng.random(NF) < 0.5, s[a, o[4]], S - 1 - s[a, o[4]])
        fr[a, o[4]] = np.where(rng.random((16, NF)) < 0.4, -1, PH * rng.choice(np.array([0, S - 1]), (16, NF)) + rng.choice(np.array([0, NF - 1, NF, PH - 1]), (16, NF)))
        th[a, o[5]] = 4080; th[a, o[6]] = 0; th[a, o[7]] = 4080; th[a, o[7], rng.permutation(16)[:8]] = 0
        f[a, o[5]] = np.where(even, i, f[a, o[5]]); c[a, o[5]] = np.where(even, s[a, o[5]], c[a, o[5]]); fr[a, o[5]] = np.where(even, -1, fr[a, o[5]])
        pq = near[rng.integers(0, 6, NF)]
        s[a, o[6]] = np.where(even, S - pq[:, 0], s[a, o[6]]); c[a, o[6]] = np.where(even, S - pq[:, 1], c[a, o[6]])
    return pack(x, tk, fr, th, s, f, c)
def setup_inputs_ties(rng):
    v, th = records(rng); tk, fr, s, f, c = parts(rng)
    x = np.broadcast_to(60 * rng.integers(0, 5, (N, 8, 1, R)), (N, 8, 16, R)).copy()
    th = rng.choice(np.array([959, 960, 961, 1919, 1920, 1921]), (N, 8, 16, 1))
    off = rng.integers(0, 4, (N, 2, 16, R)) * (rng.random((N, 2, 1, R)) < 0.5)
    x[:, 1::4] = np.abs(255 * rng.integers(0, 2, (N, 2, 1, R)) - off)
    lev = np.array([0, 0, 0, 24, 24, 24, 4048, 4056, 4060, 4064, 4078, 4079, 4079, 4079, 4080, 4080])
    th[:, 1::4] = lev[np.argsort(rng.random((N, 2, 16, 1)), axis=2)]
    few = rng.integers(0, S, (N, 4, 3)); which = rng.integers(0, 3, (2, N, 4, NF))
    s[:, ::2] = np.take_along_axis(few, which[0], 2); c[:, ::2] = np.take_along_axis(few, which[1], 2); f[:, ::2] = rng.integers(0, 4, (N, 4, NF))
    return pack(x, tk, fr, th, s, f, c)
def check_inputs(d):
    bad = []
    for k, lo, hi in (("x", 0, 255), ("sk", 0, 2 * S - 1), ("fr", -1, S * PH - 1), ("th", 0, 4080), ("gs", 0, S - 1), ("gf", 0, NF - 1), ("gcl", 0, S - 1)):
        if k not in d: bad.append("no " + k); continue
        v = np.asarray(d[k]).astype(np.float64)
        if not (np.min(v) >= lo and np.max(v) <= hi): bad.append("range of " + k)
        elif np.any(v != np.floor(v)): bad.append("whole numbers in " + k)
    return bad
def reference(x, sk, fr, th, gs, gf, gcl):
    X = x.astype(np.float32).astype(np.int32).reshape(N, 8, 16, R); T = sk.astype(np.int64).reshape(N, 8, 16, S); lim = th.astype(np.int64).reshape(N, 8, 16, 1)
    own = fr.astype(np.int64).reshape(N, 8, 16, NF); F = np.concatenate([own, own], axis=3)
    i = np.arange(NF); mark = np.zeros((N, 8, 16, NF), bool); A = np.zeros((N, NF), np.int64)
    s = gs.astype(np.int64); f = gf.astype(np.int64); c = gcl.astype(np.int64); h = np.zeros_like(s) + i
    s0 = s; f0 = f; c0 = c
    def molecules(a, b):
        v = np.take_along_axis(T, a[:, :, None, :], 3); w = np.take_along_axis(F, b[:, :, None, :], 3)
        return np.where((v >= S) & (w >= 0), w, (v & (S - 1)) * PH + b[:, :, None, :]), (v >= S) & (w < 0)
    def pick(m):
        return np.take_along_axis(X, place(m >> LB, m & (PH - 1)).reshape(N, 8, 1, 16 * NF), 3)
    for rnd in range(RO):
        goal, _ = molecules(s, f); clause, hole = molecules(c, h)
        free = hole & (h == i)[:, :, None, :]; clause = np.where(free, goal, clause)
        D = np.add.reduce(np.abs(pick(goal) - pick(clause)), axis=2).astype(np.int64).reshape(N, 8, 16, NF)
        over = D > lim; clash = np.add.reduce(over.astype(np.int64), axis=2) >= 8 + (A & 1)[:, None, :]
        m = np.argmax(np.where(over, -1, D), axis=2)[:, :, None, :]
        gm = np.take_along_axis(goal, m, 2)[:, :, 0]; cm = np.take_along_axis(clause, m, 2)[:, :, 0]
        dm = np.take_along_axis(D, m, 2)[:, :, 0]; tm = np.take_along_axis(np.broadcast_to(lim, D.shape), m, 2)[:, :, 0]
        save = ~clash & (2 * dm < tm)
        bind = free & ~clash[:, :, None, :]
        own = np.where(mark & clash[:, :, None, :], -1, np.where(bind, goal, own))
        mark = (mark | bind) & ~(clash | save)[:, :, None, :]
        nxt = ((c0 * s0 >> 5) + c0 + 1) & (S - 1)
        s = np.where(clash, s0, gm >> LB); f = np.where(clash, f0, gm & (PH - 1))
        c = np.where(clash, nxt, cm >> LB); h = np.where(clash, i, cm & (PH - 1))
        s0 = np.where(save, s, s0); f0 = np.where(save, f, f0); c0 = np.where(clash, nxt, np.where(save, c, c0))
        A = np.add.reduce(clash.astype(np.int64), axis=1)
        F = np.concatenate([own, F[..., NF:]], axis=3)
        if rnd < RO - 1:
            d = 1 + rnd % (N - 1); col = np.take_along_axis(F, f[:, :, None, :], 3)
            F = np.concatenate([own, np.roll(col, d, axis=0)], axis=3); s = np.roll(s, d, axis=0); f = np.zeros_like(s) + NF + i
    return {"yf": np.where(own < 0, -1, 2 * own + mark).reshape(N, 128, NF).astype(np.float32), "yg": (PH * s + f).astype(np.float32), "yc": (PH * c + h).astype(np.float32),
            "ysg": (PH * s0 + f0).astype(np.float32), "yk": c0.astype(np.float32)}

@@ -1,0 +1,555 @@
+from concourse.bass import DstId, RemoteDMATransfer
+from concourse.mybir import AluOpType as OP, ActivationFunctionType as AF
+
+N = 8
+RO = 4
+NEG = -8388608.0
+B = 1 << 21
+KE = 592 * 1024 + 16
+PARTS = [(0, 4), (4, 8), (8, 12), (12, 14), (14, 16)]
+SUMS = [(0, 4, "ab0"), (4, 8, "ab1"), (8, 12, "ab2"), (12, 16, "ab3 ab4")]
+HELP = [[], [4], [4], []]
+LAT, GAP, PATIENCE = 0.14, 0.8, 0.3
+HOP = 8
+LOADS = ["l_gs0", "l_gs1", "l_gf0", "l_gf1", "l_gc0", "l_gc1", "l_gfr", "l_fr", "l_sk", "l_th", "l_x0", "l_x1"]
+
+
+def f32(*s):
+    return ("sbuf", [128] + list(s), "float32")
+
+
+def i32(*s):
+    return ("sbuf", [128] + list(s), "int32")
+
+
+def b16(*s):
+    return ("sbuf", [128] + list(s), "bfloat16")
+
+
+def u16(*s):
+    return ("sbuf", [128] + list(s), "uint16")
+
+
+SCRATCH = {
+    "XR": b16(4096), "SKI": i32(1024), "SKU": f32(1024), "SKV": f32(1024), "FRI": i32(256), "FRQ": i32(256), "OW": f32(256),
+    "BASE": f32(256), "MK": f32(256), "YA": f32(256), "FLG": f32(256), "F0": f32(528), "F1": f32(528), "F2": f32(528), "F3": f32(528),
+    "COL0": f32(272), "COL1": f32(272), "COL2": f32(272), "RB0": f32(136), "RB2": f32(136),
+    "TT": i32(96), "TX": i32(3, 2, 16), "TA": f32(3, 16), "TB": f32(3, 16), "TL": f32(3, 16),
+    "GFR": ("sbuf", [8, 256], "int32"), "GFB": ("sbuf", [8, 256], "bfloat16"), "R16": ("sbuf", [16, 256], "bfloat16"), "R8": ("sbuf", [8, 128], "bfloat16"),
+    "THI": i32(1), "THF": f32(1), "THD": f32(256), "THA": f32(256), "THB": f32(256), "THW": i32(256),
+    "ONEB": b16(256), "ONEF": f32(4, 2, 16), "ONEG": f32(128), "IDF": f32(128), "IDB": b16(128),
+    "BLKF": f32(128), "BLKH": ("sbuf", [128, 128], "float16"), "NPR": ("sbuf", [1, 512], "bfloat16"),
+    "ONEH": ("sbuf", [1, 128], "float16"), "NIH": ("sbuf", [1, 256], "float16"),
+    "DIAG": b16(256), "DIF": f32(16), "SQ": b16(2048), "TQ": b16(2048), "SWP": f32(4, 4, 2, 16),
+    "KB": b16(256), "RST": b16(512), "IOT": f32(256), "BIA": f32(256), "BG": f32(256),
+    "C16": f32(16), "PIO": i32(16), "PM": i32(16), "LIK": f32(16), "MUI": i32(16), "MU1": f32(16), "MU0": f32(16),
+    "BC15": u16(16), "SL": u16(16), "FL": u16(16), "CL": u16(16), "HL": u16(16), "BCC": u16(16),
+    "CG": f32(256), "VC": f32(256), "WC": f32(256), "XC": f32(256), "MG": i32(256),
+    "XI": i32(512), "PI": i32(512), "QI": i32(512), "ZI": i32(512), "RI": i32(512), "RL": u16(512),
+    "U": b16(4096), "DB": b16(4096), "AB": b16(16, 16, 16), "XF": f32(512), "XT": f32(16, 2, 16),
+    "NOV": b16(256), "NS": b16(256), "SV": b16(256), "SB": b16(16), "S2": b16(2, 16), "KY": f32(256), "KM": f32(256), "MASK": b16(256),
+    "MX": f32(512), "SC": f32(512), "EH": ("sbuf", [128, 256], "float16"), "HA": f32(256), "WN": f32(256),
+    "LF": f32(512), "LI": i32(256), "SAV": i32(32),
+    "FLD": f32(4, 2, 16), "FLT": f32(4, 2, 16), "FO": f32(4, 16), "FP": f32(4, 16), "YO": f32(256), "YM": f32(256),
+    "P0": ("psum", [128, 2, 16, 16], "float32"), "P1": ("psum", [128, 2, 8, 2, 16], "float32"), "P2": ("psum", [128, 512], "float32"),
+    "P3": ("psum", [128, 2, 16, 16], "float32"), "P4": ("psum", [128, 512], "float32"), "P5": ("psum", [128, 512], "float32"),
+    "P6": ("psum", [128, 512], "float32"), "P7": ("psum", [128, 2, 8, 2, 16], "float32"),
+}
+SEMAPHORES = LOADS + ["v", "s", "pe", "gq", "out", "sent", "in0", "in2", "arr0", "arr1", "arr2"]
+
+
+def routes(topo, a, b):
+    if topo.may_write(a, b):
+        return []
+    own = [c for c in topo.cores_of(a) if c != a and topo.may_write(c, b)]
+    return [[c for c in own if topo.die(c) == die][0] for die in sorted(set(topo.die(c) for c in own))]
+
+
+def only(engines, n):
+    return sum(1 << e for e in engines[:n])
+
+
+def hand(ins):
+    return None
+
+
+SMALL = "sl fl cl hl thr sav cols pm mui mu0 mu1 lik bc15 bcc tl ta tb s2a s2b fo fp npr thf oneh dif fld0 fld1 fle0 fle1".split()
+LONG = {"cg": .37, "mask": .37, "eh": .37, "col": .37, "wc": .39, "vc": .39, "xt": .44, "skv": .44, "zic": .44, "zig0": .23, "zig1": .23,
+        "xf": 1.05, "skf": 1.9, "ns": .13, "sku0": .44, "sku1": .44, "tq": .13, "sq": .1, "idf": .4, "r8": .4, "r16": .6, "c16": .16, "pio": .16,
+        "iot": .55, "kb": .55, "bia": .55, "sw0": .3, "sw1": .3, "sw2": .3, "sw3": .3}
+
+
+def guess(q, key):
+    if key in LONG:
+        return LONG[key]
+    if key in SMALL or key[0] in "li" and key[1:].isdigit():
+        return 0.075
+    if key[0] == "u" and key[1:].isdigit() or key[:2] == "db" and key[2:].isdigit():
+        a, b = PARTS[int(key[-1])]
+        return 0.06 + 0.32 * (b - a)
+    if key[:2] == "ab":
+        a, b = PARTS[int(key[-1])]
+        return 0.02 + 0.213 * (b - a)
+    return 0.13 if key[-2:] in ("g0", "g1") else 0.235
+
+
+def plan(nodes):
+    m = len(nodes)
+    succ = [[] for _ in range(m)]
+    left = [len(x["deps"]) for x in nodes]
+    for n, x in enumerate(nodes):
+        for d in x["deps"]:
+            succ[d].append(n)
+    way = [0.0] * m
+    for n in range(m - 1, -1, -1):
+        way[n] = nodes[n]["cost"] + nodes[n]["lat"] + max([way[k] for k in succ[n]] + [0.0])
+    start = [0.0] * m
+    free, can, order = {}, {}, []
+    for n in range(m):
+        if not left[n]:
+            can.setdefault(nodes[n]["q"], []).append(n)
+    while len(order) < m:
+        best = None
+        for q in can:
+            if can[q]:
+                t = max(free.get(q, 0.0), min(start[n] for n in can[q]))
+                if best is None or t < best[0]:
+                    best = (t, q)
+        t, q = best
+        now = [n for n in can[q] if start[n] <= t + 1e-9]
+        n = max(now, key=lambda k: (way[k], -k))
+        for k in sorted(can[q], key=lambda k: -way[k]):
+            if way[k] > way[n] + GAP and start[k] < t + PATIENCE * nodes[n]["cost"]:
+                n = k
+                break
+        t = max(t, start[n])
+        can[q].remove(n)
+        order.append((t, len(order), n))
+        free[q] = t + nodes[n]["cost"]
+        for k in succ[n]:
+            left[k] -= 1
+            start[k] = max(start[k], t + nodes[n]["cost"] + nodes[n]["lat"])
+            if not left[k]:
+                can.setdefault(nodes[k]["q"], []).append(k)
+    return [n for _, _, n in sorted(order)]
+
+
+def relay(g, core, T, topo):
+    sent = 0
+    for t in range(RO - 1):
+        d = 1 + t % (N - 1)
+        for r in range(N):
+            a, b = T.cores[r], T.cores[(r + d) % N]
+            if a not in topo.cores_of(core):
+                continue
+            rel = routes(topo, a, b)
+            if core not in rel:
+                continue
+            k, w = rel.index(core), 272 // len(rel)
+            g.wait_ge(T.sem["in%d" % t], HOP)
+            rid, pid = topo.addr(b, core)
+            g.remote_dma(T["F%d" % (t + 1)][:, 256 + k * w:256 + (k + 1) * w], T["RB%d" % t][:, 0:w], T.sem["arr%d" % t], T.sem.sent,
+                         pid, rid, topo.mask(core, b))
+            sent += len(topo.engines(core, b))
+    if sent:
+        g.wait_ge(T.sem.sent, sent)
+
+
+def rank_program(g, core, T, topo):
+    rank = T.rank_of(core)
+    if rank is None:
+        return relay(g, core, T, topo)
+    ENG = {"v": g.vector, "s": g.scalar, "pe": g.tensor, "gq": g, "sync": g.sync}
+    V = g.vector
+    nodes, lastw, readers = [], {}, {}
+
+    def add(q, emit, reads, writes, cost, lat, sem, inc):
+        reads, writes = reads.split(), writes.split()
+        deps = set(lastw[k] for k in reads + writes if k in lastw)
+        for k in writes:
+            deps |= readers.get(k, set())
+        n = len(nodes)
+        nodes.append({"q": q, "emit": emit, "deps": deps, "cost": cost, "lat": lat, "sem": sem, "inc": inc})
+        for k in writes:
+            lastw[k] = n
+            readers[k] = set()
+        for k in reads:
+            readers.setdefault(k, set()).add(n)
+
+    def run(q, fn, reads, writes, *a, **kw):
+        add(q, lambda: fn(*a, **kw), reads, writes, guess(q, writes.split()[0]), LAT, q, 1)
+
+    def load(q, out, in_, sem, key, reads=""):
+        add(q, lambda: ENG[q].dma_start(out, in_), reads, key, 0.06, 1.9, sem, 16)
+
+    def issue():
+        cnt, seen, tok = {}, {}, {}
+        for n in plan(nodes):
+            x = nodes[n]
+            q = x["q"]
+            need = {}
+            for d in x["deps"]:
+                if d in tok and not (q == "pe" and tok[d][0] == "pe"):
+                    need[tok[d][0]] = max(need.get(tok[d][0], 0), tok[d][1])
+            for sm in sorted(need):
+                if q in ENG and seen.get((q, sm), 0) < need[sm]:
+                    ENG[q].wait_ge(T.sem[sm], need[sm])
+                    seen[(q, sm)] = need[sm]
+            ins = x["emit"]()
+            if x["sem"]:
+                cnt[x["sem"]] = cnt.get(x["sem"], 0) + x["inc"]
+                tok[n] = (x["sem"], cnt[x["sem"]])
+                if ins is not None:
+                    ins.then_inc(T.sem[x["sem"]], x["inc"])
+        return cnt, seen
+
+    def tt(reads, w, out, a, b, op):
+        run("v", V.tensor_tensor, reads, w, out, a, b, op)
+
+    def ts(reads, w, out, a, s1, op0, s2=None, op1=None):
+        if op1 is None:
+            run("v", V.tensor_scalar, reads, w, out, a, s1, None, op0)
+        else:
+            run("v", V.tensor_scalar, reads, w, out, a, s1, s2, op0, op1)
+
+    def cp(reads, w, out, a):
+        run("v", V.tensor_copy, reads, w, out, a)
+
+    def scan(reads, w, out, d0, d1, op):
+        run("v", V.tensor_tensor_scan, reads, w, out, d0, d1, 0.0, OP.mult, op)
+
+    def act(reads, w, out, a, func=AF.Copy, **kw):
+        run("s", g.scalar.activation, reads, w, out, a, func, **kw)
+
+    def mms(reads, w, calls):
+        def emit():
+            for c in calls:
+                ins = g.tensor.matmul(*c)
+            return ins
+        add("pe", emit, reads, w, 0.9 if len(calls) == 16 else 1.7 if len(calls) == 4 else 0.25 * len(calls), LAT, "pe", 1)
+
+    def lf(j, n=1):
+        return T.LF[:, 16 * j:16 * j + 16 * n]
+
+    def li(j, n=1):
+        return T.LI[:, 16 * j:16 * j + 16 * n]
+
+    SG, SCL = T.SAV[:, 0:16], T.SAV[:, 16:32]
+    ONES = T.ONEB[0:1, 0:128]
+
+    load("sync", T.TT[:, 0:16], T.gs[:], "l_gs0", "tt0")
+    load("sync", T.TT[:, 16:32], T.gs[:], "l_gs1", "tt1")
+    load("sync", T.SKI[:], T.sk[:], "l_sk", "ski")
+    load("sync", T.GFR[:], T.gf[:], "l_gfr", "gfr")
+    load("sync", T.XR[:, 592:4096], T.x[:, 0:3504], "l_x0", "xr0")
+    load("s", T.TT[:, 32:48], T.gf[:], "l_gf0", "tt2")
+    load("s", T.TT[:, 48:64], T.gf[:], "l_gf1", "tt3")
+    load("s", T.FRI[:], T.fr[:], "l_fr", "fri")
+    load("s", T.TT[:, 64:80], T.gcl[:], "l_gc0", "tt4")
+    load("s", T.TT[:, 80:96], T.gcl[:], "l_gc1", "tt5")
+    load("s", T.XR[:, 0:592], T.x[:, 3504:4096], "l_x1", "xr1")
+    load("s", T.THI[:], T.th[:], "l_th", "thi")
+    XRK = "xr0 xr1 "
+
+    run("v", V.memset, "", "oneb", T.ONEB[:], 1.0)
+    run("v", V.memset, "", "onef", T.ONEF[:], 1.0)
+    run("v", V.memset, "", "oneg", T.ONEG[:], 1.0)
+
+    def sel(o, i, p, base, r, w):
+        run("gq", g.affine_select, r, w, o, i, p, OP.is_equal, 0.0, base, 1)
+
+    def iota(o, p, base, cm, w):
+        run("gq", g.iota, "", w, o, p, base, cm, allow_small_or_imprecise_dtypes=True)
+    iota(T.C16[:], [[16, 16]], KE, 0, "c16")
+    iota(T.PIO[:], [[0, 16]], 0, 1, "pio")
+    sel(T.R8[:], T.ONEB[0:8, 0:128], [[-1, 8], [0, 16]], 0, "oneb", "r8")
+    sel(T.R16[:], T.ONEB[0:16, :], [[0, 16], [-1, 16]], 0, "oneb", "r16")
+    iota(T.IOT[:], [[1, 256]], 0, 0, "iot")
+    iota(T.KB[:], [[0, 16], [-1, 16]], 15, 0, "kb")
+    sel(T.IDF[:], T.ONEG[:], [[-1, 128]], 0, "oneg", "idf")
+    iota(T.BIA[:], [[1, 256]], 256, 0, "bia")
+    ts("pio", "pm", T.PM[:], T.PIO[:], 15, OP.bitwise_and)
+    ts("pio", "mui", T.MUI[:], T.PIO[:], 4, OP.arith_shift_right, 1, OP.bitwise_and)
+    ts("c16", "bc15", T.BC15[:], T.C16[:], float(15 - KE), OP.add)
+    cp("mui", "mu1", T.MU1[:], T.MUI[:])
+    ts("mui", "mu0", T.MU0[:], T.MUI[:], -1.0, OP.mult, 1.0, OP.add)
+    tt("pm c16", "lik", T.LIK[:], T.PM[:], T.C16[:], OP.add)
+    ts("c16", "bcc", T.BCC[:], T.C16[:], float(-KE), OP.add, 0.0625, OP.mult)
+    mms("r8", "p4", [(T.P4[:, 0:128], T.R8[:], T.R8[:], True, True)])
+    mms("r16", "p0", [(T.P0[:, 0], T.R16[:, 0:128], T.R16[:], True, True)])
+    for j in range(8):
+        act("oneb", "sq", T.SQ[:, 256 * j:256 * j + 256], T.ONEB[:], scale=0.0)
+    for j in range(2):
+        act("oneb", "swp", T.SWP[:, 2 * j:2 * j + 2], T.ONEB[:], scale=0.0)
+    for u in range(2):
+        for gl in range(2):
+            sel(T.SWP[:, 2 * u + gl, :, gl, :], T.ONEF[:, :, 0, :], [[-32, 4], [-1, 16]], -16 * u, "onef swp", "sw%d" % (2 * u + gl))
+
+    run("v", V.transpose, "tt0 tt1 tt2 tt3 tt4 tt5", "tx", T.TX[:], T.TT[:])
+    ts("tx mu0", "ta", T.TA[:], T.TX[:, :, 0, :], T.MU0[:, 0:1], OP.mult)
+    ts("tx mu1", "tb", T.TB[:], T.TX[:, :, 1, :], T.MU1[:, 0:1], OP.mult)
+    ts("fri", "frq", T.FRQ[:], T.FRI[:], 511, OP.bitwise_and)
+    tt("ta tb", "tl", T.TL[:], T.TA[:], T.TB[:], OP.add)
+    cp("gfr", "gfb", T.GFB[:], T.GFR[:])
+    mms("r8 gfb", "p2", [(T.P2[:, 0:256], T.R8[:], T.GFB[:], True, True)])
+    act("p2", "bg", T.BG[:], T.P2[:, 0:256])
+    ts("fri", "m1", T.P6[:, 0:256], T.FRI[:], 2.0, OP.mult, float(KE), OP.add)
+    ts("fri", "eq", T.P5[:, 0:256], T.FRI[:], 0.0, OP.is_lt, NEG, OP.mult)
+    tt("m1 frq", "ow", T.OW[:], T.P6[:, 0:256], T.FRQ[:], OP.subtract)
+    cp("tl", "sl", T.SL[:], T.TL[:, 0, :])
+    tt("eq ow", "f0o", T.F0[:, 0:256], T.P5[:, 0:256], T.OW[:], OP.add)
+    cp("tl", "fl", T.FL[:], T.TL[:, 1, :])
+    act("f0o", "f0g", T.F0[:, 256:512], T.F0[:, 0:256])
+    run("gq", g.affine_select, "ski", "skf", T.SKU[:], T.SKI[:], [[1, 1024]], OP.is_ge, 0.0, 0, 0)
+    BANK = {"P5": "eq t2", "P6": "m1 m2"}
+    for j, p in ((0, "P5"), (1, "P6")):
+        cs = slice(512 * j, 512 * j + 512)
+        ts("ski", BANK[p], T[p][:], T.SKI[:, cs], 1024.0, OP.is_ge, float(-(1 << 20) - 2 * B), OP.mult)
+        act("skf", "sku%d" % j, T.SKU[:, cs], T.SKU[:, cs], AF.Identity, bias=float(KE + B), scale=1024.0)
+    for j, p in ((0, "P5"), (1, "P6")):
+        cs = slice(512 * j, 512 * j + 512)
+        tt("%s sku%d" % (BANK[p], j), "skv", T.SKV[:, cs], T[p][:], T.SKU[:, cs], OP.add)
+    cp("tl", "cl", T.CL[:], T.TL[:, 2, :])
+    act("p0", "diag", T.DIAG[:], T.P0[:, 0])
+    act("p4", "blkf", T.BLKF[:], T.P4[:, 0:128])
+    act("p0", "dif", T.DIF[:], T.P0[:, 0, 0, :], scale=-2.0 * NEG)
+    for q in range(16):
+        act("p4", "sq", T.SQ[:, 128 * q + q:128 * q + 128:16], T.P4[:, q:128:16], scale=16.0)
+    act("idf", "idb", T.IDB[:], T.IDF[:], scale=-NEG)
+    act("f0o", "base", T.BASE[:], T.F0[:, 0:256])
+
+    def later_constants():
+        cp("thi", "thf", T.THF[:], T.THI[:])
+        ts("diag thf", "thd", T.THD[:], T.DIAG[:], T.THF[:, 0:1], OP.mult)
+        mms("blkf thd", "p2", [(T.P2[:, 0:256], T.BLKF[:], T.THD[:], True, True)])
+        act("kb", "rst0", T.RST[:, 0:256], T.KB[:], AF.Sign, scale=-1.0, bias=15.0)
+        act("kb", "rst1", T.RST[:, 256:512], T.KB[:], AF.Sign, scale=-1.0, bias=15.0)
+        run("v", V.memset, "", "thr", lf(3), 8.0)
+        act("oneb", "mk", T.MK[:], T.ONEB[:], AF.Identity, scale=0.0, bias=NEG)
+        ts("tl", "l2", lf(2), T.TL[:, 0, :], 1024.0, OP.mult, float(KE), OP.add)
+        run("v", V.memset, "", "npr", T.NPR[:, 0:256], NEG)
+        run("v", V.memset, "", "npr", T.NPR[:, 256:512], -NEG)
+        cp("tl", "sav", SCL, T.TL[:, 2, :])
+        tt("tl l2", "sav", SG, T.TL[:, 1, :], lf(2), OP.add)
+        ts("p2", "thw", T.THW[:], T.P2[:, 0:256], -1.0, OP.add)
+        ts("p2", "tha", T.THA[:], T.P2[:, 0:256], 16.0, OP.mult, 15.0, OP.add)
+        ts("thw", "thw", T.THW[:], T.THW[:], 1, OP.arith_shift_right)
+        ts("thw", "thb", T.THB[:], T.THW[:], 16.0, OP.mult, 15.0, OP.add)
+        cp("blkf", "blkh", T.BLKH[:], T.BLKF[:])
+        cp("oneb", "oneh", T.ONEH[:], T.ONEB[0:1, 0:128])
+        ts("iot", "nih", T.NIH[:], T.IOT[0:1, :], -1.0, OP.mult)
+        new_saved_clause()
+
+    def new_saved_clause():
+        ts("sav", "i1", li(1), SG, 10, OP.arith_shift_right, 2047, OP.bitwise_and)
+        ts("i1", "l5", lf(5), li(1), -560.0, OP.add)
+        tt("l5 sav", "l6", lf(6), lf(5), SCL, OP.mult)
+        ts("l6", "i2", li(2), lf(6), 32.0, OP.add)
+        ts("i2", "i5", li(5), li(2), 5, OP.arith_shift_right, 1023, OP.bitwise_and)
+        ts("i5", "l7", lf(7), li(5), 1024.0, OP.mult)
+        tt("l7 lik", "l4", lf(4), lf(7), T.LIK[:], OP.add)
+
+    def recs(o, n, key):
+        c = slice(o, o + n)
+        ts("xi" + key, "pi" + key, T.PI[:, c], T.XI[:, c], 10, OP.arith_shift_right, 2047, OP.bitwise_and)
+        ts("xi" + key, "qi" + key, T.QI[:, c], T.XI[:, c], 1023, OP.bitwise_and)
+        tt("pi%s qi%s" % (key, key), "zi" + key, T.ZI[:, c], T.PI[:, c], T.QI[:, c], OP.mult)
+        ts("zi" + key, "ri" + key, T.RI[:, c], T.ZI[:, c], 4, OP.arith_shift_right, 4095, OP.bitwise_and)
+        cp("ri" + key, "rl" + key, T.RL[:, c], T.RI[:, c])
+
+    def save_numbers(parity):
+        tt("l18 l10", "l22", lf(19), lf(18), lf(10), OP.add)
+        tt("i6 i7 sav", "l20", lf(20, 2), li(6, 2), T.SAV[:], OP.subtract)
+        if parity:
+            cp("p2", "i12", li(12), T.P2[:, 256:272])
+        tt("l20 l18 l22", "l21", lf(22, 2), lf(20, 2), lf(18, 2), OP.mult)
+        if parity:
+            ts("i12", "i13", li(13), li(12), 1, OP.bitwise_and)
+        tt("l21 sav", "sav", T.SAV[:], lf(22, 2), T.SAV[:], OP.add)
+        if parity:
+            ts("i13", "thr", lf(3), li(13), -1.0, OP.mult, 8.0, OP.add)
+
+    def swap(p, j, stop):
+        mms("xt sw0 sw1 sw2 sw3", p.lower(), [(T[p][:, 0, :, u, :], T.SWP[:, 2 * u + gl], T.XT[:, 8 * j:8 * j + 8, gl, :],
+                                               u + gl == 0, stop and u + gl == 2) for u in range(2) for gl in range(2)])
+
+    def sv_payload():
+        tt("p0 thb", "sv", T.SV[:], D, T.THB[:], OP.is_le)
+        mms("sv idb", "p7", [(T.P7[:, 0], T.IDB[:], T.SV[:], False, True)])
+
+    sent = 0
+    D = T.P0[:, 0]
+    EQ, T2 = T.P5[:, 0:256], T.P5[:, 256:512]
+    M1, M2 = T.P6[:, 0:256], T.P6[:, 256:512]
+    for t in range(RO):
+        F = T["F%d" % t]
+        fo, fg, fs = "f%do" % t, "f%dg" % t, "f%ds" % t
+        last = t == RO - 1
+        if t == 0:
+            tt("skv sl bg", "cg", T.CG[:], T.SKV[:].indirect(T.SL[:]), T.BG[:], OP.add)
+        else:
+            act(fg, "p3", T.P3[:, 0], F[:, 256:512])
+            act("hl " + fo + " " + fg, "wc", T.WC[:], F[:, 0:512].indirect(T.HL[:]))
+            cp(fs, "sl", T.SL[:], F[:, 512:528])
+            tt("skv sl bia", "cg", T.CG[:], T.SKV[:].indirect(T.SL[:]), T.BIA[:], OP.add)
+        for k in range(2):
+            c = slice(128 * k, 128 * k + 128)
+            if t == 0:
+                tt(fo + " " + fg + " fl cg", "xig%d" % k, T.XI[:, c], F[:, 0:512].indirect(T.FL[:, 8 * k:8 * k + 8]), T.CG[:, c], OP.max)
+            else:
+                tt("cg p3", "xig%d" % k, T.XI[:, c], T.P3[:, 0, 8 * k:8 * k + 8, :], T.CG[:, c], OP.max)
+            recs(128 * k, 128, "g%d" % k)
+        for j, (a, b) in enumerate(PARTS):
+            if j not in HELP[t]:
+                act(XRK + "rlg%d" % (a // 8), "u%d" % j, T.U[:, 256 * a:256 * b], T.XR[:].indirect(T.RL[:, 16 * a:16 * b]))
+        if t == 0:
+            for q in range(16):
+                act("p4 dif", "tq", T.TQ[:, 128 * q:128 * q + 128], T.P4[:, 0:128], scale=T.DIF[:, q:q + 1])
+            tt("skv cl iot", "vc", T.VC[:], T.SKV[:].indirect(T.CL[:]), T.IOT[:], OP.add)
+            tt("vc " + fo, "xc", T.XC[:], T.VC[:], F[:, 0:256], OP.max)
+            ts(fo, "eq", EQ, F[:, 0:256], -2.0, OP.mult, NEG, OP.add)
+        else:
+            tt("m2 wc", "xc", T.XC[:], M2, T.WC[:], OP.max)
+        ts("xig0 xig1", "mg", T.MG[:], T.XI[:, 0:256], B - 1, OP.bitwise_and)
+        tt("eq mg", "t2", T2, EQ, T.MG[:], OP.min)
+        tt("t2 xc", "xic", T.XI[:, 256:512], T2, T.XC[:], OP.max)
+        run("gq", g.affine_select, "xig0 xig1 xic", "xf", T.XF[:], T.XI[:], [[1, 512]], OP.is_ge, 0.0, 0, 0)
+        recs(256, 256, "c")
+        if t == 0:
+            later_constants()
+        mms("oneb kb", "p0", [(D, ONES, T.KB[0:1, :], True, False)])
+        for j, (a, b) in enumerate(PARTS):
+            if j in HELP[t]:
+                cp(XRK + "rlg1 db1", "u%d" % j, T.U[:, 256 * a:256 * b], T.XR[:].indirect(T.RL[:, 16 * a:16 * b]))
+            tt(XRK + "rlc u%d" % j, "db%d" % j, T.DB[:, 256 * a:256 * b], T.XR[:].indirect(T.RL[:, 256 + 16 * a:256 + 16 * b]),
+               T.U[:, 256 * a:256 * b], OP.subtract)
+            act("db%d" % j, "ab%d" % j, T.AB[:, a:b], T.DB[:, 256 * a:256 * b], AF.Abs)
+        for j, (a, b, need) in enumerate(SUMS):
+            mms(need + " sq", "p0", [(T.P0[:, 0, a:b, :], T.SQ[:, 128 * q:128 * q + 128], T.AB[:, a:b, q, :], False, j == len(SUMS) - 1 and q == 15)
+                                     for q in range(16)])
+        mms("oneb npr", "p2", [(T.P2[:, 0:256], ONES, T.NPR[0:1, 0:256], True, False)])
+        act("xf", "flg", T.FLG[:], T.XF[:, 256:512], AF.Relu, bias=float(-16 * (B - 1)), scale=16.0)
+        run("v", V.transpose, "xf", "xt", T.XT[:], T.XF[:])
+        swap("P1", 0, True)
+        if t:
+            new_saved_clause()
+        tt("t2 flg", "eq", EQ, T2, T.FLG[:], OP.subtract)
+        tt("eq mk", "ya", T.YA[:], EQ, T.MK[:], OP.max)
+        tt("p0 tha", "nov", T.NOV[:], D, T.THA[:], OP.is_le)
+        scan("rst0 nov", "ns", T.NS[:], T.RST[:, 0:256], T.NOV[:], OP.add)
+        tt("p0 nov", "ky", T.KY[:], D, T.NOV[:], OP.mult)
+        tt("ns thr", "l8", T.SB[:], T.NS[:, 15::16], lf(3), OP.is_gt)
+        mms("l8 tq", "p2", [(T.P2[:, q:256:16], T.TQ[:, 128 * q:128 * q + 128], T.SB[:], False, q == 15) for q in range(16)])
+        swap("P7", 1, False)
+        mms("oneb npr", "p3", [(T.P3[:], ONES, T.NPR[0:1, :], True, False)])
+        scan("rst0 ky", "km", T.KM[:], T.RST[:, 0:256], T.KY[:], OP.max)
+        tt("ns thr", "l10", lf(10), T.NS[:, 15::16], lf(3), OP.is_le)
+        tt("km bc15 ky", "mask", T.MASK[:], T.KM[:].indirect(T.BC15[:]), T.KY[:], OP.is_equal)
+        tt("l10 sav", "l11", lf(11), lf(10), SG, OP.mult)
+        tt("p1 mask", "mx0", T.MX[:, 0:256], T.P1[:, 0], T.MASK[:], OP.mult)
+        scan("rst0 mx0", "sc0", T.SC[:, 0:256], T.RST[:, 0:256], T.MX[:, 0:256], OP.add)
+        if last:
+            sv_payload()
+        tt("sc0 l8", "l12", lf(12), T.SC[:, 15:256:16], T.SB[:], OP.mult)
+        tt("p2 ya", "m1", M1, T.P2[:, 0:256], T.YA[:], OP.min)
+        tt("l12 l11", "i6", li(6), lf(12), lf(11), OP.add)
+        tt("m1 base", fo, F[:, 0:256], M1, T.BASE[:], OP.max)
+        if not last:
+            ts("i6", "i8", li(8), li(6), 1023, OP.bitwise_and)
+            ts("i6", "i9", li(9), li(6), 10, OP.arith_shift_right, 2047, OP.bitwise_and)
+            ts("i8", "fl", T.FL[:], li(8), -16.0, OP.add)
+            C = T["COL%d" % t]
+            ts("i9", "cols", C[:, 256:272], li(9), -592.0, OP.add)
+            cp("fl " + fo + " " + fg, "col", C[:, 0:256], F[:, 0:512].indirect(T.FL[:]))
+            d = 1 + t % (N - 1)
+            dst = T.cores[(rank + d) % N]
+            rel = routes(topo, core, dst)
+            tr = []
+            if rel:
+                w = 272 // len(rel)
+                for k, c in enumerate(rel):
+                    rid, pid = topo.addr(c, core)
+                    es = topo.engines(core, c)
+                    tr.append(RemoteDMATransfer(dst_ids=[DstId(rid=rid, pnc=pid)], dma_engine_mask=only(es[HOP * k:], HOP),
+                                                remote_sem=T.sem["in%d" % t], src=C[:, k * w:(k + 1) * w], dst=T["RB%d" % t][:, 0:w]))
+                add("gq", lambda tr=tr: hand(g.remote_dma_fused(tr, local_sem=T.sem.sent)), "cols col", "go", 1.0, 5.0, None, 0)
+                sent += HOP * len(rel)
+            else:
+                rid, pid = topo.addr(dst, core)
+                add("gq", lambda a=(T["F%d" % (t + 1)][:, 256:528], C[:], T.sem["arr%d" % t], T.sem.sent, pid, rid, topo.mask(core, dst)):
+                    hand(g.remote_dma(*a)), "cols col", "go", 1.0, 3.0, None, 0)
+                sent += len(topo.engines(core, dst))
+            src = T.cores[(rank - d) % N]
+            rin = routes(topo, src, core)
+            n = sum(len(topo.engines(c, core)) for c in rin) if rin else len(topo.engines(src, core))
+            add("net", lambda: None, "go", "f%dg f%ds" % (t + 1, t + 1), 0.0, 0.0, "arr%d" % t, n)
+            act(fo, "f%do" % (t + 1), T["F%d" % (t + 1)][:, 0:256], F[:, 0:256])
+            act(fo, "wn", T.WN[:], F[:, 0:256], scale=-1.0)
+            act("m1 m2 " + fo, "ya", T.YA[:], M1)
+            mms("l8 diag", "p2", [(T.P2[:, 256:272], T.DIAG[:, 0:128], T.SB[:], True, True)])
+            sv_payload()
+        tt("l10 l4", "l13", lf(13), lf(10), lf(4), OP.mult)
+        tt("p7 mask", "mx1", T.MX[:, 256:512], T.P7[:, 0], T.MASK[:], OP.mult)
+        scan("rst1 mx1", "sc1", T.SC[:, 256:512], T.RST[:, 256:512], T.MX[:, 256:512], OP.add)
+        tt("sc1 l8", "l14", lf(14), T.SC[:, 271::16], T.SB[:], OP.mult)
+        ts("sc1", "l17", lf(17), T.SC[:, 271::16], float(2 * B), OP.is_ge)
+        tt("l13 l14", "i10", li(10), lf(13), lf(14), OP.add)
+        tt("l17 l8", "l18", lf(18), lf(17), T.SB[:], OP.mult)
+        ts("i10", "i14", li(14), li(10), 1023, OP.bitwise_and)
+        ts("i10", "i11", li(11), li(10), 10, OP.arith_shift_right, 2047, OP.bitwise_and)
+        act("l18", "s2a", T.S2[:, 0, :], lf(18))
+        act("l18", "s2b", T.S2[:, 1, :], lf(18), scale=-1.0)
+        mms("s2a s2b tq", "p3", [(T.P3[:, :, :, q], T.TQ[:, 128 * q:128 * q + 128], T.S2[:], False, q == 15) for q in range(16)])
+        if not last:
+            ts("i14", "l16", lf(16), li(14), -16.0, OP.add)
+        ts("i11", "i7", li(7), li(11), -592.0, OP.add)
+        if not last:
+            tt("l16 bcc diag", "eh", T.EH[:], lf(16).indirect(T.BCC[:]), T.DIAG[:], OP.mult)
+            cp("i7", "cl", T.CL[:], li(7))
+            act("skv cl", "vc", T.VC[:], T.SKV[:].indirect(T.CL[:]))
+            mms("eh blkh oneh nih", "p4", [(T.P4[:, 0:256], T.BLKH[:], T.EH[:], True, True), (T.P4[:, 256:512], T.ONEH[:], T.NIH[:], True, False),
+                                           (T.P4[:, 256:512], T.BLKH[:], T.EH[:], False, True)])
+            cp("l16", "hl", T.HL[:], lf(16))
+            act("p4", "ha", T.HA[:], T.P4[:, 256:512], AF.Abs)
+            tt("p3 ya", "m2", M2, T.P3[:, 0], T.YA[:], OP.min)
+            tt("p3 ya", "mk", T.MK[:], T.P3[:, 1], T.YA[:], OP.min)
+            tt("m2 base", "base", T.BASE[:], M2, T.BASE[:], OP.max)
+            act("ha", "p3", T.P3[:, 1], T.HA[:], AF.Identity, bias=-NEG, scale=2.0 * NEG)
+            tt("p4 vc ha", "m2", M2, T.P4[:, 0:256], T.VC[:], OP.add)
+            save_numbers(True)
+            tt("p3 wn", "eq", EQ, T.P3[:, 1], T.WN[:], OP.min)
+        else:
+            save_numbers(False)
+    act("m1 m2 f3o", "ya", T.YA[:], M1)
+    cp("f3o", "pig0 pig1", T.PI[:, 0:256], T.F3[:, 0:256])
+    ts("pig0 pig1", "qig0 qig1", T.QI[:, 0:256], T.PI[:, 0:256], 1023, OP.bitwise_and)
+    ts("f3o ya", "m2", M2, T.F3[:, 0:256], -606240.0, OP.add)
+    tt("m2 qig0 qig1 ya", "yo", T.YO[:], M2, T.QI[:, 0:256], OP.add)
+    tt("p3 ya", "m2", M2, T.P3[:, 1], T.YA[:], OP.min)
+    ts("yo", "ym", T.YM[:], T.YO[:], -1.0, OP.max)
+    ts("m2", "p2", T.P2[:, 0:256], M2, 0.0, OP.is_ge)
+    tt("p2 ym", "yo", T.YO[:], T.P2[:, 0:256], T.YM[:], OP.add)
+    load("sync", T.yf[:], T.YO[:], "out", "yf", "yo")
+
+    srcs = [("i6", li(6)), ("i10", li(10)), ("sav", SG)]
+    for j, (key, src) in enumerate(srcs):
+        ts(key, "pic", T.PI[:, 256 + 16 * j:272 + 16 * j], src, 10, OP.arith_shift_right, 2047, OP.bitwise_and)
+        ts(key, "qic", T.QI[:, 256 + 16 * j:272 + 16 * j], src, 1023, OP.bitwise_and)
+    ts("pic", "mx0", T.MX[:, 0:48], T.PI[:, 256:304], 512.0, OP.mult, float(-592 * 512 - 16), OP.add)
+    for k in range(2):
+        tt("mx0 qic", "fld%d" % k, T.FLD[:, 0:3, k, :], T.MX[:, 0:48], T.QI[:, 256:304], OP.add)
+        cp("sav", "fle%d" % k, T.FLD[:, 3, k, :], SCL)
+    run("v", V.transpose, "fld0 fld1 fle0 fle1", "flt", T.FLT[:], T.FLD[:])
+    ts("flt mu0", "fo", T.FO[:], T.FLT[:, :, 0, :], T.MU0[:, 0:1], OP.mult)
+    ts("flt mu1", "fp", T.FP[:], T.FLT[:, :, 1, :], T.MU1[:, 0:1], OP.mult)
+    tt("fo fp", "fo", T.FO[:], T.FO[:], T.FP[:], OP.add)
+    for j, y in enumerate((T.yg, T.yc, T.ysg, T.yk)):
+        load("sync" if j % 2 else "s", y[:], T.FO[:, j, :], "out", "y%d" % j, "fo")
+    cnt, seen = issue()
+    g.sync.wait_ge(T.sem.out, cnt["out"])
+    g.wait_ge(T.sem.sent, sent)
+    for q in ("v", "s", "pe", "gq"):
+        g.sync.wait_ge(T.sem[q], cnt[q])
+    for sm in LOADS:
+        if not any(k[1] == sm for k in seen):
+            g.sync.wait_ge(T.sem[sm], 16)

@@ -3,15 +3,19 @@ from concourse.mybir import AluOpType as OP, ActivationFunctionType as AF
 
 N = 8
 RO = 4
-NEG = -8388608.0
 B = 1 << 21
 KE = 592 * 1024 + 16
-PARTS = [(0, 4), (4, 8), (8, 12), (12, 14), (14, 16)]
-SUMS = [(0, 4, "ab0"), (4, 8, "ab1"), (8, 12, "ab2"), (12, 16, "ab3 ab4")]
-HELP = [[], [4], [4], []]
-LAT, GAP, PATIENCE = 0.14, 0.8, 0.3
+BLOCKS = [(0, 4, 0, 16)] + [(4, 12, c, c + 4) for c in range(0, 16, 4)] + [(12, 16, 0, 8), (12, 16, 8, 12), (12, 16, 12, 16)]
+PARTS = [[0], [1, 2], [3, 4], [5], [6], [7]]
+GOALS = [(0, 4), (4, 16)]
+CLAUSES = [(0, 4), (4, 16)]
+RELU = 16
+SPLIT = 12
+LAT, GAP, PATIENCE, PASSES = 0.18, 0.8, 0.3, 6
+PLANS = {}
+CYC, GAT = 0.00083, 1.5
 HOP = 8
-LOADS = ["l_gs0", "l_gs1", "l_gf0", "l_gf1", "l_gc0", "l_gc1", "l_gfr", "l_fr", "l_sk", "l_th", "l_x0", "l_x1"]
+LOADS = ["l_gs", "l_gf", "l_gc", "l_fr", "l_sk", "l_th", "l_x0", "l_x1"]
 
 
 def f32(*s):
@@ -26,35 +30,44 @@ def b16(*s):
     return ("sbuf", [128] + list(s), "bfloat16")
 
 
+def h16(*s):
+    return ("sbuf", [128] + list(s), "float16")
+
+
 def u16(*s):
     return ("sbuf", [128] + list(s), "uint16")
 
 
 SCRATCH = {
-    "XR": b16(4096), "SKI": i32(1024), "SKU": f32(1024), "SKV": f32(1024), "FRI": i32(256), "FRQ": i32(256), "OW": f32(256),
-    "BASE": f32(256), "MK": f32(256), "YA": f32(256), "FLG": f32(256), "F0": f32(528), "F1": f32(528), "F2": f32(528), "F3": f32(528),
+    "XR": b16(4096), "SKI": i32(1024), "SK16": h16(1024), "SGN": b16(1024), "SKV": f32(1024), "FRI": i32(256), "FRQ": i32(256),
+    "OW": f32(256), "BASE": f32(256), "YB": f32(256), "F16": b16(256), "FR16": b16(256), "RVC": b16(256),
+    "F0": f32(528), "F1": f32(528), "F2": f32(528), "F3": f32(528),
     "COL0": f32(272), "COL1": f32(272), "COL2": f32(272), "RB0": f32(136), "RB2": f32(136),
-    "TT": i32(96), "TX": i32(3, 2, 16), "TA": f32(3, 16), "TB": f32(3, 16), "TL": f32(3, 16),
-    "GFR": ("sbuf", [8, 256], "int32"), "GFB": ("sbuf", [8, 256], "bfloat16"), "R16": ("sbuf", [16, 256], "bfloat16"), "R8": ("sbuf", [8, 128], "bfloat16"),
-    "THI": i32(1), "THF": f32(1), "THD": f32(256), "THA": f32(256), "THB": f32(256), "THW": i32(256),
-    "ONEB": b16(256), "ONEF": f32(4, 2, 16), "ONEG": f32(128), "IDF": f32(128), "IDB": b16(128),
-    "BLKF": f32(128), "BLKH": ("sbuf", [128, 128], "float16"), "NPR": ("sbuf", [1, 512], "bfloat16"),
-    "ONEH": ("sbuf", [1, 128], "float16"), "NIH": ("sbuf", [1, 256], "float16"),
-    "DIAG": b16(256), "DIF": f32(16), "SQ": b16(2048), "TQ": b16(2048), "SWP": f32(4, 4, 2, 16),
-    "KB": b16(256), "RST": b16(512), "IOT": f32(256), "BIA": f32(256), "BG": f32(256),
-    "C16": f32(16), "PIO": i32(16), "PM": i32(16), "LIK": f32(16), "MUI": i32(16), "MU1": f32(16), "MU0": f32(16),
-    "BC15": u16(16), "SL": u16(16), "FL": u16(16), "CL": u16(16), "HL": u16(16), "BCC": u16(16),
-    "CG": f32(256), "VC": f32(256), "WC": f32(256), "XC": f32(256), "MG": i32(256),
-    "XI": i32(512), "PI": i32(512), "QI": i32(512), "ZI": i32(512), "RI": i32(512), "RL": u16(512),
-    "U": b16(4096), "DB": b16(4096), "AB": b16(16, 16, 16), "XF": f32(512), "XT": f32(16, 2, 16),
-    "NOV": b16(256), "NS": b16(256), "SV": b16(256), "SB": b16(16), "S2": b16(2, 16), "KY": f32(256), "KM": f32(256), "MASK": b16(256),
-    "MX": f32(512), "SC": f32(512), "EH": ("sbuf", [128, 256], "float16"), "HA": f32(256), "WN": f32(256),
-    "LF": f32(512), "LI": i32(256), "SAV": i32(32),
-    "FLD": f32(4, 2, 16), "FLT": f32(4, 2, 16), "FO": f32(4, 16), "FP": f32(4, 16), "YO": f32(256), "YM": f32(256),
-    "P0": ("psum", [128, 2, 16, 16], "float32"), "P1": ("psum", [128, 2, 8, 2, 16], "float32"), "P2": ("psum", [128, 512], "float32"),
-    "P3": ("psum", [128, 2, 16, 16], "float32"), "P4": ("psum", [128, 512], "float32"), "P5": ("psum", [128, 512], "float32"),
-    "P6": ("psum", [128, 512], "float32"), "P7": ("psum", [128, 2, 8, 2, 16], "float32"),
+    "LS": ("sbuf", [8, 768], "int32"), "L16": ("sbuf", [9, 1024], "float16"), "ONE": b16(1024),
+    "R9": ("sbuf", [9, 128], "bfloat16"), "Z": ("sbuf", [8, 144], "bfloat16"), "R16": ("sbuf", [16, 256], "bfloat16"),
+    "KB": ("sbuf", [1, 256], "bfloat16"), "CR": ("sbuf", [2, 256], "float16"), "LG": ("sbuf", [2, 128], "bfloat16"),
+    "LC": ("sbuf", [2, 128], "bfloat16"),
+    "LU": u16(48), "SL": u16(16), "FL": u16(16), "CH": u16(32), "TL": f32(48),
+    "V16": h16(2, 256), "FG": h16(2, 256),
+    "THI": i32(1), "THJ": i32(2), "THF": f32(2), "THD": f32(512), "TH": f32(512),
+    "W": b16(160), "WS": b16(4, 160), "I1K": b16(128), "ISG": b16(128), "ISV": b16(128), "BLKF": f32(128),
+    "DIAG": b16(256), "DIF": f32(16), "SQ": b16(3, 144), "TQ": b16(2048),
+    "RST": b16(256), "RS7": b16(256), "IOT": f32(256), "BIA": f32(256),
+    "C16": f32(16), "PIO": i32(16), "PM": i32(16), "IDX": f32(16), "MUI": i32(1), "MU": f32(2),
+    "CG": f32(256), "VC": f32(256), "WC": f32(256), "XC": f32(256),
+    "XI": i32(2, 256), "PQ": i32(4, 16, 16), "ZI": i32(512), "RI": i32(2, 16, 16), "RA": i32(128), "RL": u16(512),
+    "DB": b16(4096), "TURN": u16(4), "PA4": i32(2), "PF": f32(2),
+    "U": b16(4096), "X16": h16(4, 8, 2, 16), "XT": h16(4, 8, 2, 16),
+    "NOV": b16(256), "NS": b16(256), "SV": b16(256), "NR": b16(256), "SB": b16(16), "S2": h16(3, 16), "KY": f32(256),
+    "SC": f32(512), "LF": f32(288), "LI": i32(272), "SAV": i32(32),
+    "FI": i32(256), "FQ": i32(256), "EQ": f32(256), "NM": f32(256), "YO": f32(256),
+    "FLD": f32(4, 2, 16), "FLT": f32(4, 2, 16), "FO": f32(4, 16),
+    "PA": ("psum", [128, 512], "float32"), "PB": ("psum", [128, 512], "float32"), "PG": ("psum", [128, 512], "float32"),
+    "PC": ("psum", [128, 512], "float32"), "PV": ("psum", [128, 512], "float32"), "PS": ("psum", [128, 512], "float32"),
+    "PH": ("psum", [128, 2, 16, 16], "float32"), "PX": ("psum", [128, 512], "float32"),
 }
+for _j, (_a, _b, _c, _d) in enumerate(BLOCKS):
+    SCRATCH["AB%d" % _j] = b16(_b - _a, _d - _c, 16) if _j else b16(1024)
 SEMAPHORES = LOADS + ["v", "s", "pe", "gq", "out", "sent", "in0", "in2", "arr0", "arr1", "arr2"]
 
 
@@ -73,65 +86,47 @@ def hand(ins):
     return None
 
 
-SMALL = "sl fl cl hl thr sav cols pm mui mu0 mu1 lik bc15 bcc tl ta tb s2a s2b fo fp npr thf oneh dif fld0 fld1 fle0 fle1".split()
-LONG = {"cg": .37, "mask": .37, "eh": .37, "col": .37, "wc": .39, "vc": .39, "xt": .44, "skv": .44, "zic": .44, "zig0": .23, "zig1": .23,
-        "xf": 1.05, "skf": 1.9, "ns": .13, "sku0": .44, "sku1": .44, "tq": .13, "sq": .1, "idf": .4, "r8": .4, "r16": .6, "c16": .16, "pio": .16,
-        "iot": .55, "kb": .55, "bia": .55, "sw0": .3, "sw1": .3, "sw2": .3, "sw3": .3}
-
-
-def guess(q, key):
-    if key in LONG:
-        return LONG[key]
-    if key in SMALL or key[0] in "li" and key[1:].isdigit():
-        return 0.075
-    if key[0] == "u" and key[1:].isdigit() or key[:2] == "db" and key[2:].isdigit():
-        a, b = PARTS[int(key[-1])]
-        return 0.06 + 0.32 * (b - a)
-    if key[:2] == "ab":
-        a, b = PARTS[int(key[-1])]
-        return 0.02 + 0.213 * (b - a)
-    return 0.13 if key[-2:] in ("g0", "g1") else 0.235
-
-
 def plan(nodes):
     m = len(nodes)
-    succ = [[] for _ in range(m)]
-    left = [len(x["deps"]) for x in nodes]
+    succ, pred = [[] for _ in range(m)], [[] for _ in range(m)]
     for n, x in enumerate(nodes):
-        for d in x["deps"]:
-            succ[d].append(n)
+        for d, lat in [(d, nodes[d]["lat"]) for d in x["deps"]] + [(d, 0.0) for d in x["soft"]]:
+            succ[d].append((n, lat))
+            pred[n].append((d, lat))
+
+    def place(urge, before, after, first):
+        left = [len(before[n]) for n in range(m)]
+        ready, end, free, can = list(first), [0.0] * m, {}, {}
+        for n in range(m):
+            if not left[n]:
+                can.setdefault(nodes[n]["q"], []).append(n)
+        for _ in range(m):
+            t, q = min((max(free.get(q, 0.0), min(ready[n] for n in can[q])), q) for q in can if can[q])
+            n = max([k for k in can[q] if ready[k] <= t + 1e-9], key=lambda k: (urge[k], -k))
+            for k in sorted(can[q], key=lambda k: -urge[k]):
+                if urge[k] > urge[n] + GAP and ready[k] < t + PATIENCE * nodes[n]["cost"]:
+                    n = k
+                    break
+            can[q].remove(n)
+            end[n] = free[q] = max(t, ready[n]) + nodes[n]["cost"]
+            for j, lat in after[n]:
+                left[j] -= 1
+                ready[j] = max(ready[j], end[n] + lat)
+                if not left[j]:
+                    can.setdefault(nodes[j]["q"], []).append(j)
+        return end
+
     way = [0.0] * m
     for n in range(m - 1, -1, -1):
-        way[n] = nodes[n]["cost"] + nodes[n]["lat"] + max([way[k] for k in succ[n]] + [0.0])
-    start = [0.0] * m
-    free, can, order = {}, {}, []
-    for n in range(m):
-        if not left[n]:
-            can.setdefault(nodes[n]["q"], []).append(n)
-    while len(order) < m:
-        best = None
-        for q in can:
-            if can[q]:
-                t = max(free.get(q, 0.0), min(start[n] for n in can[q]))
-                if best is None or t < best[0]:
-                    best = (t, q)
-        t, q = best
-        now = [n for n in can[q] if start[n] <= t + 1e-9]
-        n = max(now, key=lambda k: (way[k], -k))
-        for k in sorted(can[q], key=lambda k: -way[k]):
-            if way[k] > way[n] + GAP and start[k] < t + PATIENCE * nodes[n]["cost"]:
-                n = k
-                break
-        t = max(t, start[n])
-        can[q].remove(n)
-        order.append((t, len(order), n))
-        free[q] = t + nodes[n]["cost"]
-        for k in succ[n]:
-            left[k] -= 1
-            start[k] = max(start[k], t + nodes[n]["cost"] + nodes[n]["lat"])
-            if not left[k]:
-                can.setdefault(nodes[k]["q"], []).append(k)
-    return [n for _, _, n in sorted(order)]
+        way[n] = nodes[n]["cost"] + max([way[k] + lat for k, lat in succ[n]] + [nodes[n]["lat"]])
+    best = None
+    for _ in range(PASSES):
+        end = place(way, pred, succ, [0.0] * m)
+        span = max(end[n] + nodes[n]["lat"] for n in range(m))
+        if best is None or span < best[0]:
+            best = (span, end)
+        way = place(end, succ, pred, [x["lat"] for x in nodes])
+    return sorted(range(m), key=lambda n: (best[1][n] - nodes[n]["cost"], n))
 
 
 def relay(g, core, T, topo):
@@ -161,30 +156,44 @@ def rank_program(g, core, T, topo):
         return relay(g, core, T, topo)
     ENG = {"v": g.vector, "s": g.scalar, "pe": g.tensor, "gq": g, "sync": g.sync}
     V = g.vector
-    nodes, lastw, readers = [], {}, {}
+    nodes, lastw, readers, banks = [], {}, {}, {}
 
     def add(q, emit, reads, writes, cost, lat, sem, inc):
         reads, writes = reads.split(), writes.split()
+        lines = [k for k in writes if k[0] == "@"]
+        writes = [k for k in writes if k[0] != "@"]
+        soft = set(lastw[k] for k in lines if k in lastw)
+        for k in lines:
+            lastw[k] = len(nodes)
         deps = set(lastw[k] for k in reads + writes if k in lastw)
         for k in writes:
             deps |= readers.get(k, set())
         n = len(nodes)
-        nodes.append({"q": q, "emit": emit, "deps": deps, "cost": cost, "lat": lat, "sem": sem, "inc": inc})
+        for bank in sorted(set(k[:2] for k in reads + writes if k[0] == "P")):
+            who, cur, before = banks.get(bank, (q, [], []))
+            if who != q:
+                cur, before = [], cur
+            deps |= set(before)
+            banks[bank] = (q, cur + [n], before)
+        nodes.append({"q": q, "emit": emit, "deps": deps, "soft": soft - deps, "cost": cost, "lat": lat, "sem": sem, "inc": inc})
         for k in writes:
             lastw[k] = n
             readers[k] = set()
         for k in reads:
             readers.setdefault(k, set()).add(n)
 
-    def run(q, fn, reads, writes, *a, **kw):
-        add(q, lambda: fn(*a, **kw), reads, writes, guess(q, writes.split()[0]), LAT, q, 1)
+    def run(q, fn, reads, writes, cost, *a, **kw):
+        add(q, lambda: fn(*a, **kw), reads, writes, cost, LAT, q, 1)
 
-    def load(q, out, in_, sem, key, reads=""):
-        add(q, lambda: ENG[q].dma_start(out, in_), reads, key, 0.06, 1.9, sem, 16)
+    def load(q, out, in_, sem, key, lat, reads=""):
+        add(q, lambda: ENG[q].dma_start(out, in_), reads, key, 0.06, lat, sem, 16)
 
     def issue():
         cnt, seen, tok = {}, {}, {}
-        for n in plan(nodes):
+        form = tuple((x["q"], x["cost"], x["lat"]) for x in nodes)
+        if form not in PLANS:
+            PLANS[form] = plan(nodes)
+        for n in PLANS[form]:
             x = nodes[n]
             q = x["q"]
             need = {}
@@ -203,30 +212,51 @@ def rank_program(g, core, T, topo):
                     ins.then_inc(T.sem[x["sem"]], x["inc"])
         return cnt, seen
 
-    def tt(reads, w, out, a, b, op):
-        run("v", V.tensor_tensor, reads, w, out, a, b, op)
+    def us(n):
+        return 0.06 - GAT * n * CYC if n < 0 else max(64, n) * CYC + 0.02
 
-    def ts(reads, w, out, a, s1, op0, s2=None, op1=None):
+    def tt(n, reads, w, out, a, b, op):
+        run("v", V.tensor_tensor, reads, w, us(n), out, a, b, op)
+
+    def ts(n, reads, w, out, a, s1, op0, s2=None, op1=None):
         if op1 is None:
-            run("v", V.tensor_scalar, reads, w, out, a, s1, None, op0)
+            run("v", V.tensor_scalar, reads, w, us(n), out, a, s1, None, op0)
         else:
-            run("v", V.tensor_scalar, reads, w, out, a, s1, s2, op0, op1)
+            run("v", V.tensor_scalar, reads, w, us(n), out, a, s1, s2, op0, op1)
 
-    def cp(reads, w, out, a):
-        run("v", V.tensor_copy, reads, w, out, a)
+    def cp(n, reads, w, out, a):
+        run("v", V.tensor_copy, reads, w, us(n), out, a)
 
-    def scan(reads, w, out, d0, d1, op):
-        run("v", V.tensor_tensor_scan, reads, w, out, d0, d1, 0.0, OP.mult, op)
+    def fill(n, w, out, k):
+        run("v", V.memset, "", w, us(n), out, k)
 
-    def act(reads, w, out, a, func=AF.Copy, **kw):
-        run("s", g.scalar.activation, reads, w, out, a, func, **kw)
+    def scan(n, reads, w, out, d0, d1, op0, op1):
+        run("v", V.tensor_tensor_scan, reads, w, us(n), out, d0, d1, 0.0, op0, op1)
 
-    def mms(reads, w, calls):
+    def act(n, reads, w, out, a, func=AF.Copy, **kw):
+        run("s", g.scalar.activation, reads, w, us(n), out, a, func, **kw)
+
+    def mms(n, reads, w, calls):
         def emit():
             for c in calls:
                 ins = g.tensor.matmul(*c)
             return ins
-        add("pe", emit, reads, w, 0.9 if len(calls) == 16 else 1.7 if len(calls) == 4 else 0.25 * len(calls), LAT, "pe", 1)
+        add("pe", emit, reads, w, n * CYC, LAT, "pe", 1)
+
+    def sel(n, r, w, o, i, p, base, cm):
+        run("gq", g.affine_select, r, w, 0.17 + 2 * n * CYC, o, i, p, OP.is_equal, 0.0, base, cm)
+
+    def cast(r, w, o, i, *shape):
+        n = 1
+        for s in shape:
+            n *= s
+        sel(n, r, w, o, i, [[0, s] for s in shape], 0, 0)
+
+    def iota(n, w, o, p, base, cm):
+        run("gq", g.iota, "", w, 0.13 + 2 * n * CYC, o, p, base, cm, allow_small_or_imprecise_dtypes=True)
+
+    def span(name, a=0, b=16):
+        return " ".join("%s_%d" % (name, k) for k in range(a, b, 2))
 
     def lf(j, n=1):
         return T.LF[:, 16 * j:16 * j + 16 * n]
@@ -235,232 +265,264 @@ def rank_program(g, core, T, topo):
         return T.LI[:, 16 * j:16 * j + 16 * n]
 
     SG, SCL = T.SAV[:, 0:16], T.SAV[:, 16:32]
-    ONES = T.ONEB[0:1, 0:128]
+    ID = T.W[:, 16:144]
+    R8 = T.R9[0:8, :]
 
-    load("sync", T.TT[:, 0:16], T.gs[:], "l_gs0", "tt0")
-    load("sync", T.TT[:, 16:32], T.gs[:], "l_gs1", "tt1")
-    load("sync", T.SKI[:], T.sk[:], "l_sk", "ski")
-    load("sync", T.GFR[:], T.gf[:], "l_gfr", "gfr")
-    load("sync", T.XR[:, 592:4096], T.x[:, 0:3504], "l_x0", "xr0")
-    load("s", T.TT[:, 32:48], T.gf[:], "l_gf0", "tt2")
-    load("s", T.TT[:, 48:64], T.gf[:], "l_gf1", "tt3")
-    load("s", T.FRI[:], T.fr[:], "l_fr", "fri")
-    load("s", T.TT[:, 64:80], T.gcl[:], "l_gc0", "tt4")
-    load("s", T.TT[:, 80:96], T.gcl[:], "l_gc1", "tt5")
-    load("s", T.XR[:, 0:592], T.x[:, 3504:4096], "l_x1", "xr1")
-    load("s", T.THI[:], T.th[:], "l_th", "thi")
+    def spread(reads, w, out, rhs):
+        mms(1024, reads + " tq", w, [(out(q), T.TQ[:, 128 * q:128 * q + 128], rhs, True, True) for q in range(16)])
+
+    load("sync", T.LS[:, 0:256], T.gs[:], "l_gs", "ls0", 1.9)
+    load("sync", T.SKI[:], T.sk[:], "l_sk", "ski", 3.4)
+    load("sync", T.XR[:, 592:4096], T.x[:, 0:3504], "l_x0", "xr0", 6.0)
+    load("s", T.LS[:, 256:512], T.gf[:], "l_gf", "ls1", 1.9)
+    load("s", T.LS[:, 512:768], T.gcl[:], "l_gc", "ls2", 1.9)
+    load("s", T.FRI[:], T.fr[:], "l_fr", "fri", 2.3)
+    load("s", T.THI[:], T.th[:], "l_th", "thi", 2.3)
+    load("s", T.XR[:, 0:592], T.x[:, 3504:4096], "l_x1", "xr1", 5.0)
     XRK = "xr0 xr1 "
 
-    run("v", V.memset, "", "oneb", T.ONEB[:], 1.0)
-    run("v", V.memset, "", "onef", T.ONEF[:], 1.0)
-    run("v", V.memset, "", "oneg", T.ONEG[:], 1.0)
-
-    def sel(o, i, p, base, r, w):
-        run("gq", g.affine_select, r, w, o, i, p, OP.is_equal, 0.0, base, 1)
-
-    def iota(o, p, base, cm, w):
-        run("gq", g.iota, "", w, o, p, base, cm, allow_small_or_imprecise_dtypes=True)
-    iota(T.C16[:], [[16, 16]], KE, 0, "c16")
-    iota(T.PIO[:], [[0, 16]], 0, 1, "pio")
-    sel(T.R8[:], T.ONEB[0:8, 0:128], [[-1, 8], [0, 16]], 0, "oneb", "r8")
-    sel(T.R16[:], T.ONEB[0:16, :], [[0, 16], [-1, 16]], 0, "oneb", "r16")
-    iota(T.IOT[:], [[1, 256]], 0, 0, "iot")
-    iota(T.KB[:], [[0, 16], [-1, 16]], 15, 0, "kb")
-    sel(T.IDF[:], T.ONEG[:], [[-1, 128]], 0, "oneg", "idf")
-    iota(T.BIA[:], [[1, 256]], 256, 0, "bia")
-    ts("pio", "pm", T.PM[:], T.PIO[:], 15, OP.bitwise_and)
-    ts("pio", "mui", T.MUI[:], T.PIO[:], 4, OP.arith_shift_right, 1, OP.bitwise_and)
-    ts("c16", "bc15", T.BC15[:], T.C16[:], float(15 - KE), OP.add)
-    cp("mui", "mu1", T.MU1[:], T.MUI[:])
-    ts("mui", "mu0", T.MU0[:], T.MUI[:], -1.0, OP.mult, 1.0, OP.add)
-    tt("pm c16", "lik", T.LIK[:], T.PM[:], T.C16[:], OP.add)
-    ts("c16", "bcc", T.BCC[:], T.C16[:], float(-KE), OP.add, 0.0625, OP.mult)
-    mms("r8", "p4", [(T.P4[:, 0:128], T.R8[:], T.R8[:], True, True)])
-    mms("r16", "p0", [(T.P0[:, 0], T.R16[:, 0:128], T.R16[:], True, True)])
-    for j in range(8):
-        act("oneb", "sq", T.SQ[:, 256 * j:256 * j + 256], T.ONEB[:], scale=0.0)
-    for j in range(2):
-        act("oneb", "swp", T.SWP[:, 2 * j:2 * j + 2], T.ONEB[:], scale=0.0)
+    fill(512, "one", T.ONE[:], 1.0)
+    fill(64, "r9", T.R9[:], 2448.0)
+    ts(512, "one", "l16t l16i", T.L16[:], T.ONE[0:9, :], 1961.0, OP.mult)
+    sel(144, "one", "z", T.Z[:], T.ONE[0:8, 0:144], [[1, 144]], -15, -16)
+    sel(128, "one r9", "r9", R8, T.ONE[0:8, 0:128], [[-1, 8], [0, 16]], 0, 1)
+    sel(160, "one", "w", T.W[:], T.ONE[:, 0:160], [[1, 160]], -16, -1)
+    iota(256, "iot", T.IOT[:], [[1, 256]], 0, 0)
+    cp(256, "iot l16i", "l16i", T.L16[0:8, 768:1024], T.IOT[0:8, :])
+    sel(256, "one", "r16", T.R16[:], T.ONE[0:16, 0:256], [[0, 16], [-1, 16]], 0, 1)
+    iota(16, "c16", T.C16[:], [[16, 16]], 0, 0)
+    iota(16, "pio", T.PIO[:], [[0, 16]], 0, 1)
+    iota(256, "kb", T.KB[:], [[0, 16], [-1, 16]], 15, 0)
+    iota(128, "lg", T.LG[:], [[0, 128]], 1 << 19, -720 - (1 << 19))
+    iota(128, "lc", T.LC[:], [[0, 128]], 1 << 20, -720 - (1 << 20))
+    ts(128, "one", "cr", T.CR[:], T.ONE[0:2, 0:256], 421.0, OP.mult)
+    cp(128, "kb cr", "cr", T.CR[0:1, :], T.KB[:])
+    ts(16, "pio", "pm", T.PM[:], T.PIO[:], 15, OP.bitwise_and)
+    ts(1, "pio", "mui", T.MUI[:], T.PIO[:, 0:1], 4, OP.arith_shift_right, 1, OP.bitwise_and)
+    ts(1, "mui", "mu0", T.MU[:, 0:1], T.MUI[:], -1.0, OP.mult, 1.0, OP.add)
+    cp(1, "mui", "mu1", T.MU[:, 1:2], T.MUI[:])
+    tt(32, "pm c16", "idx", T.IDX[:], T.PM[:], T.C16[:], OP.add)
+    ts(1, "pio", "pa0", T.PA4[:, 0:1], T.PIO[:, 0:1], 3, OP.bitwise_and)
+    ts(1, "pio", "pa1", T.PA4[:, 1:2], T.PIO[:, 0:1], 2, OP.arith_shift_right, 3, OP.bitwise_and)
+    cp(1, "pa1", "pf1", T.PF[:, 1:2], T.PA4[:, 1:2])
+    ts(1, "pa0 pf1", "pf0", T.PF[:, 0:1], T.PA4[:, 0:1], 16.0, OP.mult, T.PF[:, 1:2], OP.add)
+    ts(4, "c16 pf0", "turn", T.TURN[:], T.C16[:, 0:4], 0.25, OP.mult, T.PF[:, 0:1], OP.add)
+    fill(128, "rst", T.RST[:], 1.0)
+    fill(16, "rst", T.RST[:, 0::16], 0.0)
+    fill(128, "rs7", T.RS7[:], 64.0)
+    fill(16, "rs7", T.RS7[:, 0::16], -7.0)
+    fill(16, "thr", li(0), 1)
+    act(128, "w", "i1k", T.I1K[:], ID, scale=1024.0)
+    act(128, "w", "isg", T.ISG[:], ID, scale=float(-5 << 19))
+    act(128, "w", "isv", T.ISV[:], ID, scale=float(1 << 19))
+    act(256, "iot", "bia", T.BIA[:], T.IOT[:], AF.Identity, bias=256.0)
     for u in range(2):
-        for gl in range(2):
-            sel(T.SWP[:, 2 * u + gl, :, gl, :], T.ONEF[:, :, 0, :], [[-32, 4], [-1, 16]], -16 * u, "onef swp", "sw%d" % (2 * u + gl))
-
-    run("v", V.transpose, "tt0 tt1 tt2 tt3 tt4 tt5", "tx", T.TX[:], T.TT[:])
-    ts("tx mu0", "ta", T.TA[:], T.TX[:, :, 0, :], T.MU0[:, 0:1], OP.mult)
-    ts("tx mu1", "tb", T.TB[:], T.TX[:, :, 1, :], T.MU1[:, 0:1], OP.mult)
-    ts("fri", "frq", T.FRQ[:], T.FRI[:], 511, OP.bitwise_and)
-    tt("ta tb", "tl", T.TL[:], T.TA[:], T.TB[:], OP.add)
-    cp("gfr", "gfb", T.GFB[:], T.GFR[:])
-    mms("r8 gfb", "p2", [(T.P2[:, 0:256], T.R8[:], T.GFB[:], True, True)])
-    act("p2", "bg", T.BG[:], T.P2[:, 0:256])
-    ts("fri", "m1", T.P6[:, 0:256], T.FRI[:], 2.0, OP.mult, float(KE), OP.add)
-    ts("fri", "eq", T.P5[:, 0:256], T.FRI[:], 0.0, OP.is_lt, NEG, OP.mult)
-    tt("m1 frq", "ow", T.OW[:], T.P6[:, 0:256], T.FRQ[:], OP.subtract)
-    cp("tl", "sl", T.SL[:], T.TL[:, 0, :])
-    tt("eq ow", "f0o", T.F0[:, 0:256], T.P5[:, 0:256], T.OW[:], OP.add)
-    cp("tl", "fl", T.FL[:], T.TL[:, 1, :])
-    act("f0o", "f0g", T.F0[:, 256:512], T.F0[:, 0:256])
-    run("gq", g.affine_select, "ski", "skf", T.SKU[:], T.SKI[:], [[1, 1024]], OP.is_ge, 0.0, 0, 0)
-    BANK = {"P5": "eq t2", "P6": "m1 m2"}
-    for j, p in ((0, "P5"), (1, "P6")):
-        cs = slice(512 * j, 512 * j + 512)
-        ts("ski", BANK[p], T[p][:], T.SKI[:, cs], 1024.0, OP.is_ge, float(-(1 << 20) - 2 * B), OP.mult)
-        act("skf", "sku%d" % j, T.SKU[:, cs], T.SKU[:, cs], AF.Identity, bias=float(KE + B), scale=1024.0)
-    for j, p in ((0, "P5"), (1, "P6")):
-        cs = slice(512 * j, 512 * j + 512)
-        tt("%s sku%d" % (BANK[p], j), "skv", T.SKV[:, cs], T[p][:], T.SKU[:, cs], OP.add)
-    cp("tl", "cl", T.CL[:], T.TL[:, 2, :])
-    act("p0", "diag", T.DIAG[:], T.P0[:, 0])
-    act("p4", "blkf", T.BLKF[:], T.P4[:, 0:128])
-    act("p0", "dif", T.DIF[:], T.P0[:, 0, 0, :], scale=-2.0 * NEG)
+        act(160, "w mu%d" % u, "ws%d" % u, T.WS[:, u, :], T.W[:], AF.Identity, scale=T.MU[:, u:u + 1])
+        act(160, "ws%d" % u, "wt%d" % u, T.WS[:, 2 + u, :], T.WS[:, u, :], scale=512.0)
+    mms(128, "r9", "PG0", [(T.PG[:, 0:128], R8, R8, True, True)])
+    mms(144, "r9 z", "PG1", [(T.PG[:, 128:272], R8, T.Z[:], True, True)])
+    mms(256, "r16", "PC0", [(T.PC[:, 0:256], T.R16[:, 0:128], T.R16[:], True, True)])
+    act(128, "PG0", "blkf", T.BLKF[:], T.PG[:, 0:128])
+    for j, w in enumerate((16.0, 32.0, -16.0)):
+        act(144, "PG1", "sq", T.SQ[:, j, :], T.PG[:, 128:272], scale=w)
+    act(256, "PC0", "diag", T.DIAG[:], T.PC[:, 0:256])
+    act(16, "PC0", "dif", T.DIF[:], T.PC[:, 0:16])
     for q in range(16):
-        act("p4", "sq", T.SQ[:, 128 * q + q:128 * q + 128:16], T.P4[:, q:128:16], scale=16.0)
-    act("idf", "idb", T.IDB[:], T.IDF[:], scale=-NEG)
-    act("f0o", "base", T.BASE[:], T.F0[:, 0:256])
+        act(128, "blkf dif", "tq", T.TQ[:, 128 * q:128 * q + 128], T.BLKF[:], AF.Identity, scale=T.DIF[:, q:q + 1])
 
-    def later_constants():
-        cp("thi", "thf", T.THF[:], T.THI[:])
-        ts("diag thf", "thd", T.THD[:], T.DIAG[:], T.THF[:, 0:1], OP.mult)
-        mms("blkf thd", "p2", [(T.P2[:, 0:256], T.BLKF[:], T.THD[:], True, True)])
-        act("kb", "rst0", T.RST[:, 0:256], T.KB[:], AF.Sign, scale=-1.0, bias=15.0)
-        act("kb", "rst1", T.RST[:, 256:512], T.KB[:], AF.Sign, scale=-1.0, bias=15.0)
-        run("v", V.memset, "", "thr", lf(3), 8.0)
-        act("oneb", "mk", T.MK[:], T.ONEB[:], AF.Identity, scale=0.0, bias=NEG)
-        ts("tl", "l2", lf(2), T.TL[:, 0, :], 1024.0, OP.mult, float(KE), OP.add)
-        run("v", V.memset, "", "npr", T.NPR[:, 0:256], NEG)
-        run("v", V.memset, "", "npr", T.NPR[:, 256:512], -NEG)
-        cp("tl", "sav", SCL, T.TL[:, 2, :])
-        tt("tl l2", "sav", SG, T.TL[:, 1, :], lf(2), OP.add)
-        ts("p2", "thw", T.THW[:], T.P2[:, 0:256], -1.0, OP.add)
-        ts("p2", "tha", T.THA[:], T.P2[:, 0:256], 16.0, OP.mult, 15.0, OP.add)
-        ts("thw", "thw", T.THW[:], T.THW[:], 1, OP.arith_shift_right)
-        ts("thw", "thb", T.THB[:], T.THW[:], 16.0, OP.mult, 15.0, OP.add)
-        cp("blkf", "blkh", T.BLKH[:], T.BLKF[:])
-        cp("oneb", "oneh", T.ONEH[:], T.ONEB[0:1, 0:128])
-        ts("iot", "nih", T.NIH[:], T.IOT[0:1, :], -1.0, OP.mult)
-        new_saved_clause()
+    ts(1, "thi", "thj0", T.THJ[:, 0:1], T.THI[:], -1.0, OP.add)
+    ts(1, "thj0", "thj1", T.THJ[:, 1:2], T.THJ[:, 0:1], 1, OP.arith_shift_right)
+    ts(1, "thi", "thf0", T.THF[:, 0:1], T.THI[:], 16.0, OP.mult, 15.0, OP.add)
+    ts(1, "thj1", "thf1", T.THF[:, 1:2], T.THJ[:, 1:2], 16.0, OP.mult, 15.0, OP.add)
+    for j, p in enumerate(("PG", "PC")):
+        c = slice(256 * j, 256 * j + 256)
+        act(256, "diag thf%d" % j, "thd%d" % j, T.THD[:, c], T.DIAG[:], AF.Identity, scale=T.THF[:, j:j + 1])
+        mms(1024, "blkf thd%d" % j, p + "0 " + p + "1", [(T[p][:, 0:256], T.BLKF[:], T.THD[:, c], True, True)])
+        act(256, p + "0", "th%d" % j, T.TH[:, c], T[p][:, 0:256])
 
-    def new_saved_clause():
-        ts("sav", "i1", li(1), SG, 10, OP.arith_shift_right, 2047, OP.bitwise_and)
-        ts("i1", "l5", lf(5), li(1), -560.0, OP.add)
-        tt("l5 sav", "l6", lf(6), lf(5), SCL, OP.mult)
-        ts("l6", "i2", li(2), lf(6), 32.0, OP.add)
-        ts("i2", "i5", li(5), li(2), 5, OP.arith_shift_right, 1023, OP.bitwise_and)
-        ts("i5", "l7", lf(7), li(5), 1024.0, OP.mult)
-        tt("l7 lik", "l4", lf(4), lf(7), T.LIK[:], OP.add)
+    cp(768, "ls0 ls1 ls2 l16t", "l16t", T.L16[0:8, 0:768], T.LS[:])
+    mms(1024, "z l16t", "PA0", [(T.PA[:, 0:48], T.Z[:, 15 - q:143 - q], T.L16[0:8, q:768:16], q == 0, q == 15) for q in range(16)])
+    cp(48, "PA0", "lu", T.LU[:], T.PA[:, 0:48])
+    cp(48, "PA0", "tl", T.TL[:], T.PA[:, 0:48])
+    ts(256, "fri", "frq", T.FRQ[:], T.FRI[:], 511 + (1 << 23), OP.bitwise_and)
+    act(256, "fri", "PS0", T.PS[:, 0:256], T.FRI[:], AF.Identity, scale=2.0, bias=float(KE + B))
+    tt(256, "PS0 frq", "ow", T.OW[:], T.PS[:, 0:256], T.FRQ[:], OP.subtract)
+    act(256, "ow", "f0o", T.F0[:, 0:256], T.OW[:], AF.Relu)
+    act(256, "ow", "f0g", T.F0[:, 256:512], T.OW[:], AF.Relu)
+    act(256, "ow", "f16", T.F16[:], T.OW[:], AF.Relu)
+    act(256, "ow", "base", T.BASE[:], T.OW[:], AF.Relu)
+    ts(16, "tl", "l2", lf(2), T.TL[:, 0:16], 512.0, OP.mult)
+    tt(32, "tl l2", "sav", SG, T.TL[:, 16:32], lf(2), OP.add)
+    cp(16, "tl sav", "sav", SCL, T.TL[:, 32:48])
 
-    def recs(o, n, key):
-        c = slice(o, o + n)
-        ts("xi" + key, "pi" + key, T.PI[:, c], T.XI[:, c], 10, OP.arith_shift_right, 2047, OP.bitwise_and)
-        ts("xi" + key, "qi" + key, T.QI[:, c], T.XI[:, c], 1023, OP.bitwise_and)
-        tt("pi%s qi%s" % (key, key), "zi" + key, T.ZI[:, c], T.PI[:, c], T.QI[:, c], OP.mult)
-        ts("zi" + key, "ri" + key, T.RI[:, c], T.ZI[:, c], 4, OP.arith_shift_right, 4095, OP.bitwise_and)
-        cp("ri" + key, "rl" + key, T.RL[:, c], T.RI[:, c])
+    def skeleton_table():
+        for j in range(4):
+            c = slice(256 * j, 256 * j + 256)
+            cast("ski", "sk16%d" % j, T.SK16[:, c], T.SKI[:, c], 256)
+        for j, (p, bank) in enumerate((("PH", T.PH[:]), ("PX", T.PX[:]))):
+            c = slice(512 * j, 512 * j + 512)
+            act(512, "ski", "sgn%d" % j, T.SGN[:, c], T.SKI[:, c], AF.Sign, bias=-1023.5)
+            mms(1024, "sk16%d sk16%d sgn%d i1k isg" % (2 * j, 2 * j + 1, j), p + "0 " + p + "1",
+                [(bank, T.I1K[:], T.SK16[:, c], True, False), (bank, T.ISG[:], T.SGN[:, c], False, True)])
+            act(512, p + "0 " + p + "1", "skv%d" % j, T.SKV[:, c], bank, AF.Identity, bias=float(KE + 2 * B - (5 << 19)))
 
-    def save_numbers(parity):
-        tt("l18 l10", "l22", lf(19), lf(18), lf(10), OP.add)
-        tt("i6 i7 sav", "l20", lf(20, 2), li(6, 2), T.SAV[:], OP.subtract)
-        if parity:
-            cp("p2", "i12", li(12), T.P2[:, 256:272])
-        tt("l20 l18 l22", "l21", lf(22, 2), lf(20, 2), lf(18, 2), OP.mult)
-        if parity:
-            ts("i12", "i13", li(13), li(12), 1, OP.bitwise_and)
-        tt("l21 sav", "sav", T.SAV[:], lf(22, 2), T.SAV[:], OP.add)
-        if parity:
-            ts("i13", "thr", lf(3), li(13), -1.0, OP.mult, 8.0, OP.add)
+    def saved_derived():
+        act(16, "sav", "l1", lf(1), SG, AF.Identity, bias=float(1 << 23))
+        ts(16, "sav", "i1", li(1), SG, 9, OP.arith_shift_right)
+        act(16, "i1", "l5", lf(5), li(1), AF.Identity, bias=32.0)
+        tt(32, "l5 sav", "l6", lf(6), lf(5), SCL, OP.mult)
+        ts(16, "l6", "i2", li(2), lf(6), 32.0, OP.add, 16.0, OP.mult)
+        ts(16, "i2", "i5", li(5), li(2), 1023 << 9, OP.bitwise_and)
+        tt(32, "i5 idx", "l4", lf(4), li(5), T.IDX[:], OP.add)
 
-    def swap(p, j, stop):
-        mms("xt sw0 sw1 sw2 sw3", p.lower(), [(T[p][:, 0, :, u, :], T.SWP[:, 2 * u + gl], T.XT[:, 8 * j:8 * j + 8, gl, :],
-                                               u + gl == 0, stop and u + gl == 2) for u in range(2) for gl in range(2)])
+    def recs(j, a, b):
+        n = 16 * (b - a)
+        xi, pi, qi, zi, ri = [span(k + str(j), a, b) for k in ("xi", "pi", "qi", "zi", "ri")]
+        x = T.XI[:, j, 16 * a:16 * b]
+        ts(n, xi, pi, T.PQ[:, 2 * j, a:b, :], x, 10, OP.arith_shift_right, 2047, OP.bitwise_and)
+        ts(n, xi, qi, T.PQ[:, 2 * j + 1, a:b, :], x, 1023, OP.bitwise_and)
+        z = 256 * j
+        tt(2 * n, pi + " " + qi, zi, T.ZI[:, z + 16 * a:z + 16 * b], T.PQ[:, 2 * j, a:b, :], T.PQ[:, 2 * j + 1, a:b, :], OP.mult)
+        if a == 0:
+            a, c = BLOCKS[0][1], slice(64 * j, 64 * j + 64)
+            ts(-64, zi + " turn", "ra%d" % j, T.RA[:, c], T.ZI[:, z:z + 64].indirect(T.TURN[:]), 4, OP.arith_shift_right, 4095, OP.bitwise_and)
+            cp(64, "ra%d" % j, "rl%d0" % j, T.RL[:, z:z + 64], T.RA[:, c])
+        if a < b:
+            ts(16 * (b - a), zi, ri, T.RI[:, j, a:b, :], T.ZI[:, z + 16 * a:z + 16 * b], 4, OP.arith_shift_right, 4095, OP.bitwise_and)
+        for k, (lo, hi, c, d) in enumerate(BLOCKS):
+            if k and a < hi <= b:
+                cast(span("ri%d" % j, lo, hi), "rl%d%d" % (j, k), T.RL[:, z + OFF[k]:z + OFF[k + 1]], T.RI[:, j, lo:hi, c:d], hi - lo, d - c)
 
-    def sv_payload():
-        tt("p0 thb", "sv", T.SV[:], D, T.THB[:], OP.is_le)
-        mms("sv idb", "p7", [(T.P7[:, 0], T.IDB[:], T.SV[:], False, True)])
+    OFF = [0]
+    for a, b, c, d in BLOCKS:
+        OFF.append(OFF[-1] + (b - a) * (d - c))
+
+    def payload(j, p, lhs, stop):
+        run("v", V.transpose, "x16%d0 x16%d1" % (j, j), "xt%d" % j, us(256), T.XT[:, 2 * j:2 * j + 2], T.X16[:, 2 * j:2 * j + 2])
+        calls = [(T[p][:, 0:256], lhs, T.CR[:], True, False)]
+        for u in range(2):
+            for gl in range(2):
+                o = 16 - 16 * (gl - u)
+                for f in range(2):
+                    calls.append((T[p][:, 128 * u:128 * u + 128], T.WS[:, 2 - 2 * f + u, o:o + 128], T.XT[:, 2 * j + f, :, gl, :],
+                                  False, stop and u + gl + f == 3))
+        mms(1280, "xt%d cr lg lc ws0 ws1 wt0 wt1" % j, p + "0", calls)
 
     sent = 0
-    D = T.P0[:, 0]
-    EQ, T2 = T.P5[:, 0:256], T.P5[:, 256:512]
-    M1, M2 = T.P6[:, 0:256], T.P6[:, 256:512]
+    PV0, PV1, PS0, PS1 = T.PV[:, 0:256], T.PV[:, 256:512], T.PS[:, 0:256], T.PS[:, 256:512]
     for t in range(RO):
         F = T["F%d" % t]
         fo, fg, fs = "f%do" % t, "f%dg" % t, "f%ds" % t
         last = t == RO - 1
         if t == 0:
-            tt("skv sl bg", "cg", T.CG[:], T.SKV[:].indirect(T.SL[:]), T.BG[:], OP.add)
+            for j, (lo, bank, key) in enumerate(((256, T.PX[:, 0:256], "PX0"), (768, T.PH[:, 0], "PH0"))):
+                cp(-256, "ski lu", "v16%d" % j, T.V16[:, j, :], T.SKI[:].indirect(T.LU[:, 32 * j:32 * j + 16]))
+                ts(128, "v16%d" % j, "fg%d" % j, T.FG[:, j, :], T.V16[:, j, :], 1024.0, OP.is_ge, -5120.0, OP.mult)
+                mms(768, "r9 l16t l16i i1k v16%d fg%d" % (j, j), key,
+                    [(bank, T.R9[:], T.L16[:, lo:lo + 256], True, False), (bank, T.I1K[:], T.V16[:, j, :], False, False),
+                     (bank, T.I1K[:], T.FG[:, j, :], False, True)])
+            act(-256, "lu f0o f0g", span("cg"), T.CG[:], F[:, 0:512].indirect(T.LU[:, 16:32]))
+            mms(512, "w f16 fg1", "PH1", [(T.PH[:, 1], ID, T.F16[:], True, False), (T.PH[:, 1], ID, T.FG[:, 1, :], False, True)])
+            free = dict(scale=-4096.0, bias=float(B - 4096 * 5120))
         else:
-            act(fg, "p3", T.P3[:, 0], F[:, 256:512])
-            act("hl " + fo + " " + fg, "wc", T.WC[:], F[:, 0:512].indirect(T.HL[:]))
-            cp(fs, "sl", T.SL[:], F[:, 512:528])
-            tt("skv sl bia", "cg", T.CG[:], T.SKV[:].indirect(T.SL[:]), T.BIA[:], OP.add)
-        for k in range(2):
-            c = slice(128 * k, 128 * k + 128)
-            if t == 0:
-                tt(fo + " " + fg + " fl cg", "xig%d" % k, T.XI[:, c], F[:, 0:512].indirect(T.FL[:, 8 * k:8 * k + 8]), T.CG[:, c], OP.max)
-            else:
-                tt("cg p3", "xig%d" % k, T.XI[:, c], T.P3[:, 0, 8 * k:8 * k + 8, :], T.CG[:, c], OP.max)
-            recs(128 * k, 128, "g%d" % k)
-        for j, (a, b) in enumerate(PARTS):
-            if j not in HELP[t]:
-                act(XRK + "rlg%d" % (a // 8), "u%d" % j, T.U[:, 256 * a:256 * b], T.XR[:].indirect(T.RL[:, 16 * a:16 * b]))
+            act(256, fg, "PX0", T.PX[:, 0:256], F[:, 256:512])
+            act(-256, "ch " + fo + " " + fg, "wc", T.WC[:], F[:, 0:512].indirect(T.CH[:, 16:32]))
+            cp(16, fs, "sl", T.SL[:], F[:, 512:528])
         if t == 0:
-            for q in range(16):
-                act("p4 dif", "tq", T.TQ[:, 128 * q:128 * q + 128], T.P4[:, 0:128], scale=T.DIF[:, q:q + 1])
-            tt("skv cl iot", "vc", T.VC[:], T.SKV[:].indirect(T.CL[:]), T.IOT[:], OP.add)
-            tt("vc " + fo, "xc", T.XC[:], T.VC[:], F[:, 0:256], OP.max)
-            ts(fo, "eq", EQ, F[:, 0:256], -2.0, OP.mult, NEG, OP.add)
+            act(256, "PH1", "PS0", PS0, T.PH[:, 1], AF.Identity, **free)
+            act(256, "PH1", "fr16", T.FR16[:], T.PH[:, 1], AF.Identity, **free)
+        for a, b in GOALS:
+            c = slice(16 * a, 16 * b)
+            if t:
+                tt(-16 * (b - a), "skv0 skv1 sl bia", span("cg", a, b), T.CG[:, c], T.SKV[:].indirect(T.SL[:, a:b]), T.BIA[:, c], OP.add)
+            tt(16 * (b - a), "PX0 " + span("cg", a, b), span("xi0", a, b), T.XI[:, 0, c], T.PX[:, c], T.CG[:, c], OP.max)
+            recs(0, a, b)
+        for j, ks in enumerate(PARTS):
+            lo, hi = OFF[ks[0]], OFF[ks[-1] + 1]
+            act(16 * (lo - hi), XRK + " ".join("rl0%d" % k for k in ks), "u%d @u" % j, T.U[:, 16 * lo:16 * hi], T.XR[:].indirect(T.RL[:, lo:hi]))
+        if t == 0:
+            tt(256, "PH0 " + fo, "xc", T.XC[:], T.PH[:, 0], F[:, 0:256], OP.max)
         else:
-            tt("m2 wc", "xc", T.XC[:], M2, T.WC[:], OP.max)
-        ts("xig0 xig1", "mg", T.MG[:], T.XI[:, 0:256], B - 1, OP.bitwise_and)
-        tt("eq mg", "t2", T2, EQ, T.MG[:], OP.min)
-        tt("t2 xc", "xic", T.XI[:, 256:512], T2, T.XC[:], OP.max)
-        run("gq", g.affine_select, "xig0 xig1 xic", "xf", T.XF[:], T.XI[:], [[1, 512]], OP.is_ge, 0.0, 0, 0)
-        recs(256, 256, "c")
+            tt(256, "PV1 wc", "xc", T.XC[:], PV1, T.WC[:], OP.max)
+        for a, b in CLAUSES:
+            c = slice(16 * a, 16 * b)
+            tt(16 * (b - a), "PS0 PV0 " + span("xi0", a, b), span("PVt", a, b), T.PV[:, c], T.PS[:, c], T.XI[:, 0, c], OP.add)
+            tt(16 * (b - a), "xc " + span("PVt", a, b), span("xi1", a, b), T.XI[:, 1, c], T.PV[:, c], T.XC[:, c], OP.max)
+            recs(1, a, b)
+        for j in range(2):
+            for u in range(2):
+                cast(span("pi%d" % j, 8 * u, 8 * u + 8) + " " + span("qi%d" % j, 8 * u, 8 * u + 8), "x16%d%d" % (j, u),
+                     T.X16[:, 2 * j:2 * j + 2, :, u, :], T.PQ[:, 2 * j:2 * j + 2, 8 * u:8 * u + 8, :], 2, 8, 16)
         if t == 0:
-            later_constants()
-        mms("oneb kb", "p0", [(D, ONES, T.KB[0:1, :], True, False)])
-        for j, (a, b) in enumerate(PARTS):
-            if j in HELP[t]:
-                cp(XRK + "rlg1 db1", "u%d" % j, T.U[:, 256 * a:256 * b], T.XR[:].indirect(T.RL[:, 16 * a:16 * b]))
-            tt(XRK + "rlc u%d" % j, "db%d" % j, T.DB[:, 256 * a:256 * b], T.XR[:].indirect(T.RL[:, 256 + 16 * a:256 + 16 * b]),
-               T.U[:, 256 * a:256 * b], OP.subtract)
-            act("db%d" % j, "ab%d" % j, T.AB[:, a:b], T.DB[:, 256 * a:256 * b], AF.Abs)
-        for j, (a, b, need) in enumerate(SUMS):
-            mms(need + " sq", "p0", [(T.P0[:, 0, a:b, :], T.SQ[:, 128 * q:128 * q + 128], T.AB[:, a:b, q, :], False, j == len(SUMS) - 1 and q == 15)
-                                     for q in range(16)])
-        mms("oneb npr", "p2", [(T.P2[:, 0:256], ONES, T.NPR[0:1, 0:256], True, False)])
-        act("xf", "flg", T.FLG[:], T.XF[:, 256:512], AF.Relu, bias=float(-16 * (B - 1)), scale=16.0)
-        run("v", V.transpose, "xf", "xt", T.XT[:], T.XF[:])
-        swap("P1", 0, True)
-        if t:
-            new_saved_clause()
-        tt("t2 flg", "eq", EQ, T2, T.FLG[:], OP.subtract)
-        tt("eq mk", "ya", T.YA[:], EQ, T.MK[:], OP.max)
-        tt("p0 tha", "nov", T.NOV[:], D, T.THA[:], OP.is_le)
-        scan("rst0 nov", "ns", T.NS[:], T.RST[:, 0:256], T.NOV[:], OP.add)
-        tt("p0 nov", "ky", T.KY[:], D, T.NOV[:], OP.mult)
-        tt("ns thr", "l8", T.SB[:], T.NS[:, 15::16], lf(3), OP.is_gt)
-        mms("l8 tq", "p2", [(T.P2[:, q:256:16], T.TQ[:, 128 * q:128 * q + 128], T.SB[:], False, q == 15) for q in range(16)])
-        swap("P7", 1, False)
-        mms("oneb npr", "p3", [(T.P3[:], ONES, T.NPR[0:1, :], True, False)])
-        scan("rst0 ky", "km", T.KM[:], T.RST[:, 0:256], T.KY[:], OP.max)
-        tt("ns thr", "l10", lf(10), T.NS[:, 15::16], lf(3), OP.is_le)
-        tt("km bc15 ky", "mask", T.MASK[:], T.KM[:].indirect(T.BC15[:]), T.KY[:], OP.is_equal)
-        tt("l10 sav", "l11", lf(11), lf(10), SG, OP.mult)
-        tt("p1 mask", "mx0", T.MX[:, 0:256], T.P1[:, 0], T.MASK[:], OP.mult)
-        scan("rst0 mx0", "sc0", T.SC[:, 0:256], T.RST[:, 0:256], T.MX[:, 0:256], OP.add)
+            skeleton_table()
+            saved_derived()
+        calls = [(PS1, ID, T.FR16[:], True, False)]
+        for u in range(2):
+            calls += [(T.PS[:, 256 + 128 * u:384 + 128 * u], T.I1K[:], T.X16[:, 0, :, u, :], False, False),
+                      (T.PS[:, 256 + 128 * u:384 + 128 * u], ID, T.X16[:, 1, :, u, :], False, u == 1)]
+        mms(768, "w i1k fr16 x1600 x1601", "PS1", calls)
+        tt(256, "PS1 " + fo, "yb", T.YB[:], PS1, F[:, 0:256], OP.max)
         if last:
-            sv_payload()
-        tt("sc0 l8", "l12", lf(12), T.SC[:, 15:256:16], T.SB[:], OP.mult)
-        tt("p2 ya", "m1", M1, T.P2[:, 0:256], T.YA[:], OP.min)
-        tt("l12 l11", "i6", li(6), lf(12), lf(11), OP.add)
-        tt("m1 base", fo, F[:, 0:256], M1, T.BASE[:], OP.max)
-        if not last:
-            ts("i6", "i8", li(8), li(6), 1023, OP.bitwise_and)
-            ts("i6", "i9", li(9), li(6), 10, OP.arith_shift_right, 2047, OP.bitwise_and)
-            ts("i8", "fl", T.FL[:], li(8), -16.0, OP.add)
+            tt(512, "yb base", "eq", T.EQ[:], T.YB[:], T.BASE[:], OP.is_equal)
+        payload(0, "PG", T.LG[:], True)
+        payload(1, "PC", T.LC[:], False)
+        cut = [slice(0, 16 * SPLIT), slice(16 * SPLIT, 256)]
+        D = [T.PA[:, cut[0]], T.PB[:, cut[1]]]
+        for u, p in enumerate(("PA0", "PB0")):
+            mms(cut[u].stop - cut[u].start, "one cr", p, [(D[u], T.ONE[0:1, 0:128], T.CR[0:1, cut[u]], True, False)])
+        for j, ks in enumerate(PARTS):
+            lo, hi = OFF[ks[0]], OFF[ks[-1] + 1]
+            e = slice(16 * lo, 16 * hi)
+            tt(e.start - e.stop, XRK + " ".join("rl1%d" % k for k in ks) + " u%d" % j, "db%d @db" % j, T.DB[:, e],
+               T.XR[:].indirect(T.RL[:, 256 + lo:256 + hi]), T.U[:, e], OP.subtract)
+            for k in ks:
+                a, b, c, d = BLOCKS[k]
+                AB, u = T["AB%d" % k], int(a >= SPLIT)
+                out, key = T[("PA", "PB")[u]][:, 16 * a:16 * b], ("PA0 @d", "PB0 @d")[u]
+                if k == 0:
+                    n = 64 * RELU
+                    if n:
+                        ts(n // 2, "db0", "ab0 @db", AB[:, 0:n], T.DB[:, 0:n], 0.0, OP.max)
+                        for w, src, r in ((2, T.DB, "db0"), (1, AB, "ab0")):
+                            mms(n, r + " sq", key, [(out, T.SQ[:, w, 15 - q:143 - q], src[:, 64 * q:64 * q + 64], False, False)
+                                                    for q in range(RELU)])
+                    if n < 1024:
+                        act(1024 - n, "db0", "ac0 @u", AB[:, n:1024], T.DB[:, n:1024], AF.Abs)
+                        mms(1024 - n, "ac0 sq", key, [(out, T.SQ[:, 0, 15 - q:143 - q], AB[:, 64 * q:64 * q + 64], False, False)
+                                                      for q in range(RELU, 16)])
+                    continue
+                stop = k + 1 == len(BLOCKS) or int(BLOCKS[k + 1][0] >= SPLIT) != u
+                n = 16 * (b - a) * (d - c)
+                act(n, "db%d" % j, "ab%d @u" % k, AB[:], T.DB[:, 16 * OFF[k]:16 * OFF[k + 1]], AF.Abs)
+                mms(n, "ab%d sq" % k, key, [(out, T.SQ[:, 0, 15 - q:143 - q], AB[:, :, q - c, :], False, stop and q == d - 1)
+                                            for q in range(c, d)])
+        for u, p in enumerate(("PA0", "PB0")):
+            c, k, n = cut[u], "%d" % u, cut[u].stop - cut[u].start
+            c2 = slice(256 + c.start, 256 + c.stop)
+            tt(n, p + " th0", "nov" + k, T.NOV[:, c], D[u], T.TH[:, c], OP.is_le)
+            scan(n // 2, "rs7 nov" + k, "ns" + k, T.NS[:, c], T.RS7[:, c], T.NOV[:, c], OP.min, OP.add)
+            tt(n, p + " nov" + k, "ky" + k, T.KY[:, c], D[u], T.NOV[:, c], OP.mult)
+            scan(n, "rst ky" + k, "PVk" + k + (" PV1" if u == 0 else ""), T.PV[:, c2], T.RST[:, c], T.KY[:, c], OP.mult, OP.max)
+            tt(n, "PVk%s ky%s" % (k, k), "nr" + k, T.NR[:, c], T.PV[:, c2], T.KY[:, c], OP.is_gt)
+            scan(n, "PG0 nr" + k, "sc" + k, T.SC[:, c], T.NR[:, c], T.PG[:, c], OP.mult, OP.max)
+            tt(n, p + " th1", "sv" + k, T.SV[:, c], D[u], T.TH[:, c2], OP.is_le)
+        tt(32, "ns0 ns1 thr", "sb", T.SB[:], T.NS[:, 15::16], li(0), OP.is_gt)
+        spread("sb", "PS0", lambda q: T.PS[:, q:256:16], T.SB[:])
+        tt(32, "ns0 ns1 thr", "l10", lf(10), T.NS[:, 15::16], li(0), OP.is_le)
+        tt(32, "l10 l1", "l11", lf(11), lf(10), lf(1), OP.mult)
+        mms(256, "sv0 sv1 isv", "PC0", [(T.PC[:, 0:256], T.ISV[:], T.SV[:], False, True)])
+        tt(32, "sc0 sc1 l11", "i6", li(6), T.SC[:, 15:256:16], lf(11), OP.max)
+        tt(256, "PS0 yb", "PV0 " + span("PVt"), PV0, PS0, T.YB[:], OP.mult)
+        if last:
+            tt(256, "PV0 base", "fi", T.FI[:], PV0, T.BASE[:], OP.max)
+        else:
+            tt(256, "PV0 base", fo, F[:, 0:256], PV0, T.BASE[:], OP.max)
+            ts(16, "i6", "i8", li(8), li(6), 511, OP.bitwise_and)
+            ts(16, "i6", "i9", li(9), li(6), 9, OP.arith_shift_right, 1023, OP.bitwise_and)
+            cp(16, "i8", "fl", T.FL[:], li(8))
             C = T["COL%d" % t]
-            ts("i9", "cols", C[:, 256:272], li(9), -592.0, OP.add)
-            cp("fl " + fo + " " + fg, "col", C[:, 0:256], F[:, 0:512].indirect(T.FL[:]))
+            act(16, "i9", "cols", C[:, 256:272], li(9))
+            cp(-256, "fl " + fo + " " + fg, "col", C[:, 0:256], F[:, 0:512].indirect(T.FL[:]))
             d = 1 + t % (N - 1)
             dst = T.cores[(rank + d) % N]
             rel = routes(topo, core, dst)
@@ -483,68 +545,61 @@ def rank_program(g, core, T, topo):
             rin = routes(topo, src, core)
             n = sum(len(topo.engines(c, core)) for c in rin) if rin else len(topo.engines(src, core))
             add("net", lambda: None, "go", "f%dg f%ds" % (t + 1, t + 1), 0.0, 0.0, "arr%d" % t, n)
-            act(fo, "f%do" % (t + 1), T["F%d" % (t + 1)][:, 0:256], F[:, 0:256])
-            act(fo, "wn", T.WN[:], F[:, 0:256], scale=-1.0)
-            act("m1 m2 " + fo, "ya", T.YA[:], M1)
-            mms("l8 diag", "p2", [(T.P2[:, 256:272], T.DIAG[:, 0:128], T.SB[:], True, True)])
-            sv_payload()
-        tt("l10 l4", "l13", lf(13), lf(10), lf(4), OP.mult)
-        tt("p7 mask", "mx1", T.MX[:, 256:512], T.P7[:, 0], T.MASK[:], OP.mult)
-        scan("rst1 mx1", "sc1", T.SC[:, 256:512], T.RST[:, 256:512], T.MX[:, 256:512], OP.add)
-        tt("sc1 l8", "l14", lf(14), T.SC[:, 271::16], T.SB[:], OP.mult)
-        ts("sc1", "l17", lf(17), T.SC[:, 271::16], float(2 * B), OP.is_ge)
-        tt("l13 l14", "i10", li(10), lf(13), lf(14), OP.add)
-        tt("l17 l8", "l18", lf(18), lf(17), T.SB[:], OP.mult)
-        ts("i10", "i14", li(14), li(10), 1023, OP.bitwise_and)
-        ts("i10", "i11", li(11), li(10), 10, OP.arith_shift_right, 2047, OP.bitwise_and)
-        act("l18", "s2a", T.S2[:, 0, :], lf(18))
-        act("l18", "s2b", T.S2[:, 1, :], lf(18), scale=-1.0)
-        mms("s2a s2b tq", "p3", [(T.P3[:, :, :, q], T.TQ[:, 128 * q:128 * q + 128], T.S2[:], False, q == 15) for q in range(16)])
+            act(256, fo, "f%do" % (t + 1), T["F%d" % (t + 1)][:, 0:256], F[:, 0:256])
+            act(256, fo, "f16", T.F16[:], F[:, 0:256])
+            mms(64, "sb diag", "PG1", [(T.PG[:, 256:272], T.DIAG[:, 0:128], T.SB[:], True, True)])
+        tt(32, "l10 l4", "l13", lf(13), lf(10), lf(4), OP.mult)
+        scan(256, "PC0 nr0 nr1", "sc2", T.SC[:, 256:512], T.NR[:], T.PC[:, 0:256], OP.mult, OP.max)
+        tt(32, "sc2 sb", "l14", lf(14), T.SC[:, 271::16], T.SB[:], OP.mult)
+        tt(32, "l13 l14", "i10", li(10), lf(13), lf(14), OP.add)
+        ts(16, "i10", "i15", li(15), li(10), 19, OP.arith_shift_right, 1, OP.bitwise_and)
+        ts(16, "i10", "i13", li(13), li(10), 9, OP.arith_shift_right, 1023, OP.bitwise_and)
+        ts(16, "i6", "i12", li(12), li(6), (1 << 19) - 1, OP.bitwise_and)
+        tt(32, "i15 l10", "i16", li(16) if not last else T.S2[:, 2, :], li(15), lf(10), OP.add)
+        tt(64, "i12 i13 sav", "l7", lf(7, 2), li(12, 2), T.SAV[:], OP.subtract)
         if not last:
-            ts("i14", "l16", lf(16), li(14), -16.0, OP.add)
-        ts("i11", "i7", li(7), li(11), -592.0, OP.add)
-        if not last:
-            tt("l16 bcc diag", "eh", T.EH[:], lf(16).indirect(T.BCC[:]), T.DIAG[:], OP.mult)
-            cp("i7", "cl", T.CL[:], li(7))
-            act("skv cl", "vc", T.VC[:], T.SKV[:].indirect(T.CL[:]))
-            mms("eh blkh oneh nih", "p4", [(T.P4[:, 0:256], T.BLKH[:], T.EH[:], True, True), (T.P4[:, 256:512], T.ONEH[:], T.NIH[:], True, False),
-                                           (T.P4[:, 256:512], T.BLKH[:], T.EH[:], False, True)])
-            cp("l16", "hl", T.HL[:], lf(16))
-            act("p4", "ha", T.HA[:], T.P4[:, 256:512], AF.Abs)
-            tt("p3 ya", "m2", M2, T.P3[:, 0], T.YA[:], OP.min)
-            tt("p3 ya", "mk", T.MK[:], T.P3[:, 1], T.YA[:], OP.min)
-            tt("m2 base", "base", T.BASE[:], M2, T.BASE[:], OP.max)
-            act("ha", "p3", T.P3[:, 1], T.HA[:], AF.Identity, bias=-NEG, scale=2.0 * NEG)
-            tt("p4 vc ha", "m2", M2, T.P4[:, 0:256], T.VC[:], OP.add)
-            save_numbers(True)
-            tt("p3 wn", "eq", EQ, T.P3[:, 1], T.WN[:], OP.min)
-        else:
-            save_numbers(False)
-    act("m1 m2 f3o", "ya", T.YA[:], M1)
-    cp("f3o", "pig0 pig1", T.PI[:, 0:256], T.F3[:, 0:256])
-    ts("pig0 pig1", "qig0 qig1", T.QI[:, 0:256], T.PI[:, 0:256], 1023, OP.bitwise_and)
-    ts("f3o ya", "m2", M2, T.F3[:, 0:256], -606240.0, OP.add)
-    tt("m2 qig0 qig1 ya", "yo", T.YO[:], M2, T.QI[:, 0:256], OP.add)
-    tt("p3 ya", "m2", M2, T.P3[:, 1], T.YA[:], OP.min)
-    ts("yo", "ym", T.YM[:], T.YO[:], -1.0, OP.max)
-    ts("m2", "p2", T.P2[:, 0:256], M2, 0.0, OP.is_ge)
-    tt("p2 ym", "yo", T.YO[:], T.P2[:, 0:256], T.YM[:], OP.add)
-    load("sync", T.yf[:], T.YO[:], "out", "yf", "yo")
+            ts(16, "i10", "i14", li(14), li(10), 511, OP.bitwise_and)
+            cp(32, "i13 i14", "ch", T.CH[:], li(13, 2))
+            cp(16, "i14", "s20", T.S2[:, 0, :], li(14))
+            tt(32, "i14 idx", "s21", T.S2[:, 1, :], li(14), T.IDX[:], OP.not_equal)
+            cp(16, "i15", "s22", T.S2[:, 2, :], li(15))
+            act(-256, "skv0 skv1 ch", "vc", T.VC[:], T.SKV[:].indirect(T.CH[:, 0:16]))
+            act(256, "vc", "rvc", T.RVC[:], T.VC[:], AF.Relu, bias=float(-2 * B))
+            calls = [(T.PH[:, :, :, q], T.TQ[:, 128 * q:128 * q + 128], T.S2[:, 0:2, :], q == 0, False) for q in range(16)]
+            mms(1024, "s20 s21 tq", "PH0 PH1", calls)
+            mms(512, "w f16 rvc", "PH1", [(T.PH[:, 1], ID, T.F16[:], False, False), (T.PH[:, 1], ID, T.RVC[:], False, True)])
+            free = dict(scale=-float(1 << 24), bias=float(B))
+            act(256, "PH1", "PS0", PS0, T.PH[:, 1], AF.Identity, **free)
+            act(256, "PH1", "fr16", T.FR16[:], T.PH[:, 1], AF.Identity, **free)
+            tt(256, "PH0 vc", "PV1 PVk0 PVk1", PV1, T.PH[:, 0], T.VC[:], OP.add)
+            spread("s22", "PS1", lambda q: T.PS[:, 256 + q:512:16], T.S2[:, 2, :])
+            tt(256, "PS1 yb", "PV0", PV0, PS1, T.YB[:], OP.mult)
+            tt(256, "PV0 base", "base", T.BASE[:], PV0, T.BASE[:], OP.max)
+            ts(16, "PG1", "i3", li(3), T.PG[:, 256:272], 1.0, OP.add)
+            ts(16, "i3", "thr", li(0), li(3), 1, OP.bitwise_and)
+            tt(64, "l7 i15 i16", "l16 l17", lf(16, 2), lf(7, 2), li(15, 2), OP.mult)
+            tt(64, "l16 l17 sav", "sav", T.SAV[:], lf(16, 2), T.SAV[:], OP.add)
+            saved_derived()
+    spread("i16", "PS1", lambda q: T.PS[:, 256 + q:512:16], T.S2[:, 2, :])
+    ts(256, "fi", "fq", T.FQ[:], T.FI[:], 1023, OP.bitwise_and)
+    act(256, "fi", "PX0", T.PX[:, 0:256], T.FI[:], AF.Identity, bias=float(-B - 606239))
+    tt(256, "PX0 fq", "yo", T.YO[:], T.PX[:, 0:256], T.FQ[:], OP.add)
+    act(256, "yo", "PX1", T.PX[:, 256:512], T.YO[:], AF.Relu)
+    tt(256, "PS1 eq", "nm", T.NM[:], PS1, T.EQ[:], OP.max)
+    tt(256, "PX1 nm yo", "yo", T.YO[:], T.PX[:, 256:512], T.NM[:], OP.subtract)
+    load("sync", T.yf[:], T.YO[:], "out", "yf", 1.9, "yo")
 
-    srcs = [("i6", li(6)), ("i10", li(10)), ("sav", SG)]
-    for j, (key, src) in enumerate(srcs):
-        ts(key, "pic", T.PI[:, 256 + 16 * j:272 + 16 * j], src, 10, OP.arith_shift_right, 2047, OP.bitwise_and)
-        ts(key, "qic", T.QI[:, 256 + 16 * j:272 + 16 * j], src, 1023, OP.bitwise_and)
-    ts("pic", "mx0", T.MX[:, 0:48], T.PI[:, 256:304], 512.0, OP.mult, float(-592 * 512 - 16), OP.add)
-    for k in range(2):
-        tt("mx0 qic", "fld%d" % k, T.FLD[:, 0:3, k, :], T.MX[:, 0:48], T.QI[:, 256:304], OP.add)
-        cp("sav", "fle%d" % k, T.FLD[:, 3, k, :], SCL)
-    run("v", V.transpose, "fld0 fld1 fle0 fle1", "flt", T.FLT[:], T.FLD[:])
-    ts("flt mu0", "fo", T.FO[:], T.FLT[:, :, 0, :], T.MU0[:, 0:1], OP.mult)
-    ts("flt mu1", "fp", T.FP[:], T.FLT[:, :, 1, :], T.MU1[:, 0:1], OP.mult)
-    tt("fo fp", "fo", T.FO[:], T.FO[:], T.FP[:], OP.add)
-    for j, y in enumerate((T.yg, T.yc, T.ysg, T.yk)):
-        load("sync" if j % 2 else "s", y[:], T.FO[:, j, :], "out", "y%d" % j, "fo")
+    ts(16, "i10", "i11", li(11), li(10), (1 << 19) - 1, OP.bitwise_and)
+    tt(32, "l7 i15", "l16", lf(16), lf(7), li(15), OP.mult)
+    tt(32, "l7 i16", "l17", lf(17), lf(8), T.S2[:, 2, :], OP.mult)
+    tt(64, "l16 l17 sav", "sav", T.SAV[:], lf(16, 2), T.SAV[:], OP.add)
+    for j, (key, src) in enumerate((("i11 i12", li(11, 2)), ("sav", T.SAV[:]))):
+        ts(32, key + " mu0", "fld%d0" % j, T.FLD[:, 2 * j:2 * j + 2, 0, :], src, T.MU[:, 0:1], OP.mult)
+        act(32, key + " mu1", "fld%d1" % j, T.FLD[:, 2 * j:2 * j + 2, 1, :], src, AF.Identity, scale=T.MU[:, 1:2])
+        run("v", V.transpose, "fld%d0 fld%d1" % (j, j), "flt%d" % j, us(64), T.FLT[:, 2 * j:2 * j + 2], T.FLD[:, 2 * j:2 * j + 2])
+        tt(64, "flt%d" % j, "fo%d" % j, T.FO[:, 2 * j:2 * j + 2, :], T.FLT[:, 2 * j:2 * j + 2, 0, :], T.FLT[:, 2 * j:2 * j + 2, 1, :], OP.add)
+    for j, y in enumerate((T.yc, T.yg, T.ysg, T.yk)):
+        load("sync" if j % 2 else "s", y[:], T.FO[:, j, :], "out", "y%d" % j, 1.9, "fo%d" % (j // 2))
     cnt, seen = issue()
     g.sync.wait_ge(T.sem.out, cnt["out"])
     g.wait_ge(T.sem.sent, sent)

@@ -1,3 +1,4 @@
+import numpy as np
 from concourse.bass import DstId, RemoteDMATransfer
 from concourse.mybir import AluOpType as OP, ActivationFunctionType as AF
 
@@ -5,13 +6,21 @@ N = 8
 RO = 4
 B = 1 << 21
 KE = 592 * 1024 + 16
-BLOCKS = [(0, 4, 0, 16)] + [(4, 12, c, c + 4) for c in range(0, 16, 4)] + [(12, 16, 0, 8), (12, 16, 8, 12), (12, 16, 12, 16)]
-PARTS = [[0], [1, 2], [3, 4], [5], [6], [7]]
+BLOCKS = [(0, 4, 0, 16)] + [(a, a + 4, c, c + 8) for c in (0, 8) for a in (4, 8)] + [(12, 16, 0, 8), (12, 16, 8, 12), (12, 16, 12, 16)]
+UPARTS = [[0], [1, 2], [3, 4], [5, 6, 7]]
+CASTS = [[1, 2], [3, 4], [5], [6], [7]]
+LATE = 0
+PARTS = [[0], [1, 2], [3], [4], [5], [6], [7]]
 GOALS = [(0, 4), (4, 16)]
 CLAUSES = [(0, 4), (4, 16)]
-RELU = 16
+RELU = 8
 SPLIT = 12
 LAT, GAP, PATIENCE, PASSES = 0.18, 0.8, 0.3, 6
+NAMED, TRIES, SHAKE = 800, 400, 1.2
+FIRST = ["blkf sq diag PS0 i1k thd0 thd1 f0o f16 cg_0 th0 base idf ws0 ws1 wt0 wt1 sgn0 PV1 fr16 u0 ab7 th1 sgn1", "thf0 thf1 frq ow",
+         "v1600 v1604 v1610", "fg00 fg04 fg10"]
+EACH = ["sl PX0 wc", "fl col f16 ch rvc", "col f+o", "cg_0 cg_4 xi0_0 xi0_4", "nov0 ky0 ns0 PVk0 cf0 nr0 sc0",
+        "nov1 ky1 ns1 PVk1 ex1 nr1 sc1 i6 i8 i9 sd0"]
 PLANS = {}
 CYC, GAT = 0.00083, 1.5
 HOP = 8
@@ -43,7 +52,7 @@ SCRATCH = {
     "OW": f32(256), "BASE": f32(256), "YB": f32(256), "F16": b16(256), "FR16": b16(256), "RVC": b16(256),
     "F0": f32(528), "F1": f32(528), "F2": f32(528), "F3": f32(528),
     "COL0": f32(272), "COL1": f32(272), "COL2": f32(272), "RB0": f32(136), "RB2": f32(136),
-    "LS": ("sbuf", [8, 768], "int32"), "L16": ("sbuf", [9, 1024], "float16"), "ONE": b16(1024),
+    "LS": ("sbuf", [8, 768], "int32"), "L16": ("sbuf", [9, 1024], "float16"), "ONE": b16(512),
     "R9": ("sbuf", [9, 128], "bfloat16"), "Z": ("sbuf", [8, 144], "bfloat16"), "R16": ("sbuf", [16, 256], "bfloat16"),
     "KB": ("sbuf", [1, 256], "bfloat16"), "CR": ("sbuf", [2, 256], "float16"), "LG": ("sbuf", [2, 128], "bfloat16"),
     "LC": ("sbuf", [2, 128], "bfloat16"),
@@ -51,15 +60,15 @@ SCRATCH = {
     "V16": h16(2, 256), "FG": h16(2, 256),
     "THI": i32(1), "THJ": i32(2), "THF": f32(2), "THD": f32(512), "TH": f32(512),
     "W": b16(160), "WS": b16(4, 160), "I1K": b16(128), "ISG": b16(128), "ISV": b16(128), "BLKF": f32(128),
-    "DIAG": b16(256), "DIF": f32(16), "SQ": b16(3, 144), "TQ": b16(2048),
+    "DIAG": b16(256), "OFFD": b16(256), "OFFR": ("sbuf", [16, 256], "bfloat16"), "RAMP": f32(32), "BLKB": b16(128), "LAST": u16(16), "EX": b16(256), "SQ": b16(3, 144), "TQ": b16(2048),
     "RST": b16(256), "RS7": b16(256), "IOT": f32(256), "BIA": f32(256),
     "C16": f32(16), "PIO": i32(16), "PM": i32(16), "IDX": f32(16), "MUI": i32(1), "MU": f32(2),
     "CG": f32(256), "VC": f32(256), "WC": f32(256), "XC": f32(256),
     "XI": i32(2, 256), "PQ": i32(4, 16, 16), "ZI": i32(512), "RI": i32(2, 16, 16), "RA": i32(128), "RL": u16(512),
     "DB": b16(4096), "TURN": u16(4), "PA4": i32(2), "PF": f32(2),
     "U": b16(4096), "X16": h16(4, 8, 2, 16), "XT": h16(4, 8, 2, 16),
-    "NOV": b16(256), "NS": b16(256), "SV": b16(256), "NR": b16(256), "SB": b16(16), "S2": h16(3, 16), "KY": f32(256),
-    "SC": f32(512), "LF": f32(288), "LI": i32(272), "SAV": i32(32),
+    "NOV": b16(256), "NS": b16(256), "SV": b16(256), "NR": b16(256), "SB": b16(16), "S2": h16(2, 16), "KY": f32(256),
+    "CF": b16(16), "SS": b16(32), "SW": b16(16), "IDF": f32(128), "SD": i32(256), "SC": f32(256), "LF": f32(288), "LI": i32(272), "SAV": i32(32),
     "FI": i32(256), "FQ": i32(256), "EQ": f32(256), "NM": f32(256), "YO": f32(256),
     "FLD": f32(4, 2, 16), "FLT": f32(4, 2, 16), "FO": f32(4, 16),
     "PA": ("psum", [128, 512], "float32"), "PB": ("psum", [128, 512], "float32"), "PG": ("psum", [128, 512], "float32"),
@@ -116,16 +125,30 @@ def plan(nodes):
                     can.setdefault(nodes[j]["q"], []).append(j)
         return end
 
-    way = [0.0] * m
-    for n in range(m - 1, -1, -1):
-        way[n] = nodes[n]["cost"] + max([way[k] + lat for k, lat in succ[n]] + [nodes[n]["lat"]])
+    way = place([0.0] * m, succ, pred, [x["lat"] for x in nodes])
     best = None
     for _ in range(PASSES):
         end = place(way, pred, succ, [0.0] * m)
         span = max(end[n] + nodes[n]["lat"] for n in range(m))
         if best is None or span < best[0]:
-            best = (span, end)
+            best = (span, end, way)
         way = place(end, succ, pred, [x["lat"] for x in nodes])
+    rng = np.random.RandomState(0)
+    names = sorted(set(x["name"] for x in nodes))
+    for _ in range(NAMED):
+        more = dict((names[k], SHAKE * rng.randn()) for k in rng.randint(len(names), size=rng.randint(1, 5)))
+        way = [w + more.get(x["name"], 0.0) for w, x in zip(best[2], nodes)]
+        end = place(way, pred, succ, [0.0] * m)
+        span = max(end[n] + nodes[n]["lat"] for n in range(m))
+        if span <= best[0]:
+            best = (span, end, way)
+    for _ in range(TRIES):
+        at, wide = rng.rand() * best[0], 1.0 + 4.0 * rng.rand()
+        way = [w + SHAKE * rng.randn() if abs(e - at) < wide else w for w, e in zip(best[2], best[1])]
+        end = place(way, pred, succ, [0.0] * m)
+        span = max(end[n] + nodes[n]["lat"] for n in range(m))
+        if span <= best[0]:
+            best = (span, end, way)
     return sorted(range(m), key=lambda n: (best[1][n] - nodes[n]["cost"], n))
 
 
@@ -175,7 +198,7 @@ def rank_program(g, core, T, topo):
                 cur, before = [], cur
             deps |= set(before)
             banks[bank] = (q, cur + [n], before)
-        nodes.append({"q": q, "emit": emit, "deps": deps, "soft": soft - deps, "cost": cost, "lat": lat, "sem": sem, "inc": inc})
+        nodes.append({"q": q, "name": writes[0], "emit": emit, "deps": deps, "soft": soft - deps, "cost": cost, "lat": lat, "sem": sem, "inc": inc})
         for k in writes:
             lastw[k] = n
             readers[k] = set()
@@ -186,7 +209,7 @@ def rank_program(g, core, T, topo):
         add(q, lambda: fn(*a, **kw), reads, writes, cost, LAT, q, 1)
 
     def load(q, out, in_, sem, key, lat, reads=""):
-        add(q, lambda: ENG[q].dma_start(out, in_), reads, key, 0.06, lat, sem, 16)
+        add(q, lambda: ENG[q].dma_start(out, in_), reads, key + ("" if reads else " @" + q), 0.06, lat, sem, 16)
 
     def issue():
         cnt, seen, tok = {}, {}, {}
@@ -268,11 +291,11 @@ def rank_program(g, core, T, topo):
     ID = T.W[:, 16:144]
     R8 = T.R9[0:8, :]
 
-    def spread(reads, w, out, rhs):
-        mms(1024, reads + " tq", w, [(out(q), T.TQ[:, 128 * q:128 * q + 128], rhs, True, True) for q in range(16)])
+    def spread(reads, w, out, rhs, alone):
+        mms(1024, reads + " tq0 tq1 tq2 tq3", w, [(out(q), T.TQ[:, 128 * q:128 * q + 128], rhs, alone, alone or q == 15) for q in range(16)])
 
     load("sync", T.LS[:, 0:256], T.gs[:], "l_gs", "ls0", 1.9)
-    load("sync", T.SKI[:], T.sk[:], "l_sk", "ski", 3.4)
+    load("sync", T.SKI[:], T.sk[:], "l_sk", "ski", 4.2)
     load("sync", T.XR[:, 592:4096], T.x[:, 0:3504], "l_x0", "xr0", 6.0)
     load("s", T.LS[:, 256:512], T.gf[:], "l_gf", "ls1", 1.9)
     load("s", T.LS[:, 512:768], T.gcl[:], "l_gc", "ls2", 1.9)
@@ -281,20 +304,23 @@ def rank_program(g, core, T, topo):
     load("s", T.XR[:, 0:592], T.x[:, 3504:4096], "l_x1", "xr1", 5.0)
     XRK = "xr0 xr1 "
 
-    fill(512, "one", T.ONE[:], 1.0)
+    fill(256, "one", T.ONE[:], 1.0)
     fill(64, "r9", T.R9[:], 2448.0)
-    ts(512, "one", "l16t l16i", T.L16[:], T.ONE[0:9, :], 1961.0, OP.mult)
-    sel(144, "one", "z", T.Z[:], T.ONE[0:8, 0:144], [[1, 144]], -15, -16)
-    sel(128, "one r9", "r9", R8, T.ONE[0:8, 0:128], [[-1, 8], [0, 16]], 0, 1)
-    sel(160, "one", "w", T.W[:], T.ONE[:, 0:160], [[1, 160]], -16, -1)
-    iota(256, "iot", T.IOT[:], [[1, 256]], 0, 0)
+    ts(128, "one", "l16t", T.L16[:, 256:512], T.ONE[0:9, 0:256], 1961.0, OP.mult)
+    ts(128, "one", "l16i", T.L16[:, 768:1024], T.ONE[0:9, 0:256], 1961.0, OP.mult)
+    iota(16, "pio @g", T.PIO[:], [[0, 16]], 0, 1)
+    iota(16, "c16 @g", T.C16[:], [[16, 16]], 0, 0)
+    sel(144, "one", "z @g", T.Z[:], T.ONE[0:8, 0:144], [[1, 144]], -15, -16)
+    sel(128, "one r9", "r9 @g", R8, T.ONE[0:8, 0:128], [[-1, 8], [0, 16]], 0, 1)
+    sel(256, "one", "r16 @g", T.R16[:], T.ONE[0:16, 0:256], [[0, 16], [-1, 16]], 0, 1)
+    sel(160, "one", "w @g", T.W[:], T.ONE[:, 0:160], [[1, 160]], -16, -1)
+    iota(256, "iot @g", T.IOT[:], [[1, 256]], 0, 0)
     cp(256, "iot l16i", "l16i", T.L16[0:8, 768:1024], T.IOT[0:8, :])
-    sel(256, "one", "r16", T.R16[:], T.ONE[0:16, 0:256], [[0, 16], [-1, 16]], 0, 1)
-    iota(16, "c16", T.C16[:], [[16, 16]], 0, 0)
-    iota(16, "pio", T.PIO[:], [[0, 16]], 0, 1)
-    iota(256, "kb", T.KB[:], [[0, 16], [-1, 16]], 15, 0)
-    iota(128, "lg", T.LG[:], [[0, 128]], 1 << 19, -720 - (1 << 19))
-    iota(128, "lc", T.LC[:], [[0, 128]], 1 << 20, -720 - (1 << 20))
+    iota(256, "kb @g", T.KB[:], [[0, 16], [-1, 16]], 15, 0)
+    iota(128, "lg @g", T.LG[:], [[0, 128]], 1 << 19, -720 - (1 << 19))
+    iota(128, "lc @g", T.LC[:], [[0, 128]], 1 << 20, -720 - (1 << 20))
+    iota(256, "offr @g", T.OFFR[:], [[-2, 16], [0, 16]], -64, 0)
+    sel(256, "offr", "offr @g", T.OFFR[:], T.OFFR[:], [[0, 16], [-1, 16]], 0, 1)
     ts(128, "one", "cr", T.CR[:], T.ONE[0:2, 0:256], 421.0, OP.mult)
     cp(128, "kb cr", "cr", T.CR[0:1, :], T.KB[:])
     ts(16, "pio", "pm", T.PM[:], T.PIO[:], 15, OP.bitwise_and)
@@ -310,8 +336,10 @@ def rank_program(g, core, T, topo):
     fill(128, "rst", T.RST[:], 1.0)
     fill(16, "rst", T.RST[:, 0::16], 0.0)
     fill(128, "rs7", T.RS7[:], 64.0)
-    fill(16, "rs7", T.RS7[:, 0::16], -7.0)
-    fill(16, "thr", li(0), 1)
+    ts(16, "c16", "ramp", T.RAMP[:, 0:16], T.C16[:], -0.125, OP.mult)
+    ts(16, "c16", "ramp8", T.RAMP[:, 16:32], T.C16[:], -0.125, OP.mult, -8.0, OP.add)
+    cp(16, "ramp8 rs7", "rs7", T.RS7[:, 0::16], T.RAMP[:, 16:32])
+    act(128, "w", "idf", T.IDF[:], ID)
     act(128, "w", "i1k", T.I1K[:], ID, scale=1024.0)
     act(128, "w", "isg", T.ISG[:], ID, scale=float(-5 << 19))
     act(128, "w", "isv", T.ISV[:], ID, scale=float(1 << 19))
@@ -326,9 +354,10 @@ def rank_program(g, core, T, topo):
     for j, w in enumerate((16.0, 32.0, -16.0)):
         act(144, "PG1", "sq", T.SQ[:, j, :], T.PG[:, 128:272], scale=w)
     act(256, "PC0", "diag", T.DIAG[:], T.PC[:, 0:256])
-    act(16, "PC0", "dif", T.DIF[:], T.PC[:, 0:16])
-    for q in range(16):
-        act(128, "blkf dif", "tq", T.TQ[:, 128 * q:128 * q + 128], T.BLKF[:], AF.Identity, scale=T.DIF[:, q:q + 1])
+    mms(256, "r16 offr", "PB1", [(T.PB[:, 256:512], T.R16[:, 0:128], T.OFFR[:], True, True)])
+    act(256, "PB1", "offd", T.OFFD[:], T.PB[:, 256:512], AF.Identity, bias=64.0)
+    act(128, "PG0", "blkb", T.BLKB[:], T.PG[:, 0:128], scale=float(1 << 24))
+    ts(16, "c16", "last", T.LAST[:], T.C16[:], 15.0, OP.add)
 
     ts(1, "thi", "thj0", T.THJ[:, 0:1], T.THI[:], -1.0, OP.add)
     ts(1, "thj0", "thj1", T.THJ[:, 1:2], T.THJ[:, 0:1], 1, OP.arith_shift_right)
@@ -342,7 +371,9 @@ def rank_program(g, core, T, topo):
 
     cp(768, "ls0 ls1 ls2 l16t", "l16t", T.L16[0:8, 0:768], T.LS[:])
     mms(1024, "z l16t", "PA0", [(T.PA[:, 0:48], T.Z[:, 15 - q:143 - q], T.L16[0:8, q:768:16], q == 0, q == 15) for q in range(16)])
+    early = [n for n, x in enumerate(nodes) if x["q"] == "v"]
     cp(48, "PA0", "lu", T.LU[:], T.PA[:, 0:48])
+    nodes[-1]["soft"] |= set(early) - nodes[-1]["deps"]
     cp(48, "PA0", "tl", T.TL[:], T.PA[:, 0:48])
     ts(256, "fri", "frq", T.FRQ[:], T.FRI[:], 511 + (1 << 23), OP.bitwise_and)
     act(256, "fri", "PS0", T.PS[:, 0:256], T.FRI[:], AF.Identity, scale=2.0, bias=float(KE + B))
@@ -358,7 +389,9 @@ def rank_program(g, core, T, topo):
     def skeleton_table():
         for j in range(4):
             c = slice(256 * j, 256 * j + 256)
-            cast("ski", "sk16%d" % j, T.SK16[:, c], T.SKI[:, c], 256)
+            cast("ski", "sk16%d @g" % j, T.SK16[:, c], T.SKI[:, c], 256)
+        for j in range(4):
+            sel(512, "one", "tq%d @g" % j, T.TQ[:, 512 * j:512 * j + 512], T.ONE[:, 0:512], [[-1, 4], [-16, 8], [0, 16]], -4 * j, 1)
         for j, (p, bank) in enumerate((("PH", T.PH[:]), ("PX", T.PX[:]))):
             c = slice(512 * j, 512 * j + 512)
             act(512, "ski", "sgn%d" % j, T.SGN[:, c], T.SKI[:, c], AF.Sign, bias=-1023.5)
@@ -371,7 +404,7 @@ def rank_program(g, core, T, topo):
         ts(16, "sav", "i1", li(1), SG, 9, OP.arith_shift_right)
         act(16, "i1", "l5", lf(5), li(1), AF.Identity, bias=32.0)
         tt(32, "l5 sav", "l6", lf(6), lf(5), SCL, OP.mult)
-        ts(16, "l6", "i2", li(2), lf(6), 32.0, OP.add, 16.0, OP.mult)
+        act(16, "l6", "i2", li(2), lf(6), AF.Identity, scale=16.0, bias=512.0)
         ts(16, "i2", "i5", li(5), li(2), 1023 << 9, OP.bitwise_and)
         tt(32, "i5 idx", "l4", lf(4), li(5), T.IDX[:], OP.add)
 
@@ -385,20 +418,27 @@ def rank_program(g, core, T, topo):
         tt(2 * n, pi + " " + qi, zi, T.ZI[:, z + 16 * a:z + 16 * b], T.PQ[:, 2 * j, a:b, :], T.PQ[:, 2 * j + 1, a:b, :], OP.mult)
         if a == 0:
             a, c = BLOCKS[0][1], slice(64 * j, 64 * j + 64)
-            ts(-64, zi + " turn", "ra%d" % j, T.RA[:, c], T.ZI[:, z:z + 64].indirect(T.TURN[:]), 4, OP.arith_shift_right, 4095, OP.bitwise_and)
-            cp(64, "ra%d" % j, "rl%d0" % j, T.RL[:, z:z + 64], T.RA[:, c])
+            ts(64, zi, "ra%d" % j, T.RA[:, c], T.ZI[:, z:z + 64], 4, OP.arith_shift_right, 4095, OP.bitwise_and)
+            (cp if j else act)(-64, "turn ra%d" % j, "rl%d0" % j, T.RL[:, z:z + 64], T.RA[:, c].indirect(T.TURN[:]))
         if a < b:
             ts(16 * (b - a), zi, ri, T.RI[:, j, a:b, :], T.ZI[:, z + 16 * a:z + 16 * b], 4, OP.arith_shift_right, 4095, OP.bitwise_and)
-        for k, (lo, hi, c, d) in enumerate(BLOCKS):
-            if k and a < hi <= b:
-                cast(span("ri%d" % j, lo, hi), "rl%d%d" % (j, k), T.RL[:, z + OFF[k]:z + OFF[k + 1]], T.RI[:, j, lo:hi, c:d], hi - lo, d - c)
+
+    def offsets(j, casts):
+        for ks in casts:
+            lo, hi, c, d = BLOCKS[ks[0]][0], BLOCKS[ks[-1]][1], BLOCKS[ks[0]][2], BLOCKS[ks[0]][3]
+            cast(span("ri%d" % j, lo, hi), " ".join("rl%d%d" % (j, k) for k in ks) + " @g",
+                 T.RL[:, 256 * j + OFF[ks[0]]:256 * j + OFF[ks[-1] + 1]], T.RI[:, j, lo:hi, c:d], hi - lo, d - c)
+
+    def halves(j, u):
+        cast(span("pi%d" % j, 8 * u, 8 * u + 8) + " " + span("qi%d" % j, 8 * u, 8 * u + 8), "x16%d%d @g" % (j, u),
+             T.X16[:, 2 * j:2 * j + 2, :, u, :], T.PQ[:, 2 * j:2 * j + 2, 8 * u:8 * u + 8, :], 2, 8, 16)
 
     OFF = [0]
     for a, b, c, d in BLOCKS:
         OFF.append(OFF[-1] + (b - a) * (d - c))
 
     def payload(j, p, lhs, stop):
-        run("v", V.transpose, "x16%d0 x16%d1" % (j, j), "xt%d" % j, us(256), T.XT[:, 2 * j:2 * j + 2], T.X16[:, 2 * j:2 * j + 2])
+        run("v", V.transpose, "x16%d0 x16%d1" % (j, j), "xt%d @db" % j, us(256), T.XT[:, 2 * j:2 * j + 2], T.X16[:, 2 * j:2 * j + 2])
         calls = [(T[p][:, 0:256], lhs, T.CR[:], True, False)]
         for u in range(2):
             for gl in range(2):
@@ -408,64 +448,76 @@ def rank_program(g, core, T, topo):
                                   False, stop and u + gl + f == 3))
         mms(1280, "xt%d cr lg lc ws0 ws1 wt0 wt1" % j, p + "0", calls)
 
-    sent = 0
+    sent, marks = 0, []
     PV0, PV1, PS0, PS1 = T.PV[:, 0:256], T.PV[:, 256:512], T.PS[:, 0:256], T.PS[:, 256:512]
     for t in range(RO):
+        marks.append(len(nodes))
         F = T["F%d" % t]
         fo, fg, fs = "f%do" % t, "f%dg" % t, "f%ds" % t
         last = t == RO - 1
         if t == 0:
-            for j, (lo, bank, key) in enumerate(((256, T.PX[:, 0:256], "PX0"), (768, T.PH[:, 0], "PH0"))):
-                cp(-256, "ski lu", "v16%d" % j, T.V16[:, j, :], T.SKI[:].indirect(T.LU[:, 32 * j:32 * j + 16]))
-                ts(128, "v16%d" % j, "fg%d" % j, T.FG[:, j, :], T.V16[:, j, :], 1024.0, OP.is_ge, -5120.0, OP.mult)
-                mms(768, "r9 l16t l16i i1k v16%d fg%d" % (j, j), key,
-                    [(bank, T.R9[:], T.L16[:, lo:lo + 256], True, False), (bank, T.I1K[:], T.V16[:, j, :], False, False),
-                     (bank, T.I1K[:], T.FG[:, j, :], False, True)])
-            act(-256, "lu f0o f0g", span("cg"), T.CG[:], F[:, 0:512].indirect(T.LU[:, 16:32]))
-            mms(512, "w f16 fg1", "PH1", [(T.PH[:, 1], ID, T.F16[:], True, False), (T.PH[:, 1], ID, T.FG[:, 1, :], False, True)])
+            for j, a, b in [(0, a, b) for a, b in GOALS] + [(1, 0, 16)]:
+                c, k = slice(16 * a, 16 * b), "%d%d" % (j, a)
+                bank, key = [(T.PA[:, 256 + c.start:256 + c.stop], "PA1"), (T.PX[:, c], "PX0"), (T.PH[:, 0], "PH0")][2 if j else int(a > 0)]
+                cp(c.start - c.stop, "ski lu", "v16" + k, T.V16[:, j, c], T.SKI[:].indirect(T.LU[:, 32 * j + a:32 * j + b]))
+                ts(8 * (b - a), "v16" + k, "fg" + k, T.FG[:, j, c], T.V16[:, j, c], 1024.0, OP.is_ge, -5120.0, OP.mult)
+                mms(16 * (b - a), "r9 l16t l16i", key, [(bank, T.R9[:], T.L16[:, 256 + 512 * j + c.start:256 + 512 * j + c.stop], True, False)])
+                mms(32 * (b - a), "i1k v16%s fg%s" % (k, k), key,
+                    [(bank, T.I1K[:], T.V16[:, j, c], False, False), (bank, T.I1K[:], T.FG[:, j, c], False, True)])
+            act(-256, "lu f0o", span("cg"), T.CG[:], F[:, 0:256].indirect(T.LU[:, 16:32]))
+            mms(512, "w f16 fg10 PH0", "PH1", [(T.PH[:, 1], ID, T.F16[:], True, False), (T.PH[:, 1], ID, T.FG[:, 1, :], False, True)])
             free = dict(scale=-4096.0, bias=float(B - 4096 * 5120))
         else:
             act(256, fg, "PX0", T.PX[:, 0:256], F[:, 256:512])
             act(-256, "ch " + fo + " " + fg, "wc", T.WC[:], F[:, 0:512].indirect(T.CH[:, 16:32]))
-            cp(16, fs, "sl", T.SL[:], F[:, 512:528])
+            act(16, fs, "sl", T.SL[:], F[:, 512:528])
         if t == 0:
-            act(256, "PH1", "PS0", PS0, T.PH[:, 1], AF.Identity, **free)
+            act(256, "PH1", "PV1", PV1, T.PH[:, 1], AF.Identity, **free)
             act(256, "PH1", "fr16", T.FR16[:], T.PH[:, 1], AF.Identity, **free)
+            mms(1024, "idf base", "PS0", [(PS0, T.IDF[:], T.BASE[:], True, False)])
         for a, b in GOALS:
             c = slice(16 * a, 16 * b)
             if t:
                 tt(-16 * (b - a), "skv0 skv1 sl bia", span("cg", a, b), T.CG[:, c], T.SKV[:].indirect(T.SL[:, a:b]), T.BIA[:, c], OP.add)
-            tt(16 * (b - a), "PX0 " + span("cg", a, b), span("xi0", a, b), T.XI[:, 0, c], T.PX[:, c], T.CG[:, c], OP.max)
+            src, key = (T.PX[:, c], "PX0 ") if t or a else (T.PA[:, 256 + c.start:256 + c.stop], "PA1 ")
+            tt(16 * (b - a), key + span("cg", a, b), span("xi0", a, b), T.XI[:, 0, c], src, T.CG[:, c], OP.max)
             recs(0, a, b)
-        for j, ks in enumerate(PARTS):
+        halves(0, 0)
+        offsets(0, CASTS[:2])
+        halves(0, 1)
+        offsets(0, CASTS[2:])
+        for ks in UPARTS:
             lo, hi = OFF[ks[0]], OFF[ks[-1] + 1]
-            act(16 * (lo - hi), XRK + " ".join("rl0%d" % k for k in ks), "u%d @u" % j, T.U[:, 16 * lo:16 * hi], T.XR[:].indirect(T.RL[:, lo:hi]))
+            act(16 * (lo - hi), XRK + " ".join("rl0%d" % k for k in ks), " ".join("u%d" % k for k in ks) + " @u",
+                T.U[:, 16 * lo:16 * hi], T.XR[:].indirect(T.RL[:, lo:hi]))
         if t == 0:
             tt(256, "PH0 " + fo, "xc", T.XC[:], T.PH[:, 0], F[:, 0:256], OP.max)
         else:
             tt(256, "PV1 wc", "xc", T.XC[:], PV1, T.WC[:], OP.max)
         for a, b in CLAUSES:
             c = slice(16 * a, 16 * b)
-            tt(16 * (b - a), "PS0 PV0 " + span("xi0", a, b), span("PVt", a, b), T.PV[:, c], T.PS[:, c], T.XI[:, 0, c], OP.add)
+            src = T["PX" if t else "PV"][:, 256 + 16 * a:256 + 16 * b]
+            tt(16 * (b - a), ("PX1 " if t else "PV1 ") + span("xi0", a, b), span("PVt", a, b), T.PV[:, c], src, T.XI[:, 0, c], OP.add)
             tt(16 * (b - a), "xc " + span("PVt", a, b), span("xi1", a, b), T.XI[:, 1, c], T.PV[:, c], T.XC[:, c], OP.max)
             recs(1, a, b)
-        for j in range(2):
-            for u in range(2):
-                cast(span("pi%d" % j, 8 * u, 8 * u + 8) + " " + span("qi%d" % j, 8 * u, 8 * u + 8), "x16%d%d" % (j, u),
-                     T.X16[:, 2 * j:2 * j + 2, :, u, :], T.PQ[:, 2 * j:2 * j + 2, 8 * u:8 * u + 8, :], 2, 8, 16)
+        halves(1, 0)
+        offsets(1, CASTS[:1])
+        halves(1, 1)
+        offsets(1, CASTS[1:])
+        if last:
+            mms(1024, "idf base PH1", "PH0", [(T.PH[:, 0], T.IDF[:], T.BASE[:], True, True)])
+        calls = [(T.PH[:, 1], ID, T.FR16[:], True, False)]
+        for u in range(2):
+            calls += [(T.PH[:, 1, 8 * u:8 * u + 8, :], T.I1K[:], T.X16[:, 0, :, u, :], False, False),
+                      (T.PH[:, 1, 8 * u:8 * u + 8, :], ID, T.X16[:, 1, :, u, :], False, u == 1)]
+        mms(768, "w i1k fr16 x1600 x1601", "PH1", calls)
+        tt(256, "PH1 " + fo, "yb", T.YB[:], T.PH[:, 1], F[:, 0:256], OP.max)
+        if last:
+            tt(256, "yb PH0", "eq", T.EQ[:], T.PH[:, 0], T.YB[:], OP.is_equal)
         if t == 0:
             skeleton_table()
             saved_derived()
-        calls = [(PS1, ID, T.FR16[:], True, False)]
-        for u in range(2):
-            calls += [(T.PS[:, 256 + 128 * u:384 + 128 * u], T.I1K[:], T.X16[:, 0, :, u, :], False, False),
-                      (T.PS[:, 256 + 128 * u:384 + 128 * u], ID, T.X16[:, 1, :, u, :], False, u == 1)]
-        mms(768, "w i1k fr16 x1600 x1601", "PS1", calls)
-        tt(256, "PS1 " + fo, "yb", T.YB[:], PS1, F[:, 0:256], OP.max)
-        if last:
-            tt(512, "yb base", "eq", T.EQ[:], T.YB[:], T.BASE[:], OP.is_equal)
         payload(0, "PG", T.LG[:], True)
-        payload(1, "PC", T.LC[:], False)
         cut = [slice(0, 16 * SPLIT), slice(16 * SPLIT, 256)]
         D = [T.PA[:, cut[0]], T.PB[:, cut[1]]]
         for u, p in enumerate(("PA0", "PB0")):
@@ -473,8 +525,10 @@ def rank_program(g, core, T, topo):
         for j, ks in enumerate(PARTS):
             lo, hi = OFF[ks[0]], OFF[ks[-1] + 1]
             e = slice(16 * lo, 16 * hi)
-            tt(e.start - e.stop, XRK + " ".join("rl1%d" % k for k in ks) + " u%d" % j, "db%d @db" % j, T.DB[:, e],
+            tt(e.start - e.stop, XRK + " ".join("rl1%d u%d" % (k, k) for k in ks), "db%d @db" % j, T.DB[:, e],
                T.XR[:].indirect(T.RL[:, 256 + lo:256 + hi]), T.U[:, e], OP.subtract)
+            if j == LATE:
+                payload(1, "PC", T.LC[:], False)
             for k in ks:
                 a, b, c, d = BLOCKS[k]
                 AB, u = T["AB%d" % k], int(a >= SPLIT)
@@ -501,28 +555,32 @@ def rank_program(g, core, T, topo):
             c2 = slice(256 + c.start, 256 + c.stop)
             tt(n, p + " th0", "nov" + k, T.NOV[:, c], D[u], T.TH[:, c], OP.is_le)
             scan(n // 2, "rs7 nov" + k, "ns" + k, T.NS[:, c], T.RS7[:, c], T.NOV[:, c], OP.min, OP.add)
+            h = slice(c.start // 16, c.stop // 16)
+            tt(32, "ramp ns" + k, "cf" + k, T.CF[:, h], T.NS[:, c.start + 15:c.stop:16], T.RAMP[:, h], OP.is_le)
+            act(16, "cf" + k, "sb" + k, T.SB[:, h], T.CF[:, h], AF.Identity, scale=-float(1 << 24), bias=float(1 << 24))
+            if u == 0 and t:
+                mms(1024, "sb0 tq0 tq1 tq2 tq3", "PS0", [(T.PS[:, q:c.stop:16], T.TQ[:, 128 * q:128 * q + 128], T.SB[:, h], False, False)
+                                                        for q in range(16)])
+            else:
+                tt(-n, "ns%s last offd" % ("0" if u == 0 else "0 ns1"), "ex" + k, T.EX[:, c],
+                   T.NS[:, 0:c.stop].indirect(T.LAST[:, h]), T.OFFD[:, c], OP.is_gt)
+                mms(n, "blkb ex" + k, "PS0", [(T.PS[:, c], T.BLKB[:], T.EX[:, c], False, u == 1)])
             tt(n, p + " nov" + k, "ky" + k, T.KY[:, c], D[u], T.NOV[:, c], OP.mult)
             scan(n, "rst ky" + k, "PVk" + k + (" PV1" if u == 0 else ""), T.PV[:, c2], T.RST[:, c], T.KY[:, c], OP.mult, OP.max)
             tt(n, "PVk%s ky%s" % (k, k), "nr" + k, T.NR[:, c], T.PV[:, c2], T.KY[:, c], OP.is_gt)
             scan(n, "PG0 nr" + k, "sc" + k, T.SC[:, c], T.NR[:, c], T.PG[:, c], OP.mult, OP.max)
-            tt(n, p + " th1", "sv" + k, T.SV[:, c], D[u], T.TH[:, c2], OP.is_le)
-        tt(32, "ns0 ns1 thr", "sb", T.SB[:], T.NS[:, 15::16], li(0), OP.is_gt)
-        spread("sb", "PS0", lambda q: T.PS[:, q:256:16], T.SB[:])
-        tt(32, "ns0 ns1 thr", "l10", lf(10), T.NS[:, 15::16], li(0), OP.is_le)
-        tt(32, "l10 l1", "l11", lf(11), lf(10), lf(1), OP.mult)
-        mms(256, "sv0 sv1 isv", "PC0", [(T.PC[:, 0:256], T.ISV[:], T.SV[:], False, True)])
+        tt(32, "cf0 cf1 l1", "l11", lf(11), T.CF[:], lf(1), OP.mult)
         tt(32, "sc0 sc1 l11", "i6", li(6), T.SC[:, 15:256:16], lf(11), OP.max)
-        tt(256, "PS0 yb", "PV0 " + span("PVt"), PV0, PS0, T.YB[:], OP.mult)
         if last:
-            tt(256, "PV0 base", "fi", T.FI[:], PV0, T.BASE[:], OP.max)
+            tt(256, "PS0 yb", "fi", T.FI[:], PS0, T.YB[:], OP.min)
         else:
-            tt(256, "PV0 base", fo, F[:, 0:256], PV0, T.BASE[:], OP.max)
+            tt(256, "PS0 yb", fo, F[:, 0:256], PS0, T.YB[:], OP.min)
             ts(16, "i6", "i8", li(8), li(6), 511, OP.bitwise_and)
+            act(16, "i8", "fl", T.FL[:], li(8))
             ts(16, "i6", "i9", li(9), li(6), 9, OP.arith_shift_right, 1023, OP.bitwise_and)
-            cp(16, "i8", "fl", T.FL[:], li(8))
             C = T["COL%d" % t]
-            act(16, "i9", "cols", C[:, 256:272], li(9))
-            cp(-256, "fl " + fo + " " + fg, "col", C[:, 0:256], F[:, 0:512].indirect(T.FL[:]))
+            cp(16, "i9", "cols", C[:, 256:272], li(9))
+            act(-256, "fl " + fo + " " + fg, "col", C[:, 0:256], F[:, 0:512].indirect(T.FL[:]))
             d = 1 + t % (N - 1)
             dst = T.cores[(rank + d) % N]
             rel = routes(topo, core, dst)
@@ -534,12 +592,12 @@ def rank_program(g, core, T, topo):
                     es = topo.engines(core, c)
                     tr.append(RemoteDMATransfer(dst_ids=[DstId(rid=rid, pnc=pid)], dma_engine_mask=only(es[HOP * k:], HOP),
                                                 remote_sem=T.sem["in%d" % t], src=C[:, k * w:(k + 1) * w], dst=T["RB%d" % t][:, 0:w]))
-                add("gq", lambda tr=tr: hand(g.remote_dma_fused(tr, local_sem=T.sem.sent)), "cols col", "go", 1.0, 5.0, None, 0)
+                add("gq", lambda tr=tr: hand(g.remote_dma_fused(tr, local_sem=T.sem.sent)), "cols col", "go", 0.5, 3.6, None, 0)
                 sent += HOP * len(rel)
             else:
                 rid, pid = topo.addr(dst, core)
                 add("gq", lambda a=(T["F%d" % (t + 1)][:, 256:528], C[:], T.sem["arr%d" % t], T.sem.sent, pid, rid, topo.mask(core, dst)):
-                    hand(g.remote_dma(*a)), "cols col", "go", 1.0, 3.0, None, 0)
+                    hand(g.remote_dma(*a)), "cols col", "go", 0.5, 2.0, None, 0)
                 sent += len(topo.engines(core, dst))
             src = T.cores[(rank - d) % N]
             rin = routes(topo, src, core)
@@ -547,52 +605,58 @@ def rank_program(g, core, T, topo):
             add("net", lambda: None, "go", "f%dg f%ds" % (t + 1, t + 1), 0.0, 0.0, "arr%d" % t, n)
             act(256, fo, "f%do" % (t + 1), T["F%d" % (t + 1)][:, 0:256], F[:, 0:256])
             act(256, fo, "f16", T.F16[:], F[:, 0:256])
-            mms(64, "sb diag", "PG1", [(T.PG[:, 256:272], T.DIAG[:, 0:128], T.SB[:], True, True)])
-        tt(32, "l10 l4", "l13", lf(13), lf(10), lf(4), OP.mult)
-        scan(256, "PC0 nr0 nr1", "sc2", T.SC[:, 256:512], T.NR[:], T.PC[:, 0:256], OP.mult, OP.max)
-        tt(32, "sc2 sb", "l14", lf(14), T.SC[:, 271::16], T.SB[:], OP.mult)
+            mms(64, "cf0 cf1 diag", "PG1", [(T.PG[:, 256:272], T.DIAG[:, 0:128], T.CF[:], True, True)])
+        for u, p in enumerate(("PA0", "PB0")):
+            c = cut[u]
+            tt(c.stop - c.start, p + " th1", "sv%d" % u, T.SV[:, c], D[u], T.TH[:, 256 + c.start:256 + c.stop], OP.is_le)
+        mms(256, "sv0 sv1 isv", "PC0 @w", [(T.PC[:, 0:256], T.ISV[:], T.SV[:], False, True)])
+        if not last:
+            mms(1024, "idf base PS0", "PS1 @w", [(PS1, T.IDF[:], T.BASE[:], True, False)])
+        tt(32, "cf0 cf1 l4", "l13", lf(13), T.CF[:], lf(4), OP.mult)
+        for u in range(2):
+            scan(cut[u].stop - cut[u].start, "PC0 nr%d" % u, "sd%d" % u, T.SD[:, cut[u]], T.NR[:, cut[u]], T.PC[:, cut[u]], OP.mult, OP.max)
+        ts(16, "sd0 sd1", "i15", li(15), T.SD[:, 15::16], 19, OP.arith_shift_right, 1, OP.bitwise_and)
+        tt(32, "i15 cf0 cf1", "ss1", T.SS[:, 16:32], li(15), T.CF[:], OP.max)
+        tt(32, "ss1 cf0 cf1", "ss0", T.SS[:, 0:16], T.SS[:, 16:32], T.CF[:], OP.subtract)
+        tt(32, "sd0 sd1 sb0 sb1", "l14", lf(14), T.SD[:, 15::16], T.SB[:], OP.min)
         tt(32, "l13 l14", "i10", li(10), lf(13), lf(14), OP.add)
-        ts(16, "i10", "i15", li(15), li(10), 19, OP.arith_shift_right, 1, OP.bitwise_and)
         ts(16, "i10", "i13", li(13), li(10), 9, OP.arith_shift_right, 1023, OP.bitwise_and)
         ts(16, "i6", "i12", li(12), li(6), (1 << 19) - 1, OP.bitwise_and)
-        tt(32, "i15 l10", "i16", li(16) if not last else T.S2[:, 2, :], li(15), lf(10), OP.add)
         tt(64, "i12 i13 sav", "l7", lf(7, 2), li(12, 2), T.SAV[:], OP.subtract)
+        tt(64, "l7 ss0 ss1", "l16", lf(16, 2), lf(7, 2), T.SS[:], OP.mult)
+        tt(64, "l16 sav", "sav", T.SAV[:], lf(16, 2), T.SAV[:], OP.add)
         if not last:
             ts(16, "i10", "i14", li(14), li(10), 511, OP.bitwise_and)
-            cp(32, "i13 i14", "ch", T.CH[:], li(13, 2))
-            cp(16, "i14", "s20", T.S2[:, 0, :], li(14))
+            act(32, "i13 i14", "ch", T.CH[:], li(13, 2))
+            act(16, "i14", "s20", T.S2[:, 0, :], li(14))
             tt(32, "i14 idx", "s21", T.S2[:, 1, :], li(14), T.IDX[:], OP.not_equal)
-            cp(16, "i15", "s22", T.S2[:, 2, :], li(15))
+            act(16, "ss0", "sw", T.SW[:], T.SS[:, 0:16], scale=float(1 << 24))
             act(-256, "skv0 skv1 ch", "vc", T.VC[:], T.SKV[:].indirect(T.CH[:, 0:16]))
             act(256, "vc", "rvc", T.RVC[:], T.VC[:], AF.Relu, bias=float(-2 * B))
             calls = [(T.PH[:, :, :, q], T.TQ[:, 128 * q:128 * q + 128], T.S2[:, 0:2, :], q == 0, False) for q in range(16)]
-            mms(1024, "s20 s21 tq", "PH0 PH1", calls)
-            mms(512, "w f16 rvc", "PH1", [(T.PH[:, 1], ID, T.F16[:], False, False), (T.PH[:, 1], ID, T.RVC[:], False, True)])
+            mms(1024, "s20 s21 tq0 tq1 tq2 tq3", "PH0 PH1 @w", calls)
+            mms(512, "w f16 rvc", "PH1 @w", [(T.PH[:, 1], ID, T.F16[:], False, False), (T.PH[:, 1], ID, T.RVC[:], False, True)])
             free = dict(scale=-float(1 << 24), bias=float(B))
-            act(256, "PH1", "PS0", PS0, T.PH[:, 1], AF.Identity, **free)
+            act(256, "PH1", "PX1", T.PX[:, 256:512], T.PH[:, 1], AF.Identity, **free)
             act(256, "PH1", "fr16", T.FR16[:], T.PH[:, 1], AF.Identity, **free)
             tt(256, "PH0 vc", "PV1 PVk0 PVk1", PV1, T.PH[:, 0], T.VC[:], OP.add)
-            spread("s22", "PS1", lambda q: T.PS[:, 256 + q:512:16], T.S2[:, 2, :])
-            tt(256, "PS1 yb", "PV0", PV0, PS1, T.YB[:], OP.mult)
-            tt(256, "PV0 base", "base", T.BASE[:], PV0, T.BASE[:], OP.max)
-            ts(16, "PG1", "i3", li(3), T.PG[:, 256:272], 1.0, OP.add)
-            ts(16, "i3", "thr", li(0), li(3), 1, OP.bitwise_and)
-            tt(64, "l7 i15 i16", "l16 l17", lf(16, 2), lf(7, 2), li(15, 2), OP.mult)
-            tt(64, "l16 l17 sav", "sav", T.SAV[:], lf(16, 2), T.SAV[:], OP.add)
+            spread("sw", "PS1 @w", lambda q: T.PS[:, 256 + q:512:16], T.SW[:], False)
+            tt(256, "PS1 yb", "base", T.BASE[:], PS1, T.YB[:], OP.min)
+            mms(1024, "idf base", "PS0", [(PS0, T.IDF[:], T.BASE[:], True, False)])
+            act(16, "PG1", "i3", li(3), T.PG[:, 256:272])
+            ts(16, "i3", "i4", li(4), li(3), 1, OP.bitwise_and)
+            tt(32, "i4 ramp8", "rs7", T.RS7[:, 0::16], li(4), T.RAMP[:, 16:32], OP.add)
             saved_derived()
-    spread("i16", "PS1", lambda q: T.PS[:, 256 + q:512:16], T.S2[:, 2, :])
+    spread("ss1", "PH0", lambda q: T.PH[:, 0, :, q], T.SS[:, 16:32], True)
     ts(256, "fi", "fq", T.FQ[:], T.FI[:], 1023, OP.bitwise_and)
     act(256, "fi", "PX0", T.PX[:, 0:256], T.FI[:], AF.Identity, bias=float(-B - 606239))
     tt(256, "PX0 fq", "yo", T.YO[:], T.PX[:, 0:256], T.FQ[:], OP.add)
     act(256, "yo", "PX1", T.PX[:, 256:512], T.YO[:], AF.Relu)
-    tt(256, "PS1 eq", "nm", T.NM[:], PS1, T.EQ[:], OP.max)
+    tt(256, "PH0 eq", "nm", T.NM[:], T.PH[:, 0], T.EQ[:], OP.max)
     tt(256, "PX1 nm yo", "yo", T.YO[:], T.PX[:, 256:512], T.NM[:], OP.subtract)
     load("sync", T.yf[:], T.YO[:], "out", "yf", 1.9, "yo")
 
     ts(16, "i10", "i11", li(11), li(10), (1 << 19) - 1, OP.bitwise_and)
-    tt(32, "l7 i15", "l16", lf(16), lf(7), li(15), OP.mult)
-    tt(32, "l7 i16", "l17", lf(17), lf(8), T.S2[:, 2, :], OP.mult)
-    tt(64, "l16 l17 sav", "sav", T.SAV[:], lf(16, 2), T.SAV[:], OP.add)
     for j, (key, src) in enumerate((("i11 i12", li(11, 2)), ("sav", T.SAV[:]))):
         ts(32, key + " mu0", "fld%d0" % j, T.FLD[:, 2 * j:2 * j + 2, 0, :], src, T.MU[:, 0:1], OP.mult)
         act(32, key + " mu1", "fld%d1" % j, T.FLD[:, 2 * j:2 * j + 2, 1, :], src, AF.Identity, scale=T.MU[:, 1:2])
@@ -600,6 +664,17 @@ def rank_program(g, core, T, topo):
         tt(64, "flt%d" % j, "fo%d" % j, T.FO[:, 2 * j:2 * j + 2, :], T.FLT[:, 2 * j:2 * j + 2, 0, :], T.FLT[:, 2 * j:2 * j + 2, 1, :], OP.add)
     for j, y in enumerate((T.yc, T.yg, T.ysg, T.yk)):
         load("sync" if j % 2 else "s", y[:], T.FO[:, j, :], "out", "y%d" % j, 1.9, "fo%d" % (j // 2))
+    def keep(line, lo, hi):
+        at = [[n for n in range(lo, hi) if nodes[n]["name"] == k][:1] for k in line.split()]
+        at = [a[0] for a in at if a]
+        for a, b in zip(at, at[1:]):
+            nodes[b]["soft"] |= set([a]) - nodes[b]["deps"]
+    for line in FIRST:
+        keep(line, 0, len(nodes))
+    marks.append(len(nodes))
+    for t in range(RO):
+        for line in EACH:
+            keep(line.replace("#", str(t)).replace("+", str(t + 1)), marks[t], marks[t + 1])
     cnt, seen = issue()
     g.sync.wait_ge(T.sem.out, cnt["out"])
     g.wait_ge(T.sem.sent, sent)

@@ -16,11 +16,16 @@ CLAUSES = [(0, 4), (4, 16)]
 RELU = 8
 SPLIT = 12
 LAT, GAP, PATIENCE, PASSES = 0.18, 0.8, 0.3, 6
-NAMED, TRIES, SHAKE = 800, 400, 1.2
-FIRST = ["blkf sq diag PS0 i1k thd0 thd1 f0o f16 cg_0 th0 base idf ws0 ws1 wt0 wt1 sgn0 PV1 fr16 u0 ab7 th1 sgn1", "thf0 thf1 frq ow",
-         "v1600 v1604 v1610", "fg00 fg04 fg10"]
-EACH = ["sl PX0 wc", "fl col f16 ch rvc", "col f+o", "cg_0 cg_4 xi0_0 xi0_4", "nov0 ky0 ns0 PVk0 cf0 nr0 sc0",
-        "nov1 ky1 ns1 PVk1 ex1 nr1 sc1 i6 i8 i9 sd0"]
+WIDE = 256
+AHEAD = 0.5
+WAY = [3.2, 1.6, 2.8]
+SEED = 2
+EARLY, HEAT, MOVES, SPEEDS = 0.1, 0.3, 24000, [(1.0, 0.15, 1.1), (1.2, 0.24, 0.9)]
+FIRST = ["blkb sq diag PS0 i1k l16i2 f0o f16 ws0 ws1 cg_0 wt0 wt1 fr0 u0", "v1600 v1604 v1610", "fg00 fg04 fg10",
+         "l16c frq ow thj0", "PH1 PC1", "PG2 pre0", "xr1 blkb", "ab7 sgn0 sgn1"]
+EACH = ["slb PX0 wc x16a x1601 x1600 rl00 u0", "su fl cols col f16 ch s20 vc rvc sw fr16 f+o",
+        "cg_0 xi0_0 cg_12 pi0_0 qi0_0 xi0_4 pi0_4 zi0_0 qi0_4 ra0 xc xi1_0 xt0 pi1_0 qi1_0 zi0_4 zi1_0 ri0_4 xi1_4 ra1 qi1_4 pi1_4 rl10 zi1_4 yb ri1_4",
+        "nov0 sv0 ns0 ky0 cf0 PVk0 nov1 sv1 nr0 ky1 ns1 PVk1 cf1 sc0 nr1 ex1 l111 sc1 sd1 i61 l13 i91 i8 f#o sd0 l14 i15 i10 i14 i13 s21"]
 PLANS = {}
 CYC, GAT = 0.00083, 1.5
 HOP = 8
@@ -48,20 +53,21 @@ def u16(*s):
 
 
 SCRATCH = {
-    "XR": b16(4096), "SKI": i32(1024), "SK16": h16(1024), "SGN": b16(1024), "SKV": f32(1024), "FRI": i32(256), "FRQ": i32(256),
-    "OW": f32(256), "BASE": f32(256), "YB": f32(256), "F16": b16(256), "FR16": b16(256), "RVC": b16(256),
+    "XR": b16(4096), "SKI": i32(1024), "SK16": h16(1024), "SGN": h16(1024), "SKV": f32(1024), "FRI": i32(256), "FRQ": i32(256),
+    "OW": f32(256), "BASE": f32(256), "YB": f32(256), "F16": b16(256), "FR16": b16(256), "RVC": b16(256), "B16": b16(256),
     "F0": f32(528), "F1": f32(528), "F2": f32(528), "F3": f32(528),
     "COL0": f32(272), "COL1": f32(272), "COL2": f32(272), "RB0": f32(136), "RB2": f32(136),
+    "SU": u16(3, 16), "SL": u16(3, 16), "SLB": u16(8),
     "LS": ("sbuf", [8, 768], "int32"), "L16": ("sbuf", [9, 1024], "float16"), "ONE": b16(512),
     "R9": ("sbuf", [9, 128], "bfloat16"), "Z": ("sbuf", [8, 144], "bfloat16"), "R16": ("sbuf", [16, 256], "bfloat16"),
     "KB": ("sbuf", [1, 256], "bfloat16"), "CR": ("sbuf", [2, 256], "float16"), "LG": ("sbuf", [2, 128], "bfloat16"),
     "LC": ("sbuf", [2, 128], "bfloat16"),
-    "LU": u16(48), "SL": u16(16), "FL": u16(16), "CH": u16(32), "TL": f32(48),
+    "LU": u16(48), "FL": u16(16), "CH": u16(32), "TL": f32(48),
     "V16": h16(2, 256), "FG": h16(2, 256),
-    "THI": i32(1), "THJ": i32(2), "THF": f32(2), "THD": f32(512), "TH": f32(512),
-    "W": b16(160), "WS": b16(4, 160), "I1K": b16(128), "ISG": b16(128), "ISV": b16(128), "BLKF": f32(128),
+    "THI": i32(1), "THJ": i32(3), "THF": f32(2), "THD": h16(512), "TH": f32(512),
+    "W": b16(160), "WS": b16(4, 160), "I1K": b16(128), "ISV": b16(128), "ISG": b16(128),
     "DIAG": b16(256), "OFFD": b16(256), "OFFR": ("sbuf", [16, 256], "bfloat16"), "RAMP": f32(32), "BLKB": b16(128), "LAST": u16(16), "EX": b16(256), "SQ": b16(3, 144), "TQ": b16(2048),
-    "RST": b16(256), "RS7": b16(256), "IOT": f32(256), "BIA": f32(256),
+    "RST": b16(256), "RS7": b16(256), "BIA": f32(256),
     "C16": f32(16), "PIO": i32(16), "PM": i32(16), "IDX": f32(16), "MUI": i32(1), "MU": f32(2),
     "CG": f32(256), "VC": f32(256), "WC": f32(256), "XC": f32(256),
     "XI": i32(2, 256), "PQ": i32(4, 16, 16), "ZI": i32(512), "RI": i32(2, 16, 16), "RA": i32(128), "RL": u16(512),
@@ -77,14 +83,15 @@ SCRATCH = {
 }
 for _j, (_a, _b, _c, _d) in enumerate(BLOCKS):
     SCRATCH["AB%d" % _j] = b16(_b - _a, _d - _c, 16) if _j else b16(1024)
-SEMAPHORES = LOADS + ["v", "s", "pe", "gq", "out", "sent", "in0", "in2", "arr0", "arr1", "arr2"]
+SEMAPHORES = LOADS + ["v", "s", "pe", "gq", "out", "sent", "in0", "in2", "arr0", "arr1", "arr2", "list0", "list1", "list2"]
 
 
 def routes(topo, a, b):
     if topo.may_write(a, b):
-        return []
+        return [], None
     own = [c for c in topo.cores_of(a) if c != a and topo.may_write(c, b)]
-    return [[c for c in own if topo.die(c) == die][0] for die in sorted(set(topo.die(c) for c in own))]
+    rel = [[c for c in own if topo.die(c) == die][0] for die in sorted(set(topo.die(c) for c in own))]
+    return rel, [c for c in own if c not in rel and topo.die(c) == topo.die(a)][0]
 
 
 def only(engines, n):
@@ -99,7 +106,8 @@ def plan(nodes):
     m = len(nodes)
     succ, pred = [[] for _ in range(m)], [[] for _ in range(m)]
     for n, x in enumerate(nodes):
-        for d, lat in [(d, nodes[d]["lat"]) for d in x["deps"]] + [(d, 0.0) for d in x["soft"]]:
+        hard = [(d, 0.0 if x["q"] == nodes[d]["q"] == "pe" else nodes[d]["lat"]) for d in x["deps"]]
+        for d, lat in hard + [(d, 0.0) for d in x["soft"] | x["hint"]]:
             succ[d].append((n, lat))
             pred[n].append((d, lat))
 
@@ -133,23 +141,79 @@ def plan(nodes):
         if best is None or span < best[0]:
             best = (span, end, way)
         way = place(end, succ, pred, [x["lat"] for x in nodes])
-    rng = np.random.RandomState(0)
-    names = sorted(set(x["name"] for x in nodes))
-    for _ in range(NAMED):
-        more = dict((names[k], SHAKE * rng.randn()) for k in rng.randint(len(names), size=rng.randint(1, 5)))
-        way = [w + more.get(x["name"], 0.0) for w, x in zip(best[2], nodes)]
-        end = place(way, pred, succ, [0.0] * m)
-        span = max(end[n] + nodes[n]["lat"] for n in range(m))
-        if span <= best[0]:
-            best = (span, end, way)
-    for _ in range(TRIES):
-        at, wide = rng.rand() * best[0], 1.0 + 4.0 * rng.rand()
-        way = [w + SHAKE * rng.randn() if abs(e - at) < wide else w for w, e in zip(best[2], best[1])]
-        end = place(way, pred, succ, [0.0] * m)
-        span = max(end[n] + nodes[n]["lat"] for n in range(m))
-        if span <= best[0]:
-            best = (span, end, way)
-    return sorted(range(m), key=lambda n: (best[1][n] - nodes[n]["cost"], n))
+    succ = [[e for e in s if n not in nodes[e[0]]["hint"]] for n, s in enumerate(succ)]
+    pred = [[e for e in p if e[0] not in nodes[n]["hint"]] for n, p in enumerate(pred)]
+    lines, made, ends = {}, {}, [n for n in range(m) if not succ[n]]
+    for n in sorted(range(m), key=lambda n: (best[1][n] - nodes[n]["cost"], n)):
+        lines.setdefault(nodes[n]["q"], []).append(n)
+
+    def timing(slow, wait, far):
+        if slow not in made:
+            made[slow] = ([slow * x["cost"] for x in nodes],
+                          [[(j, wait if lat == LAT else far * lat if x["name"] in ("go", "gs") else lat) for j, lat in s]
+                           for x, s in zip(nodes, succ)])
+        cost, edges = made[slow]
+        left, nxt, todo = [len(p) + 1 for p in pred], [m] * m, []
+        for line in lines.values():
+            for a, b in zip(line, line[1:]):
+                nxt[a] = b
+            left[line[0]] -= 1
+            if not left[line[0]]:
+                todo.append(line[0])
+        left.append(m + 1)
+        start, why = [0.0] * (m + 1), [-1] * (m + 1)
+        for n in todo:
+            e = start[n] + cost[n]
+            for j, lat in edges[n]:
+                if e + lat > start[j]:
+                    start[j], why[j] = e + lat, n
+                left[j] -= 1
+                if not left[j]:
+                    todo.append(j)
+            j = nxt[n]
+            if e > start[j]:
+                start[j], why[j] = e, n
+            left[j] -= 1
+            if not left[j]:
+                todo.append(j)
+        if len(todo) < m:
+            return None
+        last = max((start[n] + cost[n] + nodes[n]["lat"], n) for n in ends)
+        chain, n = [], last[1]
+        while why[n] >= 0:
+            if nxt[why[n]] == n:
+                chain.append(n)
+            n = why[n]
+        return (last[0] + EARLY * sum(start) / m) / slow, start, chain
+
+    same = {}
+    for n, x in enumerate(nodes):
+        same.setdefault(x["tag"], {})[x["round"]] = n
+    rng = np.random.RandomState(SEED)
+    now = [timing(*s) for s in SPEEDS]
+    for move in range(MOVES):
+        chain = now[rng.randint(len(now))][2]
+        n = chain[rng.randint(len(chain))] if rng.rand() < 0.5 else rng.randint(m)
+        line = lines[nodes[n]["q"]]
+        k, hop = max(1, line.index(n)), 1 + rng.randint((2, 4, 10)[move % 3])
+        if len(line) < 2:
+            continue
+        a, b = (k, max(0, k - hop)) if rng.rand() < 0.5 else (k - 1, min(len(line) - 1, k - 1 + hop))
+        old, pairs = line[:], [(line[a], line[b])]
+        if move % 2:
+            pairs = [(same[nodes[line[a]]["tag"]][r], y) for r, y in same[nodes[line[b]]["tag"]].items() if r in same[nodes[line[a]]["tag"]]]
+        for x, y in pairs:
+            if x != y:
+                line.remove(x)
+                line.insert(line.index(y) + int(b > a), x)
+        new = [timing(*SPEEDS[0])]
+        if new[0] is not None:
+            new += [timing(*s) for s in SPEEDS[1:]]
+        if new[0] is not None and sum(x[0] for x in new) <= sum(x[0] for x in now) + HEAT * (1.0 - move / MOVES) * rng.rand() ** 6:
+            now = new
+        else:
+            line[:] = old
+    return sorted(range(m), key=lambda n: (now[0][1][n], n))
 
 
 def relay(g, core, T, topo):
@@ -160,14 +224,18 @@ def relay(g, core, T, topo):
             a, b = T.cores[r], T.cores[(r + d) % N]
             if a not in topo.cores_of(core):
                 continue
-            rel = routes(topo, a, b)
-            if core not in rel:
+            rel, other = routes(topo, a, b)
+            if core == other:
+                g.wait_ge(T.sem["in%d" % t], len(topo.engines(a, core)))
+                out, src, sem = T.SL[:, t, :], T.SU[:, t, :], T.sem["list%d" % t]
+            elif core in rel:
+                k, w = rel.index(core), WIDE // len(rel)
+                g.wait_ge(T.sem["in%d" % t], HOP)
+                out, src, sem = T["F%d" % (t + 1)][:, 256 + k * w:256 + (k + 1) * w], T["RB%d" % t][:, 0:w], T.sem["arr%d" % t]
+            else:
                 continue
-            k, w = rel.index(core), 272 // len(rel)
-            g.wait_ge(T.sem["in%d" % t], HOP)
             rid, pid = topo.addr(b, core)
-            g.remote_dma(T["F%d" % (t + 1)][:, 256 + k * w:256 + (k + 1) * w], T["RB%d" % t][:, 0:w], T.sem["arr%d" % t], T.sem.sent,
-                         pid, rid, topo.mask(core, b))
+            g.remote_dma(out, src, sem, T.sem.sent, pid, rid, topo.mask(core, b))
             sent += len(topo.engines(core, b))
     if sent:
         g.wait_ge(T.sem.sent, sent)
@@ -179,7 +247,7 @@ def rank_program(g, core, T, topo):
         return relay(g, core, T, topo)
     ENG = {"v": g.vector, "s": g.scalar, "pe": g.tensor, "gq": g, "sync": g.sync}
     V = g.vector
-    nodes, lastw, readers, banks = [], {}, {}, {}
+    nodes, lastw, readers, banks, marks = [], {}, {}, {}, [0]
 
     def add(q, emit, reads, writes, cost, lat, sem, inc):
         reads, writes = reads.split(), writes.split()
@@ -198,7 +266,8 @@ def rank_program(g, core, T, topo):
                 cur, before = [], cur
             deps |= set(before)
             banks[bank] = (q, cur + [n], before)
-        nodes.append({"q": q, "name": writes[0], "emit": emit, "deps": deps, "soft": soft - deps, "cost": cost, "lat": lat, "sem": sem, "inc": inc})
+        tag = (q, writes[0], len([x for x in nodes[marks[-1]:] if (x["q"], x["name"]) == (q, writes[0])]))
+        nodes.append({"q": q, "name": writes[0], "tag": tag, "round": len(marks), "emit": emit, "deps": deps, "soft": soft - deps, "hint": set(), "cost": cost, "lat": lat, "sem": sem, "inc": inc})
         for k in writes:
             lastw[k] = n
             readers[k] = set()
@@ -295,7 +364,7 @@ def rank_program(g, core, T, topo):
         mms(1024, reads + " tq0 tq1 tq2 tq3", w, [(out(q), T.TQ[:, 128 * q:128 * q + 128], rhs, alone, alone or q == 15) for q in range(16)])
 
     load("sync", T.LS[:, 0:256], T.gs[:], "l_gs", "ls0", 1.9)
-    load("sync", T.SKI[:], T.sk[:], "l_sk", "ski", 4.2)
+    load("sync", T.SKI[:], T.sk[:], "l_sk", "ski", 4.3)
     load("sync", T.XR[:, 592:4096], T.x[:, 0:3504], "l_x0", "xr0", 6.0)
     load("s", T.LS[:, 256:512], T.gf[:], "l_gf", "ls1", 1.9)
     load("s", T.LS[:, 512:768], T.gcl[:], "l_gc", "ls2", 1.9)
@@ -314,8 +383,8 @@ def rank_program(g, core, T, topo):
     sel(128, "one r9", "r9 @g", R8, T.ONE[0:8, 0:128], [[-1, 8], [0, 16]], 0, 1)
     sel(256, "one", "r16 @g", T.R16[:], T.ONE[0:16, 0:256], [[0, 16], [-1, 16]], 0, 1)
     sel(160, "one", "w @g", T.W[:], T.ONE[:, 0:160], [[1, 160]], -16, -1)
-    iota(256, "iot @g", T.IOT[:], [[1, 256]], 0, 0)
-    cp(256, "iot l16i", "l16i", T.L16[0:8, 768:1024], T.IOT[0:8, :])
+    iota(256, "bia @g", T.BIA[:], [[1, 256]], 256, 0)
+    act(256, "bia l16i", "l16i2 l16i", T.L16[0:8, 768:1024], T.BIA[0:8, :], AF.Identity, bias=-256.0)
     iota(256, "kb @g", T.KB[:], [[0, 16], [-1, 16]], 15, 0)
     iota(128, "lg @g", T.LG[:], [[0, 128]], 1 << 19, -720 - (1 << 19))
     iota(128, "lc @g", T.LC[:], [[0, 128]], 1 << 20, -720 - (1 << 20))
@@ -343,14 +412,12 @@ def rank_program(g, core, T, topo):
     act(128, "w", "i1k", T.I1K[:], ID, scale=1024.0)
     act(128, "w", "isg", T.ISG[:], ID, scale=float(-5 << 19))
     act(128, "w", "isv", T.ISV[:], ID, scale=float(1 << 19))
-    act(256, "iot", "bia", T.BIA[:], T.IOT[:], AF.Identity, bias=256.0)
     for u in range(2):
         act(160, "w mu%d" % u, "ws%d" % u, T.WS[:, u, :], T.W[:], AF.Identity, scale=T.MU[:, u:u + 1])
         act(160, "ws%d" % u, "wt%d" % u, T.WS[:, 2 + u, :], T.WS[:, u, :], scale=512.0)
     mms(128, "r9", "PG0", [(T.PG[:, 0:128], R8, R8, True, True)])
     mms(144, "r9 z", "PG1", [(T.PG[:, 128:272], R8, T.Z[:], True, True)])
     mms(256, "r16", "PC0", [(T.PC[:, 0:256], T.R16[:, 0:128], T.R16[:], True, True)])
-    act(128, "PG0", "blkf", T.BLKF[:], T.PG[:, 0:128])
     for j, w in enumerate((16.0, 32.0, -16.0)):
         act(144, "PG1", "sq", T.SQ[:, j, :], T.PG[:, 128:272], scale=w)
     act(256, "PC0", "diag", T.DIAG[:], T.PC[:, 0:256])
@@ -361,17 +428,23 @@ def rank_program(g, core, T, topo):
 
     ts(1, "thi", "thj0", T.THJ[:, 0:1], T.THI[:], -1.0, OP.add)
     ts(1, "thj0", "thj1", T.THJ[:, 1:2], T.THJ[:, 0:1], 1, OP.arith_shift_right)
-    ts(1, "thi", "thf0", T.THF[:, 0:1], T.THI[:], 16.0, OP.mult, 15.0, OP.add)
-    ts(1, "thj1", "thf1", T.THF[:, 1:2], T.THJ[:, 1:2], 16.0, OP.mult, 15.0, OP.add)
-    for j, p in enumerate(("PG", "PC")):
-        c = slice(256 * j, 256 * j + 256)
-        act(256, "diag thf%d" % j, "thd%d" % j, T.THD[:, c], T.DIAG[:], AF.Identity, scale=T.THF[:, j:j + 1])
-        mms(1024, "blkf thd%d" % j, p + "0 " + p + "1", [(T[p][:, 0:256], T.BLKF[:], T.THD[:, c], True, True)])
-        act(256, p + "0", "th%d" % j, T.TH[:, c], T[p][:, 0:256])
+    ts(1, "thj0", "thj2", T.THJ[:, 2:3], T.THJ[:, 0:1], 1, OP.bitwise_and)
+    cp(1, "thj1", "thf0", T.THF[:, 0:1], T.THJ[:, 1:2])
+    ts(1, "thj2", "thf1", T.THF[:, 1:2], T.THJ[:, 2:3], 0.5, OP.mult)
+    for j in range(2):
+        ts(128, "diag thf%d" % j, "thd%d" % j, T.THD[:, 256 * j:256 * j + 256], T.DIAG[:], T.THF[:, j:j + 1], OP.mult)
+    mms(768, "blkb thd0 thd1", "PC1 PC0", [(T.PC[:, 256:512], T.BLKB[:], T.THD[:, 0:256], True, True),
+                                          (T.PC[:, 0:256], T.BLKB[:], T.THD[:, 0:256], True, False),
+                                          (T.PC[:, 0:256], T.BLKB[:], T.THD[:, 256:512], False, True)])
+    for j in range(2):
+        act(256, "PC0 PC1", "th%d" % j, T.TH[:, 256 * j:256 * j + 256], T.PC[:, 256 * j:256 * j + 256], AF.Identity,
+            scale=(32.0 - 16.0 * j) / (1 << 24), bias=31.0 - 16.0 * j)
+    for j in range(4):
+        cast("ski", "sk16%d @g" % j, T.SK16[:, 256 * j:256 * j + 256], T.SKI[:, 256 * j:256 * j + 256], 256)
 
-    cp(768, "ls0 ls1 ls2 l16t", "l16t", T.L16[0:8, 0:768], T.LS[:])
+    cp(768, "ls0 ls1 ls2 l16t", "l16c l16t", T.L16[0:8, 0:768], T.LS[:])
     mms(1024, "z l16t", "PA0", [(T.PA[:, 0:48], T.Z[:, 15 - q:143 - q], T.L16[0:8, q:768:16], q == 0, q == 15) for q in range(16)])
-    early = [n for n, x in enumerate(nodes) if x["q"] == "v"]
+    early = [n for n, x in enumerate(nodes) if x["q"] == "v" and x["name"][:2] != "th"]
     cp(48, "PA0", "lu", T.LU[:], T.PA[:, 0:48])
     nodes[-1]["soft"] |= set(early) - nodes[-1]["deps"]
     cp(48, "PA0", "tl", T.TL[:], T.PA[:, 0:48])
@@ -380,16 +453,13 @@ def rank_program(g, core, T, topo):
     tt(256, "PS0 frq", "ow", T.OW[:], T.PS[:, 0:256], T.FRQ[:], OP.subtract)
     act(256, "ow", "f0o", T.F0[:, 0:256], T.OW[:], AF.Relu)
     act(256, "ow", "f0g", T.F0[:, 256:512], T.OW[:], AF.Relu)
-    act(256, "ow", "f16", T.F16[:], T.OW[:], AF.Relu)
+    act(256, "f0o", "f16", T.F16[:], T.F0[:, 0:256], scale=-16.0)
     act(256, "ow", "base", T.BASE[:], T.OW[:], AF.Relu)
     ts(16, "tl", "l2", lf(2), T.TL[:, 0:16], 512.0, OP.mult)
     tt(32, "tl l2", "sav", SG, T.TL[:, 16:32], lf(2), OP.add)
     cp(16, "tl sav", "sav", SCL, T.TL[:, 32:48])
 
     def skeleton_table():
-        for j in range(4):
-            c = slice(256 * j, 256 * j + 256)
-            cast("ski", "sk16%d @g" % j, T.SK16[:, c], T.SKI[:, c], 256)
         for j in range(4):
             sel(512, "one", "tq%d @g" % j, T.TQ[:, 512 * j:512 * j + 512], T.ONE[:, 0:512], [[-1, 4], [-16, 8], [0, 16]], -4 * j, 1)
         for j, (p, bank) in enumerate((("PH", T.PH[:]), ("PX", T.PX[:]))):
@@ -415,7 +485,14 @@ def rank_program(g, core, T, topo):
         ts(n, xi, pi, T.PQ[:, 2 * j, a:b, :], x, 10, OP.arith_shift_right, 2047, OP.bitwise_and)
         ts(n, xi, qi, T.PQ[:, 2 * j + 1, a:b, :], x, 1023, OP.bitwise_and)
         z = 256 * j
-        tt(2 * n, pi + " " + qi, zi, T.ZI[:, z + 16 * a:z + 16 * b], T.PQ[:, 2 * j, a:b, :], T.PQ[:, 2 * j + 1, a:b, :], OP.mult)
+        if a == 0 or j:
+            tt(2 * n, pi + " " + qi, zi, T.ZI[:, z + 16 * a:z + 16 * b], T.PQ[:, 2 * j, a:b, :], T.PQ[:, 2 * j + 1, a:b, :], OP.mult)
+        else:
+            halves(0, 0, a, 8, act)
+            halves(0, 1, 0, 8, act)
+            mms(n, "w x1600 x1601", "PG2", [(T.PG[:, 256 + 16 * a:384], ID, T.X16[:, 0, a:8, 0, :], True, True),
+                                           (T.PG[:, 384:512], ID, T.X16[:, 0, :, 1, :], True, True)])
+            tt(n, "PG2 " + qi, zi, T.ZI[:, 16 * a:16 * b], T.PG[:, 256 + 16 * a:256 + 16 * b], T.PQ[:, 1, a:b, :], OP.mult)
         if a == 0:
             a, c = BLOCKS[0][1], slice(64 * j, 64 * j + 64)
             ts(64, zi, "ra%d" % j, T.RA[:, c], T.ZI[:, z:z + 64], 4, OP.arith_shift_right, 4095, OP.bitwise_and)
@@ -429,16 +506,20 @@ def rank_program(g, core, T, topo):
             cast(span("ri%d" % j, lo, hi), " ".join("rl%d%d" % (j, k) for k in ks) + " @g",
                  T.RL[:, 256 * j + OFF[ks[0]]:256 * j + OFF[ks[-1] + 1]], T.RI[:, j, lo:hi, c:d], hi - lo, d - c)
 
-    def halves(j, u):
-        cast(span("pi%d" % j, 8 * u, 8 * u + 8) + " " + span("qi%d" % j, 8 * u, 8 * u + 8), "x16%d%d @g" % (j, u),
-             T.X16[:, 2 * j:2 * j + 2, :, u, :], T.PQ[:, 2 * j:2 * j + 2, 8 * u:8 * u + 8, :], 2, 8, 16)
+    def halves(j, u, a, b, by):
+        lo, hi = 8 * u + a, 8 * u + b
+        r, out, src = span("pi%d" % j, lo, hi) + " " + span("qi%d" % j, lo, hi), T.X16[:, 2 * j:2 * j + 2, a:b, u, :], T.PQ[:, 2 * j:2 * j + 2, lo:hi, :]
+        if by is cast:
+            cast(r, "x16%d%d @g" % (j, u), out, src, 2, b - a, 16)
+        else:
+            act(32 * (b - a), r, "x16%d%d" % (j, u) if hi > 4 else "x16a", out, src)
 
     OFF = [0]
     for a, b, c, d in BLOCKS:
         OFF.append(OFF[-1] + (b - a) * (d - c))
 
     def payload(j, p, lhs, stop):
-        run("v", V.transpose, "x16%d0 x16%d1" % (j, j), "xt%d @db" % j, us(256), T.XT[:, 2 * j:2 * j + 2], T.X16[:, 2 * j:2 * j + 2])
+        run("v", V.transpose, "x16a x16%d0 x16%d1" % (j, j), "xt%d @db" % j, us(256), T.XT[:, 2 * j:2 * j + 2], T.X16[:, 2 * j:2 * j + 2])
         calls = [(T[p][:, 0:256], lhs, T.CR[:], True, False)]
         for u in range(2):
             for gl in range(2):
@@ -448,7 +529,7 @@ def rank_program(g, core, T, topo):
                                   False, stop and u + gl + f == 3))
         mms(1280, "xt%d cr lg lc ws0 ws1 wt0 wt1" % j, p + "0", calls)
 
-    sent, marks = 0, []
+    sent = 0
     PV0, PV1, PS0, PS1 = T.PV[:, 0:256], T.PV[:, 256:512], T.PS[:, 0:256], T.PS[:, 256:512]
     for t in range(RO):
         marks.append(len(nodes))
@@ -465,27 +546,20 @@ def rank_program(g, core, T, topo):
                 mms(32 * (b - a), "i1k v16%s fg%s" % (k, k), key,
                     [(bank, T.I1K[:], T.V16[:, j, c], False, False), (bank, T.I1K[:], T.FG[:, j, c], False, True)])
             act(-256, "lu f0o", span("cg"), T.CG[:], F[:, 0:256].indirect(T.LU[:, 16:32]))
-            mms(512, "w f16 fg10 PH0", "PH1", [(T.PH[:, 1], ID, T.F16[:], True, False), (T.PH[:, 1], ID, T.FG[:, 1, :], False, True)])
-            free = dict(scale=-4096.0, bias=float(B - 4096 * 5120))
+            act(256, "fg10", "fr0 fr16", T.FR16[:], T.FG[:, 1, :], AF.Identity, scale=-4096.0, bias=float(B - 4096 * 5120))
         else:
-            act(256, fg, "PX0", T.PX[:, 0:256], F[:, 256:512])
+            tt(-256, "skv0 skv1 sl bia", span("cg"), T.CG[:], T.SKV[:].indirect(T.SL[:, t - 1, :]), T.BIA[:], OP.add)
+            act(192, fg, "PX0", T.PX[:, 64:256], F[:, 320:512])
             act(-256, "ch " + fo + " " + fg, "wc", T.WC[:], F[:, 0:512].indirect(T.CH[:, 16:32]))
-            act(16, fs, "sl", T.SL[:], F[:, 512:528])
         if t == 0:
-            act(256, "PH1", "PV1", PV1, T.PH[:, 1], AF.Identity, **free)
-            act(256, "PH1", "fr16", T.FR16[:], T.PH[:, 1], AF.Identity, **free)
-            mms(1024, "idf base", "PS0", [(PS0, T.IDF[:], T.BASE[:], True, False)])
+            mms(1024, "idf base", "pre0 PS0", [(PS0, T.IDF[:], T.BASE[:], True, False)])
         for a, b in GOALS:
             c = slice(16 * a, 16 * b)
-            if t:
-                tt(-16 * (b - a), "skv0 skv1 sl bia", span("cg", a, b), T.CG[:, c], T.SKV[:].indirect(T.SL[:, a:b]), T.BIA[:, c], OP.add)
-            src, key = (T.PX[:, c], "PX0 ") if t or a else (T.PA[:, 256 + c.start:256 + c.stop], "PA1 ")
-            tt(16 * (b - a), key + span("cg", a, b), span("xi0", a, b), T.XI[:, 0, c], src, T.CG[:, c], OP.max)
+            src, key = (T.PX[:, c], "PX0 ") if a else (F[:, 256:320], fg + " ") if t else (T.PA[:, 256:320], "PA1 ")
+            tt(16 * (b - a) * (1 if key[0] == "P" else 2), key + span("cg", a, b), span("xi0", a, b), T.XI[:, 0, c], src, T.CG[:, c], OP.max)
             recs(0, a, b)
-        halves(0, 0)
-        offsets(0, CASTS[:2])
-        halves(0, 1)
-        offsets(0, CASTS[2:])
+        halves(0, 0, 0, 4, act)
+        offsets(0, CASTS)
         for ks in UPARTS:
             lo, hi = OFF[ks[0]], OFF[ks[-1] + 1]
             act(16 * (lo - hi), XRK + " ".join("rl0%d" % k for k in ks), " ".join("u%d" % k for k in ks) + " @u",
@@ -494,26 +568,34 @@ def rank_program(g, core, T, topo):
             tt(256, "PH0 " + fo, "xc", T.XC[:], T.PH[:, 0], F[:, 0:256], OP.max)
         else:
             tt(256, "PV1 wc", "xc", T.XC[:], PV1, T.WC[:], OP.max)
-        for a, b in CLAUSES:
-            c = slice(16 * a, 16 * b)
-            src = T["PX" if t else "PV"][:, 256 + 16 * a:256 + 16 * b]
-            tt(16 * (b - a), ("PX1 " if t else "PV1 ") + span("xi0", a, b), span("PVt", a, b), T.PV[:, c], src, T.XI[:, 0, c], OP.add)
-            tt(16 * (b - a), "xc " + span("PVt", a, b), span("xi1", a, b), T.XI[:, 1, c], T.PV[:, c], T.XC[:, c], OP.max)
-            recs(1, a, b)
-        halves(1, 0)
-        offsets(1, CASTS[:1])
-        halves(1, 1)
-        offsets(1, CASTS[1:])
         if last:
             mms(1024, "idf base PH1", "PH0", [(T.PH[:, 0], T.IDF[:], T.BASE[:], True, True)])
-        calls = [(T.PH[:, 1], ID, T.FR16[:], True, False)]
-        for u in range(2):
-            calls += [(T.PH[:, 1, 8 * u:8 * u + 8, :], T.I1K[:], T.X16[:, 0, :, u, :], False, False),
-                      (T.PH[:, 1, 8 * u:8 * u + 8, :], ID, T.X16[:, 1, :, u, :], False, u == 1)]
-        mms(768, "w i1k fr16 x1600 x1601", "PH1", calls)
-        tt(256, "PH1 " + fo, "yb", T.YB[:], T.PH[:, 1], F[:, 0:256], OP.max)
+        for a, b in CLAUSES:
+            c = slice(16 * a, 16 * b)
+            calls = [(T.PH[:, 1, a:b, :], ID, T.FR16[:, c], True, False)]
+            if t == 0:
+                calls.append((T.PH[:, 1, a:b, :], ID, T.F16[:, c], False, False))
+            for lo, hi in [(a, min(b, 8))] + ([(8, b)] if b > 8 else []):
+                for f, lhs in enumerate((T.I1K[:], ID)):
+                    calls.append((T.PH[:, 1, lo:hi, :], lhs, T.X16[:, f, lo % 8:lo % 8 + hi - lo, lo // 8, :], False, f == 1 and hi == b))
+            mms(16 * (b - a) * (3 if t else 4), "w i1k fr16 f16 PH0 x16a" + (" x1600 x1601" if b > 4 else ""), "PH1", calls)
+            tt(16 * (b - a), "xc PH1", span("xi1", a, b), T.XI[:, 1, c], T.PH[:, 1, a:b, :], T.XC[:, c], OP.max)
+            recs(1, a, b)
+        halves(1, 0, 0, 8, cast)
+        offsets(1, CASTS[:1])
+        halves(1, 1, 0, 8, cast)
+        offsets(1, CASTS[1:])
         if last:
+            calls = [(T.PX[:, 256:512], ID, T.FR16[:], True, False)]
+            for u in range(2):
+                for f, lhs in ((0, T.I1K[:]), (1, ID), (1, ID)):
+                    calls.append((T.PX[:, 256 + 128 * u:384 + 128 * u], lhs, T.X16[:, f, :, u, :], False, False))
+            calls[-1] = calls[-1][:4] + (True,)
+            mms(1024, "w i1k fr16 x16a x1600 x1601", "PX1", calls)
+            tt(256, "PX1 yo", "yb", T.YB[:], T.PX[:, 256:512], T.YO[:], OP.max)
             tt(256, "yb PH0", "eq", T.EQ[:], T.PH[:, 0], T.YB[:], OP.is_equal)
+        else:
+            tt(256, "PH1 " + fo, "yb", T.YB[:], T.PH[:, 1], F[:, 0:256], OP.max)
         if t == 0:
             skeleton_table()
             saved_derived()
@@ -569,38 +651,48 @@ def rank_program(g, core, T, topo):
             scan(n, "rst ky" + k, "PVk" + k + (" PV1" if u == 0 else ""), T.PV[:, c2], T.RST[:, c], T.KY[:, c], OP.mult, OP.max)
             tt(n, "PVk%s ky%s" % (k, k), "nr" + k, T.NR[:, c], T.PV[:, c2], T.KY[:, c], OP.is_gt)
             scan(n, "PG0 nr" + k, "sc" + k, T.SC[:, c], T.NR[:, c], T.PG[:, c], OP.mult, OP.max)
-        tt(32, "cf0 cf1 l1", "l11", lf(11), T.CF[:], lf(1), OP.mult)
-        tt(32, "sc0 sc1 l11", "i6", li(6), T.SC[:, 15:256:16], lf(11), OP.max)
+        for a, b, ks in [(0, 16, "01")]:
+            l11, i6 = T.LF[:, 176 + a:176 + b], T.LI[:, 96 + a:96 + b]
+            tt(32, "l1 " + " ".join("cf" + k for k in ks), " ".join("l11" + k for k in ks[::-1]), l11, T.CF[:, a:b], T.LF[:, 16 + a:16 + b],
+               OP.mult)
+            tt(32, " ".join("sc%s l11%s" % (k, k) for k in ks), " ".join("i6" + k for k in ks[::-1]), i6, T.SC[:, 16 * a + 15:16 * b:16], l11,
+               OP.max)
+            if not last:
+                ts(16, "i60 i61", "i91", T.LI[:, 144 + a:144 + b], i6, 9, OP.arith_shift_right, 1023, OP.bitwise_and)
         if last:
-            tt(256, "PS0 yb", "fi", T.FI[:], PS0, T.YB[:], OP.min)
+            tt(256, "PS0 yb", "yo", T.YO[:], PS0, T.YB[:], OP.min)
         else:
             tt(256, "PS0 yb", fo, F[:, 0:256], PS0, T.YB[:], OP.min)
-            ts(16, "i6", "i8", li(8), li(6), 511, OP.bitwise_and)
+            ts(16, "i60 i61", "i8", li(8), li(6), 511, OP.bitwise_and)
             act(16, "i8", "fl", T.FL[:], li(8))
-            ts(16, "i6", "i9", li(9), li(6), 9, OP.arith_shift_right, 1023, OP.bitwise_and)
             C = T["COL%d" % t]
-            cp(16, "i9", "cols", C[:, 256:272], li(9))
+            act(16, "i91", "su", T.SU[:, t, :], li(9))
             act(-256, "fl " + fo + " " + fg, "col", C[:, 0:256], F[:, 0:512].indirect(T.FL[:]))
             d = 1 + t % (N - 1)
-            dst = T.cores[(rank + d) % N]
-            rel = routes(topo, core, dst)
+            dst, src = T.cores[(rank + d) % N], T.cores[(rank - d) % N]
+            (rel, other), (rin, before) = routes(topo, core, dst), routes(topo, src, core)
+            to, out, sem = (other, T.SU, "in%d" % t) if rel else (dst, T.SL, "list%d" % t)
+            rid, pid = topo.addr(to, core)
+            add("gq", lambda a=(out[:, t, :], T.SU[:, t, :], T.sem[sem], T.sem.sent, pid, rid, topo.mask(core, to)):
+                hand(g.remote_dma(*a)), "su", "gs @gs", AHEAD, WAY[t] - AHEAD, None, 0)
+            sent += len(topo.engines(core, to))
+            add("net", lambda: None, "gs", "sl", 0.0, 0.0, "list%d" % t, len(topo.engines(before if rin else src, core)))
             tr = []
             if rel:
-                w = 272 // len(rel)
+                w = WIDE // len(rel)
                 for k, c in enumerate(rel):
                     rid, pid = topo.addr(c, core)
                     es = topo.engines(core, c)
                     tr.append(RemoteDMATransfer(dst_ids=[DstId(rid=rid, pnc=pid)], dma_engine_mask=only(es[HOP * k:], HOP),
                                                 remote_sem=T.sem["in%d" % t], src=C[:, k * w:(k + 1) * w], dst=T["RB%d" % t][:, 0:w]))
-                add("gq", lambda tr=tr: hand(g.remote_dma_fused(tr, local_sem=T.sem.sent)), "cols col", "go", 0.5, 3.6, None, 0)
+                add("gq", lambda tr=tr: hand(g.remote_dma_fused(tr, local_sem=T.sem.sent)), "col", "go @gs", 0.5,
+                    WAY[t], None, 0)
                 sent += HOP * len(rel)
             else:
                 rid, pid = topo.addr(dst, core)
-                add("gq", lambda a=(T["F%d" % (t + 1)][:, 256:528], C[:], T.sem["arr%d" % t], T.sem.sent, pid, rid, topo.mask(core, dst)):
-                    hand(g.remote_dma(*a)), "cols col", "go", 0.5, 2.0, None, 0)
+                add("gq", lambda a=(T["F%d" % (t + 1)][:, 256:256 + WIDE], C[:, 0:WIDE], T.sem["arr%d" % t], T.sem.sent, pid, rid,
+                                    topo.mask(core, dst)): hand(g.remote_dma(*a)), "col", "go @gs", 0.5, WAY[t], None, 0)
                 sent += len(topo.engines(core, dst))
-            src = T.cores[(rank - d) % N]
-            rin = routes(topo, src, core)
             n = sum(len(topo.engines(c, core)) for c in rin) if rin else len(topo.engines(src, core))
             add("net", lambda: None, "go", "f%dg f%ds" % (t + 1, t + 1), 0.0, 0.0, "arr%d" % t, n)
             act(256, fo, "f%do" % (t + 1), T["F%d" % (t + 1)][:, 0:256], F[:, 0:256])
@@ -610,7 +702,10 @@ def rank_program(g, core, T, topo):
             c = cut[u]
             tt(c.stop - c.start, p + " th1", "sv%d" % u, T.SV[:, c], D[u], T.TH[:, 256 + c.start:256 + c.stop], OP.is_le)
         mms(256, "sv0 sv1 isv", "PC0 @w", [(T.PC[:, 0:256], T.ISV[:], T.SV[:], False, True)])
-        if not last:
+        if t == RO - 2:
+            act(256, "base", "b16", T.B16[:], T.BASE[:])
+            mms(256, "i1k b16 PS0", "PS1 @w", [(PS1, T.I1K[:], T.B16[:], True, False)])
+        elif not last:
             mms(1024, "idf base PS0", "PS1 @w", [(PS1, T.IDF[:], T.BASE[:], True, False)])
         tt(32, "cf0 cf1 l4", "l13", lf(13), T.CF[:], lf(4), OP.mult)
         for u in range(2):
@@ -621,7 +716,7 @@ def rank_program(g, core, T, topo):
         tt(32, "sd0 sd1 sb0 sb1", "l14", lf(14), T.SD[:, 15::16], T.SB[:], OP.min)
         tt(32, "l13 l14", "i10", li(10), lf(13), lf(14), OP.add)
         ts(16, "i10", "i13", li(13), li(10), 9, OP.arith_shift_right, 1023, OP.bitwise_and)
-        ts(16, "i6", "i12", li(12), li(6), (1 << 19) - 1, OP.bitwise_and)
+        ts(16, "i60 i61", "i12", li(12), li(6), (1 << 19) - 1, OP.bitwise_and)
         tt(64, "i12 i13 sav", "l7", lf(7, 2), li(12, 2), T.SAV[:], OP.subtract)
         tt(64, "l7 ss0 ss1", "l16", lf(16, 2), lf(7, 2), T.SS[:], OP.mult)
         tt(64, "l16 sav", "sav", T.SAV[:], lf(16, 2), T.SAV[:], OP.add)
@@ -637,44 +732,56 @@ def rank_program(g, core, T, topo):
             mms(1024, "s20 s21 tq0 tq1 tq2 tq3", "PH0 PH1 @w", calls)
             mms(512, "w f16 rvc", "PH1 @w", [(T.PH[:, 1], ID, T.F16[:], False, False), (T.PH[:, 1], ID, T.RVC[:], False, True)])
             free = dict(scale=-float(1 << 24), bias=float(B))
-            act(256, "PH1", "PX1", T.PX[:, 256:512], T.PH[:, 1], AF.Identity, **free)
             act(256, "PH1", "fr16", T.FR16[:], T.PH[:, 1], AF.Identity, **free)
             tt(256, "PH0 vc", "PV1 PVk0 PVk1", PV1, T.PH[:, 0], T.VC[:], OP.add)
             spread("sw", "PS1 @w", lambda q: T.PS[:, 256 + q:512:16], T.SW[:], False)
-            tt(256, "PS1 yb", "base", T.BASE[:], PS1, T.YB[:], OP.min)
+            if t == RO - 2:
+                act(256, fo, "fi", T.FI[:], F[:, 0:256])
+                act(256, fo, "PV0", PV0, F[:, 0:256])
+                ts(256, "fi", "fq", T.FQ[:], T.FI[:], 1023, OP.bitwise_and)
+                tt(256, "PV0 fq", "yo", T.YO[:], PV0, T.FQ[:], OP.add)
+                tt(256, "PS1 yo", "base", T.BASE[:], PS1, T.YO[:], OP.min)
+            else:
+                tt(256, "PS1 yb", "base", T.BASE[:], PS1, T.YB[:], OP.min)
             mms(1024, "idf base", "PS0", [(PS0, T.IDF[:], T.BASE[:], True, False)])
             act(16, "PG1", "i3", li(3), T.PG[:, 256:272])
             ts(16, "i3", "i4", li(4), li(3), 1, OP.bitwise_and)
             tt(32, "i4 ramp8", "rs7", T.RS7[:, 0::16], li(4), T.RAMP[:, 16:32], OP.add)
             saved_derived()
     spread("ss1", "PH0", lambda q: T.PH[:, 0, :, q], T.SS[:, 16:32], True)
-    ts(256, "fi", "fq", T.FQ[:], T.FI[:], 1023, OP.bitwise_and)
-    act(256, "fi", "PX0", T.PX[:, 0:256], T.FI[:], AF.Identity, bias=float(-B - 606239))
-    tt(256, "PX0 fq", "yo", T.YO[:], T.PX[:, 0:256], T.FQ[:], OP.add)
-    act(256, "yo", "PX1", T.PX[:, 256:512], T.YO[:], AF.Relu)
+    act(256, "yo", "PX1", T.PX[:, 256:512], T.YO[:], AF.Relu, bias=float(-B - 606239))
     tt(256, "PH0 eq", "nm", T.NM[:], T.PH[:, 0], T.EQ[:], OP.max)
     tt(256, "PX1 nm yo", "yo", T.YO[:], T.PX[:, 256:512], T.NM[:], OP.subtract)
     load("sync", T.yf[:], T.YO[:], "out", "yf", 1.9, "yo")
 
     ts(16, "i10", "i11", li(11), li(10), (1 << 19) - 1, OP.bitwise_and)
     for j, (key, src) in enumerate((("i11 i12", li(11, 2)), ("sav", T.SAV[:]))):
-        ts(32, key + " mu0", "fld%d0" % j, T.FLD[:, 2 * j:2 * j + 2, 0, :], src, T.MU[:, 0:1], OP.mult)
+        if j:
+            ts(32, key + " mu0", "fld%d0" % j, T.FLD[:, 2 * j:2 * j + 2, 0, :], src, T.MU[:, 0:1], OP.mult)
+        else:
+            act(32, key + " mu0", "fld%d0" % j, T.FLD[:, 2 * j:2 * j + 2, 0, :], src, AF.Identity, scale=T.MU[:, 0:1])
         act(32, key + " mu1", "fld%d1" % j, T.FLD[:, 2 * j:2 * j + 2, 1, :], src, AF.Identity, scale=T.MU[:, 1:2])
         run("v", V.transpose, "fld%d0 fld%d1" % (j, j), "flt%d" % j, us(64), T.FLT[:, 2 * j:2 * j + 2], T.FLD[:, 2 * j:2 * j + 2])
         tt(64, "flt%d" % j, "fo%d" % j, T.FO[:, 2 * j:2 * j + 2, :], T.FLT[:, 2 * j:2 * j + 2, 0, :], T.FLT[:, 2 * j:2 * j + 2, 1, :], OP.add)
     for j, y in enumerate((T.yc, T.yg, T.ysg, T.yk)):
         load("sync" if j % 2 else "s", y[:], T.FO[:, j, :], "out", "y%d" % j, 1.9, "fo%d" % (j // 2))
-    def keep(line, lo, hi):
+    def keep(line, lo, hi, kind="hint"):
         at = [[n for n in range(lo, hi) if nodes[n]["name"] == k][:1] for k in line.split()]
         at = [a[0] for a in at if a]
         for a, b in zip(at, at[1:]):
-            nodes[b]["soft"] |= set([a]) - nodes[b]["deps"]
+            if nodes[a]["q"] == nodes[b]["q"]:
+                nodes[b][kind] |= set([a]) - nodes[b]["deps"] - nodes[b]["soft"]
     for line in FIRST:
-        keep(line, 0, len(nodes))
+        keep(line, 0, len(nodes), "soft")
     marks.append(len(nodes))
     for t in range(RO):
+        if t:
+            a = [n for n in range(marks[t], marks[t + 1]) if nodes[n]["name"] == "i1"][-1]
+            [x for x in nodes[marks[t + 1]:] if x["name"] == "cg_0"][0]["hint"].add(a)
+        for line in ("fl col f16", "col f%do" % (t + 1), "col i3"):
+            keep(line, marks[t + 1], marks[t + 2], "soft")
         for line in EACH:
-            keep(line.replace("#", str(t)).replace("+", str(t + 1)), marks[t], marks[t + 1])
+            keep(line.replace("#", str(t)).replace("+", str(t + 1)), marks[t + 1], marks[t + 2])
     cnt, seen = issue()
     g.sync.wait_ge(T.sem.out, cnt["out"])
     g.wait_ge(T.sem.sent, sent)

import numpy as np
from concourse.bass import DstId, RemoteDMATransfer
from concourse.mybir import AluOpType as OP, ActivationFunctionType as AF

N = 8
RO = 4
B = 1 << 21
KE = 592 * 1024 + 16
BLOCKS = [(0, 4, 0, 16)] + [(a, a + 4, c, c + 8) for c in (0, 8) for a in (4, 8)] + [(12, 16, 0, 8), (12, 16, 8, 12), (12, 16, 12, 16)]
UPARTS = [[0], [1, 2], [3, 4], [5, 6, 7]]
CASTS = [[1, 2], [3, 4], [5], [6], [7]]
LATE = 0
PARTS = [[0], [1, 2], [3], [4], [5], [6], [7]]
GOALS = [(0, 4), (4, 16)]
CLAUSES = [(0, 4), (4, 16)]
RELU = 8
SPLIT = 12
LAT, GAP, PATIENCE, PASSES = 0.18, 0.8, 0.3, 6
WIDE = 256
AHEAD = 0.5
WAY = [3.2, 1.6, 2.8]
SEED = 2
EARLY, HEAT, MOVES, SPEEDS = 0.1, 0.3, 24000, [(1.0, 0.15, 1.1), (1.2, 0.24, 0.9)]
FIRST = ["blkb sq diag PS0 i1k l16i2 f0o f16 ws0 ws1 cg_0 wt0 wt1 fr0 u0", "v1600 v1604 v1610", "fg00 fg04 fg10",
         "l16c frq ow thj0", "PH1 PC1", "PG2 pre0", "xr1 blkb", "ab7 sgn0 sgn1"]
EACH = ["slb PX0 wc x16a x1601 x1600 rl00 u0", "su fl cols col f16 ch s20 vc rvc sw fr16 f+o",
        "cg_0 xi0_0 cg_12 pi0_0 qi0_0 xi0_4 pi0_4 zi0_0 qi0_4 ra0 xc xi1_0 xt0 pi1_0 qi1_0 zi0_4 zi1_0 ri0_4 xi1_4 ra1 qi1_4 pi1_4 rl10 zi1_4 yb ri1_4",
        "nov0 sv0 ns0 ky0 cf0 PVk0 nov1 sv1 nr0 ky1 ns1 PVk1 cf1 sc0 nr1 ex1 l111 sc1 sd1 i61 l13 i91 i8 f#o sd0 l14 i15 i10 i14 i13 s21"]
PLANS = {}
CYC, GAT = 0.00083, 1.5
HOP = 8
LOADS = ["l_gs", "l_gf", "l_gc", "l_fr", "l_sk", "l_th", "l_x0", "l_x1"]


def f32(*s):
    return ("sbuf", [128] + list(s), "float32")


def i32(*s):
    return ("sbuf", [128] + list(s), "int32")


def b16(*s):
    return ("sbuf", [128] + list(s), "bfloat16")


def h16(*s):
    return ("sbuf", [128] + list(s), "float16")


def u16(*s):
    return ("sbuf", [128] + list(s), "uint16")


SCRATCH = {
    "XR": b16(4096), "SKI": i32(1024), "SK16": h16(1024), "SGN": h16(1024), "SKV": f32(1024), "FRI": i32(256), "FRQ": i32(256),
    "OW": f32(256), "BASE": f32(256), "YB": f32(256), "F16": b16(256), "FR16": b16(256), "RVC": b16(256), "B16": b16(256),
    "F0": f32(528), "F1": f32(528), "F2": f32(528), "F3": f32(528),
    "COL0": f32(272), "COL1": f32(272), "COL2": f32(272), "RB0": f32(136), "RB2": f32(136),
    "SU": u16(3, 16), "SL": u16(3, 16), "SLB": u16(8),
    "LS": ("sbuf", [8, 768], "int32"), "L16": ("sbuf", [9, 1024], "float16"), "ONE": b16(512),
    "R9": ("sbuf", [9, 128], "bfloat16"), "Z": ("sbuf", [8, 144], "bfloat16"), "R16": ("sbuf", [16, 256], "bfloat16"),
    "KB": ("sbuf", [1, 256], "bfloat16"), "CR": ("sbuf", [2, 256], "float16"), "LG": ("sbuf", [2, 128], "bfloat16"),
    "LC": ("sbuf", [2, 128], "bfloat16"),
    "LU": u16(48), "FL": u16(16), "CH": u16(32), "TL": f32(48),
    "V16": h16(2, 256), "FG": h16(2, 256),
    "THI": i32(1), "THJ": i32(3), "THF": f32(2), "THD": h16(512), "TH": f32(512),
    "W": b16(160), "WS": b16(4, 160), "I1K": b16(128), "ISV": b16(128), "ISG": b16(128),
    "DIAG": b16(256), "OFFD": b16(256), "OFFR": ("sbuf", [16, 256], "bfloat16"), "RAMP": f32(32), "BLKB": b16(128), "LAST": u16(16), "EX": b16(256), "SQ": b16(3, 144), "TQ": b16(2048),
    "RST": b16(256), "RS7": b16(256), "BIA": f32(256),
    "C16": f32(16), "PIO": i32(16), "PM": i32(16), "IDX": f32(16), "MUI": i32(1), "MU": f32(2),
    "CG": f32(256), "VC": f32(256), "WC": f32(256), "XC": f32(256),
    "XI": i32(2, 256), "PQ": i32(4, 16, 16), "ZI": i32(512), "RI": i32(2, 16, 16), "RA": i32(128), "RL": u16(512),
    "DB": b16(4096), "TURN": u16(4), "PA4": i32(2), "PF": f32(2),
    "U": b16(4096), "X16": h16(4, 8, 2, 16), "XT": h16(4, 8, 2, 16),
    "NOV": b16(256), "NS": b16(256), "SV": b16(256), "NR": b16(256), "SB": b16(16), "S2": h16(2, 16), "KY": f32(256),
    "CF": b16(16), "SS": b16(32), "SW": b16(16), "IDF": f32(128), "SD": i32(256), "SC": f32(256), "LF": f32(288), "LI": i32(272), "SAV": i32(32),
    "FI": i32(256), "FQ": i32(256), "EQ": f32(256), "NM": f32(256), "YO": f32(256),
    "FLD": f32(4, 2, 16), "FLT": f32(4, 2, 16), "FO": f32(4, 16),
    "PA": ("psum", [128, 512], "float32"), "PB": ("psum", [128, 512], "float32"), "PG": ("psum", [128, 512], "float32"),
    "PC": ("psum", [128, 512], "float32"), "PV": ("psum", [128, 512], "float32"), "PS": ("psum", [128, 512], "float32"),
    "PH": ("psum", [128, 2, 16, 16], "float32"), "PX": ("psum", [128, 512], "float32"),
}
for _j, (_a, _b, _c, _d) in enumerate(BLOCKS):
    SCRATCH["AB%d" % _j] = b16(_b - _a, _d - _c, 16) if _j else b16(1024)
SEMAPHORES = LOADS + ["v", "s", "pe", "gq", "out", "sent", "in0", "in2", "arr0", "arr1", "arr2", "list0", "list1", "list2"]


def routes(topo, a, b):
    if topo.may_write(a, b):
        return [], None
    own = [c for c in topo.cores_of(a) if c != a and topo.may_write(c, b)]
    rel = [[c for c in own if topo.die(c) == die][0] for die in sorted(set(topo.die(c) for c in own))]
    return rel, [c for c in own if c not in rel and topo.die(c) == topo.die(a)][0]


def only(engines, n):
    return sum(1 << e for e in engines[:n])


def hand(ins):
    return None


def plan(nodes):
    m = len(nodes)
    succ, pred = [[] for _ in range(m)], [[] for _ in range(m)]
    for n, x in enumerate(nodes):
        hard = [(d, 0.0 if x["q"] == nodes[d]["q"] == "pe" else nodes[d]["lat"]) for d in x["deps"]]
        for d, lat in hard + [(d, 0.0) for d in x["soft"] | x["hint"]]:
            succ[d].append((n, lat))
            pred[n].append((d, lat))

    def place(urge, before, after, first):
        left = [len(before[n]) for n in range(m)]
        ready, end, free, can = list(first), [0.0] * m, {}, {}
        for n in range(m):
            if not left[n]:
                can.setdefault(nodes[n]["q"], []).append(n)
        for _ in range(m):
            t, q = min((max(free.get(q, 0.0), min(ready[n] for n in can[q])), q) for q in can if can[q])
            n = max([k for k in can[q] if ready[k] <= t + 1e-9], key=lambda k: (urge[k], -k))
            for k in sorted(can[q], key=lambda k: -urge[k]):
                if urge[k] > urge[n] + GAP and ready[k] < t + PATIENCE * nodes[n]["cost"]:
                    n = k
                    break
            can[q].remove(n)
            end[n] = free[q] = max(t, ready[n]) + nodes[n]["cost"]
            for j, lat in after[n]:
                left[j] -= 1
                ready[j] = max(ready[j], end[n] + lat)
                if not left[j]:
                    can.setdefault(nodes[j]["q"], []).append(j)
        return end

    way = place([0.0] * m, succ, pred, [x["lat"] for x in nodes])
    best = None
    for _ in range(PASSES):
        end = place(way, pred, succ, [0.0] * m)
        span = max(end[n] + nodes[n]["lat"] for n in range(m))
        if best is None or span < best[0]:
            best = (span, end, way)
        way = place(end, succ, pred, [x["lat"] for x in nodes])
    succ = [[e for e in s if n not in nodes[e[0]]["hint"]] for n, s in enumerate(succ)]
    pred = [[e for e in p if e[0] not in nodes[n]["hint"]] for n, p in enumerate(pred)]
    lines, made, ends = {}, {}, [n for n in range(m) if not succ[n]]
    for n in sorted(range(m), key=lambda n: (best[1][n] - nodes[n]["cost"], n)):
        lines.setdefault(nodes[n]["q"], []).append(n)

    def timing(slow, wait, far):
        if slow not in made:
            made[slow] = ([slow * x["cost"] for x in nodes],
                          [[(j, wait if lat == LAT else far * lat if x["name"] in ("go", "gs") else lat) for j, lat in s]
                           for x, s in zip(nodes, succ)])
        cost, edges = made[slow]
        left, nxt, todo = [len(p) + 1 for p in pred], [m] * m, []
        for line in lines.values():
            for a, b in zip(line, line[1:]):
                nxt[a] = b
            left[line[0]] -= 1
            if not left[line[0]]:
                todo.append(line[0])
        left.append(m + 1)
        start, why = [0.0] * (m + 1), [-1] * (m + 1)
        for n in todo:
            e = start[n] + cost[n]
            for j, lat in edges[n]:
                if e + lat > start[j]:
                    start[j], why[j] = e + lat, n
                left[j] -= 1
                if not left[j]:
                    todo.append(j)
            j = nxt[n]
            if e > start[j]:
                start[j], why[j] = e, n
            left[j] -= 1
            if not left[j]:
                todo.append(j)
        if len(todo) < m:
            return None
        last = max((start[n] + cost[n] + nodes[n]["lat"], n) for n in ends)
        chain, n = [], last[1]
        while why[n] >= 0:
            if nxt[why[n]] == n:
                chain.append(n)
            n = why[n]
        return (last[0] + EARLY * sum(start) / m) / slow, start, chain

    same = {}
    for n, x in enumerate(nodes):
        same.setdefault(x["tag"], {})[x["round"]] = n
    rng = np.random.RandomState(SEED)
    now = [timing(*s) for s in SPEEDS]
    for move in range(MOVES):
        chain = now[rng.randint(len(now))][2]
        n = chain[rng.randint(len(chain))] if rng.rand() < 0.5 else rng.randint(m)
        line = lines[nodes[n]["q"]]
        k, hop = max(1, line.index(n)), 1 + rng.randint((2, 4, 10)[move % 3])
        if len(line) < 2:
            continue
        a, b = (k, max(0, k - hop)) if rng.rand() < 0.5 else (k - 1, min(len(line) - 1, k - 1 + hop))
        old, pairs = line[:], [(line[a], line[b])]
        if move % 2:
            pairs = [(same[nodes[line[a]]["tag"]][r], y) for r, y in same[nodes[line[b]]["tag"]].items() if r in same[nodes[line[a]]["tag"]]]
        for x, y in pairs:
            if x != y:
                line.remove(x)
                line.insert(line.index(y) + int(b > a), x)
        new = [timing(*SPEEDS[0])]
        if new[0] is not None:
            new += [timing(*s) for s in SPEEDS[1:]]
        if new[0] is not None and sum(x[0] for x in new) <= sum(x[0] for x in now) + HEAT * (1.0 - move / MOVES) * rng.rand() ** 6:
            now = new
        else:
            line[:] = old
    return sorted(range(m), key=lambda n: (now[0][1][n], n))


def relay(g, core, T, topo):
    sent = 0
    for t in range(RO - 1):
        d = 1 + t % (N - 1)
        for r in range(N):
            a, b = T.cores[r], T.cores[(r + d) % N]
            if a not in topo.cores_of(core):
                continue
            rel, other = routes(topo, a, b)
            if core == other:
                g.wait_ge(T.sem["in%d" % t], len(topo.engines(a, core)))
                out, src, sem = T.SL[:, t, :], T.SU[:, t, :], T.sem["list%d" % t]
            elif core in rel:
                k, w = rel.index(core), WIDE // len(rel)
                g.wait_ge(T.sem["in%d" % t], HOP)
                out, src, sem = T["F%d" % (t + 1)][:, 256 + k * w:256 + (k + 1) * w], T["RB%d" % t][:, 0:w], T.sem["arr%d" % t]
            else:
                continue
            rid, pid = topo.addr(b, core)
            g.remote_dma(out, src, sem, T.sem.sent, pid, rid, topo.mask(core, b))
            sent += len(topo.engines(core, b))
    if sent:
        g.wait_ge(T.sem.sent, sent)


def rank_program(g, core, T, topo):
    rank = T.rank_of(core)
    if rank is None:
        return relay(g, core, T, topo)
    ENG = {"v": g.vector, "s": g.scalar, "pe": g.tensor, "gq": g, "sync": g.sync}
    V = g.vector
    nodes, lastw, readers, banks, marks = [], {}, {}, {}, [0]

    def add(q, emit, reads, writes, cost, lat, sem, inc):
        reads, writes = reads.split(), writes.split()
        lines = [k for k in writes if k[0] == "@"]
        writes = [k for k in writes if k[0] != "@"]
        soft = set(lastw[k] for k in lines if k in lastw)
        for k in lines:
            lastw[k] = len(nodes)
        deps = set(lastw[k] for k in reads + writes if k in lastw)
        for k in writes:
            deps |= readers.get(k, set())
        n = len(nodes)
        for bank in sorted(set(k[:2] for k in reads + writes if k[0] == "P")):
            who, cur, before = banks.get(bank, (q, [], []))
            if who != q:
                cur, before = [], cur
            deps |= set(before)
            banks[bank] = (q, cur + [n], before)
        tag = (q, writes[0], len([x for x in nodes[marks[-1]:] if (x["q"], x["name"]) == (q, writes[0])]))
        nodes.append({"q": q, "name": writes[0], "tag": tag, "round": len(marks), "emit": emit, "deps": deps, "soft": soft - deps, "hint": set(), "cost": cost, "lat": lat, "sem": sem, "inc": inc})
        for k in writes:
            lastw[k] = n
            readers[k] = set()
        for k in reads:
            readers.setdefault(k, set()).add(n)

    def run(q, fn, reads, writes, cost, *a, **kw):
        add(q, lambda: fn(*a, **kw), reads, writes, cost, LAT, q, 1)

    def load(q, out, in_, sem, key, lat, reads=""):
        add(q, lambda: ENG[q].dma_start(out, in_), reads, key + ("" if reads else " @" + q), 0.06, lat, sem, 16)

    def issue():
        cnt, seen, tok = {}, {}, {}
        form = tuple((x["q"], x["cost"], x["lat"]) for x in nodes)
        if form not in PLANS:
            PLANS[form] = plan(nodes)
        for n in PLANS[form]:
            x = nodes[n]
            q = x["q"]
            need = {}
            for d in x["deps"]:
                if d in tok and not (q == "pe" and tok[d][0] == "pe"):
                    need[tok[d][0]] = max(need.get(tok[d][0], 0), tok[d][1])
            for sm in sorted(need):
                if q in ENG and seen.get((q, sm), 0) < need[sm]:
                    ENG[q].wait_ge(T.sem[sm], need[sm])
                    seen[(q, sm)] = need[sm]
            ins = x["emit"]()
            if x["sem"]:
                cnt[x["sem"]] = cnt.get(x["sem"], 0) + x["inc"]
                tok[n] = (x["sem"], cnt[x["sem"]])
                if ins is not None:
                    ins.then_inc(T.sem[x["sem"]], x["inc"])
        return cnt, seen

    def us(n):
        return 0.06 - GAT * n * CYC if n < 0 else max(64, n) * CYC + 0.02

    def tt(n, reads, w, out, a, b, op):
        run("v", V.tensor_tensor, reads, w, us(n), out, a, b, op)

    def ts(n, reads, w, out, a, s1, op0, s2=None, op1=None):
        if op1 is None:
            run("v", V.tensor_scalar, reads, w, us(n), out, a, s1, None, op0)
        else:
            run("v", V.tensor_scalar, reads, w, us(n), out, a, s1, s2, op0, op1)

    def cp(n, reads, w, out, a):
        run("v", V.tensor_copy, reads, w, us(n), out, a)

    def fill(n, w, out, k):
        run("v", V.memset, "", w, us(n), out, k)

    def scan(n, reads, w, out, d0, d1, op0, op1):
        run("v", V.tensor_tensor_scan, reads, w, us(n), out, d0, d1, 0.0, op0, op1)

    def act(n, reads, w, out, a, func=AF.Copy, **kw):
        run("s", g.scalar.activation, reads, w, us(n), out, a, func, **kw)

    def mms(n, reads, w, calls):
        def emit():
            for c in calls:
                ins = g.tensor.matmul(*c)
            return ins
        add("pe", emit, reads, w, n * CYC, LAT, "pe", 1)

    def sel(n, r, w, o, i, p, base, cm):
        run("gq", g.affine_select, r, w, 0.17 + 2 * n * CYC, o, i, p, OP.is_equal, 0.0, base, cm)

    def cast(r, w, o, i, *shape):
        n = 1
        for s in shape:
            n *= s
        sel(n, r, w, o, i, [[0, s] for s in shape], 0, 0)

    def iota(n, w, o, p, base, cm):
        run("gq", g.iota, "", w, 0.13 + 2 * n * CYC, o, p, base, cm, allow_small_or_imprecise_dtypes=True)

    def span(name, a=0, b=16):
        return " ".join("%s_%d" % (name, k) for k in range(a, b, 2))

    def lf(j, n=1):
        return T.LF[:, 16 * j:16 * j + 16 * n]

    def li(j, n=1):
        return T.LI[:, 16 * j:16 * j + 16 * n]

    SG, SCL = T.SAV[:, 0:16], T.SAV[:, 16:32]
    ID = T.W[:, 16:144]
    R8 = T.R9[0:8, :]

    def spread(reads, w, out, rhs, alone):
        mms(1024, reads + " tq0 tq1 tq2 tq3", w, [(out(q), T.TQ[:, 128 * q:128 * q + 128], rhs, alone, alone or q == 15) for q in range(16)])

    load("sync", T.LS[:, 0:256], T.gs[:], "l_gs", "ls0", 1.9)
    load("sync", T.SKI[:], T.sk[:], "l_sk", "ski", 4.3)
    load("sync", T.XR[:, 592:4096], T.x[:, 0:3504], "l_x0", "xr0", 6.0)
    load("s", T.LS[:, 256:512], T.gf[:], "l_gf", "ls1", 1.9)
    load("s", T.LS[:, 512:768], T.gcl[:], "l_gc", "ls2", 1.9)
    load("s", T.FRI[:], T.fr[:], "l_fr", "fri", 2.3)
    load("s", T.THI[:], T.th[:], "l_th", "thi", 2.3)
    load("s", T.XR[:, 0:592], T.x[:, 3504:4096], "l_x1", "xr1", 5.0)
    XRK = "xr0 xr1 "

    fill(256, "one", T.ONE[:], 1.0)
    fill(64, "r9", T.R9[:], 2448.0)
    ts(128, "one", "l16t", T.L16[:, 256:512], T.ONE[0:9, 0:256], 1961.0, OP.mult)
    ts(128, "one", "l16i", T.L16[:, 768:1024], T.ONE[0:9, 0:256], 1961.0, OP.mult)
    iota(16, "pio @g", T.PIO[:], [[0, 16]], 0, 1)
    iota(16, "c16 @g", T.C16[:], [[16, 16]], 0, 0)
    sel(144, "one", "z @g", T.Z[:], T.ONE[0:8, 0:144], [[1, 144]], -15, -16)
    sel(128, "one r9", "r9 @g", R8, T.ONE[0:8, 0:128], [[-1, 8], [0, 16]], 0, 1)
    sel(256, "one", "r16 @g", T.R16[:], T.ONE[0:16, 0:256], [[0, 16], [-1, 16]], 0, 1)
    sel(160, "one", "w @g", T.W[:], T.ONE[:, 0:160], [[1, 160]], -16, -1)
    iota(256, "bia @g", T.BIA[:], [[1, 256]], 256, 0)
    act(256, "bia l16i", "l16i2 l16i", T.L16[0:8, 768:1024], T.BIA[0:8, :], AF.Identity, bias=-256.0)
    iota(256, "kb @g", T.KB[:], [[0, 16], [-1, 16]], 15, 0)
    iota(128, "lg @g", T.LG[:], [[0, 128]], 1 << 19, -720 - (1 << 19))
    iota(128, "lc @g", T.LC[:], [[0, 128]], 1 << 20, -720 - (1 << 20))
    iota(256, "offr @g", T.OFFR[:], [[-2, 16], [0, 16]], -64, 0)
    sel(256, "offr", "offr @g", T.OFFR[:], T.OFFR[:], [[0, 16], [-1, 16]], 0, 1)
    ts(128, "one", "cr", T.CR[:], T.ONE[0:2, 0:256], 421.0, OP.mult)
    cp(128, "kb cr", "cr", T.CR[0:1, :], T.KB[:])
    ts(16, "pio", "pm", T.PM[:], T.PIO[:], 15, OP.bitwise_and)
    ts(1, "pio", "mui", T.MUI[:], T.PIO[:, 0:1], 4, OP.arith_shift_right, 1, OP.bitwise_and)
    ts(1, "mui", "mu0", T.MU[:, 0:1], T.MUI[:], -1.0, OP.mult, 1.0, OP.add)
    cp(1, "mui", "mu1", T.MU[:, 1:2], T.MUI[:])
    tt(32, "pm c16", "idx", T.IDX[:], T.PM[:], T.C16[:], OP.add)
    ts(1, "pio", "pa0", T.PA4[:, 0:1], T.PIO[:, 0:1], 3, OP.bitwise_and)
    ts(1, "pio", "pa1", T.PA4[:, 1:2], T.PIO[:, 0:1], 2, OP.arith_shift_right, 3, OP.bitwise_and)
    cp(1, "pa1", "pf1", T.PF[:, 1:2], T.PA4[:, 1:2])
    ts(1, "pa0 pf1", "pf0", T.PF[:, 0:1], T.PA4[:, 0:1], 16.0, OP.mult, T.PF[:, 1:2], OP.add)
    ts(4, "c16 pf0", "turn", T.TURN[:], T.C16[:, 0:4], 0.25, OP.mult, T.PF[:, 0:1], OP.add)
    fill(128, "rst", T.RST[:], 1.0)
    fill(16, "rst", T.RST[:, 0::16], 0.0)
    fill(128, "rs7", T.RS7[:], 64.0)
    ts(16, "c16", "ramp", T.RAMP[:, 0:16], T.C16[:], -0.125, OP.mult)
    ts(16, "c16", "ramp8", T.RAMP[:, 16:32], T.C16[:], -0.125, OP.mult, -8.0, OP.add)
    cp(16, "ramp8 rs7", "rs7", T.RS7[:, 0::16], T.RAMP[:, 16:32])
    act(128, "w", "idf", T.IDF[:], ID)
    act(128, "w", "i1k", T.I1K[:], ID, scale=1024.0)
    act(128, "w", "isg", T.ISG[:], ID, scale=float(-5 << 19))
    act(128, "w", "isv", T.ISV[:], ID, scale=float(1 << 19))
    for u in range(2):
        act(160, "w mu%d" % u, "ws%d" % u, T.WS[:, u, :], T.W[:], AF.Identity, scale=T.MU[:, u:u + 1])
        act(160, "ws%d" % u, "wt%d" % u, T.WS[:, 2 + u, :], T.WS[:, u, :], scale=512.0)
    mms(128, "r9", "PG0", [(T.PG[:, 0:128], R8, R8, True, True)])
    mms(144, "r9 z", "PG1", [(T.PG[:, 128:272], R8, T.Z[:], True, True)])
    mms(256, "r16", "PC0", [(T.PC[:, 0:256], T.R16[:, 0:128], T.R16[:], True, True)])
    for j, w in enumerate((16.0, 32.0, -16.0)):
        act(144, "PG1", "sq", T.SQ[:, j, :], T.PG[:, 128:272], scale=w)
    act(256, "PC0", "diag", T.DIAG[:], T.PC[:, 0:256])
    mms(256, "r16 offr", "PB1", [(T.PB[:, 256:512], T.R16[:, 0:128], T.OFFR[:], True, True)])
    act(256, "PB1", "offd", T.OFFD[:], T.PB[:, 256:512], AF.Identity, bias=64.0)
    act(128, "PG0", "blkb", T.BLKB[:], T.PG[:, 0:128], scale=float(1 << 24))
    ts(16, "c16", "last", T.LAST[:], T.C16[:], 15.0, OP.add)

    ts(1, "thi", "thj0", T.THJ[:, 0:1], T.THI[:], -1.0, OP.add)
    ts(1, "thj0", "thj1", T.THJ[:, 1:2], T.THJ[:, 0:1], 1, OP.arith_shift_right)
    ts(1, "thj0", "thj2", T.THJ[:, 2:3], T.THJ[:, 0:1], 1, OP.bitwise_and)
    cp(1, "thj1", "thf0", T.THF[:, 0:1], T.THJ[:, 1:2])
    ts(1, "thj2", "thf1", T.THF[:, 1:2], T.THJ[:, 2:3], 0.5, OP.mult)
    for j in range(2):
        ts(128, "diag thf%d" % j, "thd%d" % j, T.THD[:, 256 * j:256 * j + 256], T.DIAG[:], T.THF[:, j:j + 1], OP.mult)
    mms(768, "blkb thd0 thd1", "PC1 PC0", [(T.PC[:, 256:512], T.BLKB[:], T.THD[:, 0:256], True, True),
                                          (T.PC[:, 0:256], T.BLKB[:], T.THD[:, 0:256], True, False),
                                          (T.PC[:, 0:256], T.BLKB[:], T.THD[:, 256:512], False, True)])
    for j in range(2):
        act(256, "PC0 PC1", "th%d" % j, T.TH[:, 256 * j:256 * j + 256], T.PC[:, 256 * j:256 * j + 256], AF.Identity,
            scale=(32.0 - 16.0 * j) / (1 << 24), bias=31.0 - 16.0 * j)
    for j in range(4):
        cast("ski", "sk16%d @g" % j, T.SK16[:, 256 * j:256 * j + 256], T.SKI[:, 256 * j:256 * j + 256], 256)

    cp(768, "ls0 ls1 ls2 l16t", "l16c l16t", T.L16[0:8, 0:768], T.LS[:])
    mms(1024, "z l16t", "PA0", [(T.PA[:, 0:48], T.Z[:, 15 - q:143 - q], T.L16[0:8, q:768:16], q == 0, q == 15) for q in range(16)])
    early = [n for n, x in enumerate(nodes) if x["q"] == "v" and x["name"][:2] != "th"]
    cp(48, "PA0", "lu", T.LU[:], T.PA[:, 0:48])
    nodes[-1]["soft"] |= set(early) - nodes[-1]["deps"]
    cp(48, "PA0", "tl", T.TL[:], T.PA[:, 0:48])
    ts(256, "fri", "frq", T.FRQ[:], T.FRI[:], 511 + (1 << 23), OP.bitwise_and)
    act(256, "fri", "PS0", T.PS[:, 0:256], T.FRI[:], AF.Identity, scale=2.0, bias=float(KE + B))
    tt(256, "PS0 frq", "ow", T.OW[:], T.PS[:, 0:256], T.FRQ[:], OP.subtract)
    act(256, "ow", "f0o", T.F0[:, 0:256], T.OW[:], AF.Relu)
    act(256, "ow", "f0g", T.F0[:, 256:512], T.OW[:], AF.Relu)
    act(256, "f0o", "f16", T.F16[:], T.F0[:, 0:256], scale=-16.0)
    act(256, "ow", "base", T.BASE[:], T.OW[:], AF.Relu)
    ts(16, "tl", "l2", lf(2), T.TL[:, 0:16], 512.0, OP.mult)
    tt(32, "tl l2", "sav", SG, T.TL[:, 16:32], lf(2), OP.add)
    cp(16, "tl sav", "sav", SCL, T.TL[:, 32:48])

    def skeleton_table():
        for j in range(4):
            sel(512, "one", "tq%d @g" % j, T.TQ[:, 512 * j:512 * j + 512], T.ONE[:, 0:512], [[-1, 4], [-16, 8], [0, 16]], -4 * j, 1)
        for j, (p, bank) in enumerate((("PH", T.PH[:]), ("PX", T.PX[:]))):
            c = slice(512 * j, 512 * j + 512)
            act(512, "ski", "sgn%d" % j, T.SGN[:, c], T.SKI[:, c], AF.Sign, bias=-1023.5)
            mms(1024, "sk16%d sk16%d sgn%d i1k isg" % (2 * j, 2 * j + 1, j), p + "0 " + p + "1",
                [(bank, T.I1K[:], T.SK16[:, c], True, False), (bank, T.ISG[:], T.SGN[:, c], False, True)])
            act(512, p + "0 " + p + "1", "skv%d" % j, T.SKV[:, c], bank, AF.Identity, bias=float(KE + 2 * B - (5 << 19)))

    def saved_derived():
        act(16, "sav", "l1", lf(1), SG, AF.Identity, bias=float(1 << 23))
        ts(16, "sav", "i1", li(1), SG, 9, OP.arith_shift_right)
        act(16, "i1", "l5", lf(5), li(1), AF.Identity, bias=32.0)
        tt(32, "l5 sav", "l6", lf(6), lf(5), SCL, OP.mult)
        act(16, "l6", "i2", li(2), lf(6), AF.Identity, scale=16.0, bias=512.0)
        ts(16, "i2", "i5", li(5), li(2), 1023 << 9, OP.bitwise_and)
        tt(32, "i5 idx", "l4", lf(4), li(5), T.IDX[:], OP.add)

    def recs(j, a, b):
        n = 16 * (b - a)
        xi, pi, qi, zi, ri = [span(k + str(j), a, b) for k in ("xi", "pi", "qi", "zi", "ri")]
        x = T.XI[:, j, 16 * a:16 * b]
        ts(n, xi, pi, T.PQ[:, 2 * j, a:b, :], x, 10, OP.arith_shift_right, 2047, OP.bitwise_and)
        ts(n, xi, qi, T.PQ[:, 2 * j + 1, a:b, :], x, 1023, OP.bitwise_and)
        z = 256 * j
        if a == 0 or j:
            tt(2 * n, pi + " " + qi, zi, T.ZI[:, z + 16 * a:z + 16 * b], T.PQ[:, 2 * j, a:b, :], T.PQ[:, 2 * j + 1, a:b, :], OP.mult)
        else:
            halves(0, 0, a, 8, act)
            halves(0, 1, 0, 8, act)
            mms(n, "w x1600 x1601", "PG2", [(T.PG[:, 256 + 16 * a:384], ID, T.X16[:, 0, a:8, 0, :], True, True),
                                           (T.PG[:, 384:512], ID, T.X16[:, 0, :, 1, :], True, True)])
            tt(n, "PG2 " + qi, zi, T.ZI[:, 16 * a:16 * b], T.PG[:, 256 + 16 * a:256 + 16 * b], T.PQ[:, 1, a:b, :], OP.mult)
        if a == 0:
            a, c = BLOCKS[0][1], slice(64 * j, 64 * j + 64)
            ts(64, zi, "ra%d" % j, T.RA[:, c], T.ZI[:, z:z + 64], 4, OP.arith_shift_right, 4095, OP.bitwise_and)
            (cp if j else act)(-64, "turn ra%d" % j, "rl%d0" % j, T.RL[:, z:z + 64], T.RA[:, c].indirect(T.TURN[:]))
        if a < b:
            ts(16 * (b - a), zi, ri, T.RI[:, j, a:b, :], T.ZI[:, z + 16 * a:z + 16 * b], 4, OP.arith_shift_right, 4095, OP.bitwise_and)

    def offsets(j, casts):
        for ks in casts:
            lo, hi, c, d = BLOCKS[ks[0]][0], BLOCKS[ks[-1]][1], BLOCKS[ks[0]][2], BLOCKS[ks[0]][3]
            cast(span("ri%d" % j, lo, hi), " ".join("rl%d%d" % (j, k) for k in ks) + " @g",
                 T.RL[:, 256 * j + OFF[ks[0]]:256 * j + OFF[ks[-1] + 1]], T.RI[:, j, lo:hi, c:d], hi - lo, d - c)

    def halves(j, u, a, b, by):
        lo, hi = 8 * u + a, 8 * u + b
        r, out, src = span("pi%d" % j, lo, hi) + " " + span("qi%d" % j, lo, hi), T.X16[:, 2 * j:2 * j + 2, a:b, u, :], T.PQ[:, 2 * j:2 * j + 2, lo:hi, :]
        if by is cast:
            cast(r, "x16%d%d @g" % (j, u), out, src, 2, b - a, 16)
        else:
            act(32 * (b - a), r, "x16%d%d" % (j, u) if hi > 4 else "x16a", out, src)

    OFF = [0]
    for a, b, c, d in BLOCKS:
        OFF.append(OFF[-1] + (b - a) * (d - c))

    def payload(j, p, lhs, stop):
        run("v", V.transpose, "x16a x16%d0 x16%d1" % (j, j), "xt%d @db" % j, us(256), T.XT[:, 2 * j:2 * j + 2], T.X16[:, 2 * j:2 * j + 2])
        calls = [(T[p][:, 0:256], lhs, T.CR[:], True, False)]
        for u in range(2):
            for gl in range(2):
                o = 16 - 16 * (gl - u)
                for f in range(2):
                    calls.append((T[p][:, 128 * u:128 * u + 128], T.WS[:, 2 - 2 * f + u, o:o + 128], T.XT[:, 2 * j + f, :, gl, :],
                                  False, stop and u + gl + f == 3))
        mms(1280, "xt%d cr lg lc ws0 ws1 wt0 wt1" % j, p + "0", calls)

    sent = 0
    PV0, PV1, PS0, PS1 = T.PV[:, 0:256], T.PV[:, 256:512], T.PS[:, 0:256], T.PS[:, 256:512]
    for t in range(RO):
        marks.append(len(nodes))
        F = T["F%d" % t]
        fo, fg, fs = "f%do" % t, "f%dg" % t, "f%ds" % t
        last = t == RO - 1
        if t == 0:
            for j, a, b in [(0, a, b) for a, b in GOALS] + [(1, 0, 16)]:
                c, k = slice(16 * a, 16 * b), "%d%d" % (j, a)
                bank, key = [(T.PA[:, 256 + c.start:256 + c.stop], "PA1"), (T.PX[:, c], "PX0"), (T.PH[:, 0], "PH0")][2 if j else int(a > 0)]
                cp(c.start - c.stop, "ski lu", "v16" + k, T.V16[:, j, c], T.SKI[:].indirect(T.LU[:, 32 * j + a:32 * j + b]))
                ts(8 * (b - a), "v16" + k, "fg" + k, T.FG[:, j, c], T.V16[:, j, c], 1024.0, OP.is_ge, -5120.0, OP.mult)
                mms(16 * (b - a), "r9 l16t l16i", key, [(bank, T.R9[:], T.L16[:, 256 + 512 * j + c.start:256 + 512 * j + c.stop], True, False)])
                mms(32 * (b - a), "i1k v16%s fg%s" % (k, k), key,
                    [(bank, T.I1K[:], T.V16[:, j, c], False, False), (bank, T.I1K[:], T.FG[:, j, c], False, True)])
            act(-256, "lu f0o", span("cg"), T.CG[:], F[:, 0:256].indirect(T.LU[:, 16:32]))
            act(256, "fg10", "fr0 fr16", T.FR16[:], T.FG[:, 1, :], AF.Identity, scale=-4096.0, bias=float(B - 4096 * 5120))
        else:
            tt(-256, "skv0 skv1 sl bia", span("cg"), T.CG[:], T.SKV[:].indirect(T.SL[:, t - 1, :]), T.BIA[:], OP.add)
            act(192, fg, "PX0", T.PX[:, 64:256], F[:, 320:512])
            act(-256, "ch " + fo + " " + fg, "wc", T.WC[:], F[:, 0:512].indirect(T.CH[:, 16:32]))
        if t == 0:
            mms(1024, "idf base", "pre0 PS0", [(PS0, T.IDF[:], T.BASE[:], True, False)])
        for a, b in GOALS:
            c = slice(16 * a, 16 * b)
            src, key = (T.PX[:, c], "PX0 ") if a else (F[:, 256:320], fg + " ") if t else (T.PA[:, 256:320], "PA1 ")
            tt(16 * (b - a) * (1 if key[0] == "P" else 2), key + span("cg", a, b), span("xi0", a, b), T.XI[:, 0, c], src, T.CG[:, c], OP.max)
            recs(0, a, b)
        halves(0, 0, 0, 4, act)
        offsets(0, CASTS)
        for ks in UPARTS:
            lo, hi = OFF[ks[0]], OFF[ks[-1] + 1]
            act(16 * (lo - hi), XRK + " ".join("rl0%d" % k for k in ks), " ".join("u%d" % k for k in ks) + " @u",
                T.U[:, 16 * lo:16 * hi], T.XR[:].indirect(T.RL[:, lo:hi]))
        if t == 0:
            tt(256, "PH0 " + fo, "xc", T.XC[:], T.PH[:, 0], F[:, 0:256], OP.max)
        else:
            tt(256, "PV1 wc", "xc", T.XC[:], PV1, T.WC[:], OP.max)
        if last:
            mms(1024, "idf base PH1", "PH0", [(T.PH[:, 0], T.IDF[:], T.BASE[:], True, True)])
        for a, b in CLAUSES:
            c = slice(16 * a, 16 * b)
            calls = [(T.PH[:, 1, a:b, :], ID, T.FR16[:, c], True, False)]
            if t == 0:
                calls.append((T.PH[:, 1, a:b, :], ID, T.F16[:, c], False, False))
            for lo, hi in [(a, min(b, 8))] + ([(8, b)] if b > 8 else []):
                for f, lhs in enumerate((T.I1K[:], ID)):
                    calls.append((T.PH[:, 1, lo:hi, :], lhs, T.X16[:, f, lo % 8:lo % 8 + hi - lo, lo // 8, :], False, f == 1 and hi == b))
            mms(16 * (b - a) * (3 if t else 4), "w i1k fr16 f16 PH0 x16a" + (" x1600 x1601" if b > 4 else ""), "PH1", calls)
            tt(16 * (b - a), "xc PH1", span("xi1", a, b), T.XI[:, 1, c], T.PH[:, 1, a:b, :], T.XC[:, c], OP.max)
            recs(1, a, b)
        halves(1, 0, 0, 8, cast)
        offsets(1, CASTS[:1])
        halves(1, 1, 0, 8, cast)
        offsets(1, CASTS[1:])
        if last:
            calls = [(T.PX[:, 256:512], ID, T.FR16[:], True, False)]
            for u in range(2):
                for f, lhs in ((0, T.I1K[:]), (1, ID), (1, ID)):
                    calls.append((T.PX[:, 256 + 128 * u:384 + 128 * u], lhs, T.X16[:, f, :, u, :], False, False))
            calls[-1] = calls[-1][:4] + (True,)
            mms(1024, "w i1k fr16 x16a x1600 x1601", "PX1", calls)
            tt(256, "PX1 yo", "yb", T.YB[:], T.PX[:, 256:512], T.YO[:], OP.max)
            tt(256, "yb PH0", "eq", T.EQ[:], T.PH[:, 0], T.YB[:], OP.is_equal)
        else:
            tt(256, "PH1 " + fo, "yb", T.YB[:], T.PH[:, 1], F[:, 0:256], OP.max)
        if t == 0:
            skeleton_table()
            saved_derived()
        payload(0, "PG", T.LG[:], True)
        cut = [slice(0, 16 * SPLIT), slice(16 * SPLIT, 256)]
        D = [T.PA[:, cut[0]], T.PB[:, cut[1]]]
        for u, p in enumerate(("PA0", "PB0")):
            mms(cut[u].stop - cut[u].start, "one cr", p, [(D[u], T.ONE[0:1, 0:128], T.CR[0:1, cut[u]], True, False)])
        for j, ks in enumerate(PARTS):
            lo, hi = OFF[ks[0]], OFF[ks[-1] + 1]
            e = slice(16 * lo, 16 * hi)
            tt(e.start - e.stop, XRK + " ".join("rl1%d u%d" % (k, k) for k in ks), "db%d @db" % j, T.DB[:, e],
               T.XR[:].indirect(T.RL[:, 256 + lo:256 + hi]), T.U[:, e], OP.subtract)
            if j == LATE:
                payload(1, "PC", T.LC[:], False)
            for k in ks:
                a, b, c, d = BLOCKS[k]
                AB, u = T["AB%d" % k], int(a >= SPLIT)
                out, key = T[("PA", "PB")[u]][:, 16 * a:16 * b], ("PA0 @d", "PB0 @d")[u]
                if k == 0:
                    n = 64 * RELU
                    if n:
                        ts(n // 2, "db0", "ab0 @db", AB[:, 0:n], T.DB[:, 0:n], 0.0, OP.max)
                        for w, src, r in ((2, T.DB, "db0"), (1, AB, "ab0")):
                            mms(n, r + " sq", key, [(out, T.SQ[:, w, 15 - q:143 - q], src[:, 64 * q:64 * q + 64], False, False)
                                                    for q in range(RELU)])
                    if n < 1024:
                        act(1024 - n, "db0", "ac0 @u", AB[:, n:1024], T.DB[:, n:1024], AF.Abs)
                        mms(1024 - n, "ac0 sq", key, [(out, T.SQ[:, 0, 15 - q:143 - q], AB[:, 64 * q:64 * q + 64], False, False)
                                                      for q in range(RELU, 16)])
                    continue
                stop = k + 1 == len(BLOCKS) or int(BLOCKS[k + 1][0] >= SPLIT) != u
                n = 16 * (b - a) * (d - c)
                act(n, "db%d" % j, "ab%d @u" % k, AB[:], T.DB[:, 16 * OFF[k]:16 * OFF[k + 1]], AF.Abs)
                mms(n, "ab%d sq" % k, key, [(out, T.SQ[:, 0, 15 - q:143 - q], AB[:, :, q - c, :], False, stop and q == d - 1)
                                            for q in range(c, d)])
        for u, p in enumerate(("PA0", "PB0")):
            c, k, n = cut[u], "%d" % u, cut[u].stop - cut[u].start
            c2 = slice(256 + c.start, 256 + c.stop)
            tt(n, p + " th0", "nov" + k, T.NOV[:, c], D[u], T.TH[:, c], OP.is_le)
            scan(n // 2, "rs7 nov" + k, "ns" + k, T.NS[:, c], T.RS7[:, c], T.NOV[:, c], OP.min, OP.add)
            h = slice(c.start // 16, c.stop // 16)
            tt(32, "ramp ns" + k, "cf" + k, T.CF[:, h], T.NS[:, c.start + 15:c.stop:16], T.RAMP[:, h], OP.is_le)
            act(16, "cf" + k, "sb" + k, T.SB[:, h], T.CF[:, h], AF.Identity, scale=-float(1 << 24), bias=float(1 << 24))
            if u == 0 and t:
                mms(1024, "sb0 tq0 tq1 tq2 tq3", "PS0", [(T.PS[:, q:c.stop:16], T.TQ[:, 128 * q:128 * q + 128], T.SB[:, h], False, False)
                                                        for q in range(16)])
            else:
                tt(-n, "ns%s last offd" % ("0" if u == 0 else "0 ns1"), "ex" + k, T.EX[:, c],
                   T.NS[:, 0:c.stop].indirect(T.LAST[:, h]), T.OFFD[:, c], OP.is_gt)
                mms(n, "blkb ex" + k, "PS0", [(T.PS[:, c], T.BLKB[:], T.EX[:, c], False, u == 1)])
            tt(n, p + " nov" + k, "ky" + k, T.KY[:, c], D[u], T.NOV[:, c], OP.mult)
            scan(n, "rst ky" + k, "PVk" + k + (" PV1" if u == 0 else ""), T.PV[:, c2], T.RST[:, c], T.KY[:, c], OP.mult, OP.max)
            tt(n, "PVk%s ky%s" % (k, k), "nr" + k, T.NR[:, c], T.PV[:, c2], T.KY[:, c], OP.is_gt)
            scan(n, "PG0 nr" + k, "sc" + k, T.SC[:, c], T.NR[:, c], T.PG[:, c], OP.mult, OP.max)
        for a, b, ks in [(0, 16, "01")]:
            l11, i6 = T.LF[:, 176 + a:176 + b], T.LI[:, 96 + a:96 + b]
            tt(32, "l1 " + " ".join("cf" + k for k in ks), " ".join("l11" + k for k in ks[::-1]), l11, T.CF[:, a:b], T.LF[:, 16 + a:16 + b],
               OP.mult)
            tt(32, " ".join("sc%s l11%s" % (k, k) for k in ks), " ".join("i6" + k for k in ks[::-1]), i6, T.SC[:, 16 * a + 15:16 * b:16], l11,
               OP.max)
            if not last:
                ts(16, "i60 i61", "i91", T.LI[:, 144 + a:144 + b], i6, 9, OP.arith_shift_right, 1023, OP.bitwise_and)
        if last:
            tt(256, "PS0 yb", "yo", T.YO[:], PS0, T.YB[:], OP.min)
        else:
            tt(256, "PS0 yb", fo, F[:, 0:256], PS0, T.YB[:], OP.min)
            ts(16, "i60 i61", "i8", li(8), li(6), 511, OP.bitwise_and)
            act(16, "i8", "fl", T.FL[:], li(8))
            C = T["COL%d" % t]
            act(16, "i91", "su", T.SU[:, t, :], li(9))
            act(-256, "fl " + fo + " " + fg, "col", C[:, 0:256], F[:, 0:512].indirect(T.FL[:]))
            d = 1 + t % (N - 1)
            dst, src = T.cores[(rank + d) % N], T.cores[(rank - d) % N]
            (rel, other), (rin, before) = routes(topo, core, dst), routes(topo, src, core)
            to, out, sem = (other, T.SU, "in%d" % t) if rel else (dst, T.SL, "list%d" % t)
            rid, pid = topo.addr(to, core)
            add("gq", lambda a=(out[:, t, :], T.SU[:, t, :], T.sem[sem], T.sem.sent, pid, rid, topo.mask(core, to)):
                hand(g.remote_dma(*a)), "su", "gs @gs", AHEAD, WAY[t] - AHEAD, None, 0)
            sent += len(topo.engines(core, to))
            add("net", lambda: None, "gs", "sl", 0.0, 0.0, "list%d" % t, len(topo.engines(before if rin else src, core)))
            tr = []
            if rel:
                w = WIDE // len(rel)
                for k, c in enumerate(rel):
                    rid, pid = topo.addr(c, core)
                    es = topo.engines(core, c)
                    tr.append(RemoteDMATransfer(dst_ids=[DstId(rid=rid, pnc=pid)], dma_engine_mask=only(es[HOP * k:], HOP),
                                                remote_sem=T.sem["in%d" % t], src=C[:, k * w:(k + 1) * w], dst=T["RB%d" % t][:, 0:w]))
                add("gq", lambda tr=tr: hand(g.remote_dma_fused(tr, local_sem=T.sem.sent)), "col", "go @gs", 0.5,
                    WAY[t], None, 0)
                sent += HOP * len(rel)
            else:
                rid, pid = topo.addr(dst, core)
                add("gq", lambda a=(T["F%d" % (t + 1)][:, 256:256 + WIDE], C[:, 0:WIDE], T.sem["arr%d" % t], T.sem.sent, pid, rid,
                                    topo.mask(core, dst)): hand(g.remote_dma(*a)), "col", "go @gs", 0.5, WAY[t], None, 0)
                sent += len(topo.engines(core, dst))
            n = sum(len(topo.engines(c, core)) for c in rin) if rin else len(topo.engines(src, core))
            add("net", lambda: None, "go", "f%dg f%ds" % (t + 1, t + 1), 0.0, 0.0, "arr%d" % t, n)
            act(256, fo, "f%do" % (t + 1), T["F%d" % (t + 1)][:, 0:256], F[:, 0:256])
            act(256, fo, "f16", T.F16[:], F[:, 0:256])
            mms(64, "cf0 cf1 diag", "PG1", [(T.PG[:, 256:272], T.DIAG[:, 0:128], T.CF[:], True, True)])
        for u, p in enumerate(("PA0", "PB0")):
            c = cut[u]
            tt(c.stop - c.start, p + " th1", "sv%d" % u, T.SV[:, c], D[u], T.TH[:, 256 + c.start:256 + c.stop], OP.is_le)
        mms(256, "sv0 sv1 isv", "PC0 @w", [(T.PC[:, 0:256], T.ISV[:], T.SV[:], False, True)])
        if t == RO - 2:
            act(256, "base", "b16", T.B16[:], T.BASE[:])
            mms(256, "i1k b16 PS0", "PS1 @w", [(PS1, T.I1K[:], T.B16[:], True, False)])
        elif not last:
            mms(1024, "idf base PS0", "PS1 @w", [(PS1, T.IDF[:], T.BASE[:], True, False)])
        tt(32, "cf0 cf1 l4", "l13", lf(13), T.CF[:], lf(4), OP.mult)
        for u in range(2):
            scan(cut[u].stop - cut[u].start, "PC0 nr%d" % u, "sd%d" % u, T.SD[:, cut[u]], T.NR[:, cut[u]], T.PC[:, cut[u]], OP.mult, OP.max)
        ts(16, "sd0 sd1", "i15", li(15), T.SD[:, 15::16], 19, OP.arith_shift_right, 1, OP.bitwise_and)
        tt(32, "i15 cf0 cf1", "ss1", T.SS[:, 16:32], li(15), T.CF[:], OP.max)
        tt(32, "ss1 cf0 cf1", "ss0", T.SS[:, 0:16], T.SS[:, 16:32], T.CF[:], OP.subtract)
        tt(32, "sd0 sd1 sb0 sb1", "l14", lf(14), T.SD[:, 15::16], T.SB[:], OP.min)
        tt(32, "l13 l14", "i10", li(10), lf(13), lf(14), OP.add)
        ts(16, "i10", "i13", li(13), li(10), 9, OP.arith_shift_right, 1023, OP.bitwise_and)
        ts(16, "i60 i61", "i12", li(12), li(6), (1 << 19) - 1, OP.bitwise_and)
        tt(64, "i12 i13 sav", "l7", lf(7, 2), li(12, 2), T.SAV[:], OP.subtract)
        tt(64, "l7 ss0 ss1", "l16", lf(16, 2), lf(7, 2), T.SS[:], OP.mult)
        tt(64, "l16 sav", "sav", T.SAV[:], lf(16, 2), T.SAV[:], OP.add)
        if not last:
            ts(16, "i10", "i14", li(14), li(10), 511, OP.bitwise_and)
            act(32, "i13 i14", "ch", T.CH[:], li(13, 2))
            act(16, "i14", "s20", T.S2[:, 0, :], li(14))
            tt(32, "i14 idx", "s21", T.S2[:, 1, :], li(14), T.IDX[:], OP.not_equal)
            act(16, "ss0", "sw", T.SW[:], T.SS[:, 0:16], scale=float(1 << 24))
            act(-256, "skv0 skv1 ch", "vc", T.VC[:], T.SKV[:].indirect(T.CH[:, 0:16]))
            act(256, "vc", "rvc", T.RVC[:], T.VC[:], AF.Relu, bias=float(-2 * B))
            calls = [(T.PH[:, :, :, q], T.TQ[:, 128 * q:128 * q + 128], T.S2[:, 0:2, :], q == 0, False) for q in range(16)]
            mms(1024, "s20 s21 tq0 tq1 tq2 tq3", "PH0 PH1 @w", calls)
            mms(512, "w f16 rvc", "PH1 @w", [(T.PH[:, 1], ID, T.F16[:], False, False), (T.PH[:, 1], ID, T.RVC[:], False, True)])
            free = dict(scale=-float(1 << 24), bias=float(B))
            act(256, "PH1", "fr16", T.FR16[:], T.PH[:, 1], AF.Identity, **free)
            tt(256, "PH0 vc", "PV1 PVk0 PVk1", PV1, T.PH[:, 0], T.VC[:], OP.add)
            spread("sw", "PS1 @w", lambda q: T.PS[:, 256 + q:512:16], T.SW[:], False)
            if t == RO - 2:
                act(256, fo, "fi", T.FI[:], F[:, 0:256])
                act(256, fo, "PV0", PV0, F[:, 0:256])
                ts(256, "fi", "fq", T.FQ[:], T.FI[:], 1023, OP.bitwise_and)
                tt(256, "PV0 fq", "yo", T.YO[:], PV0, T.FQ[:], OP.add)
                tt(256, "PS1 yo", "base", T.BASE[:], PS1, T.YO[:], OP.min)
            else:
                tt(256, "PS1 yb", "base", T.BASE[:], PS1, T.YB[:], OP.min)
            mms(1024, "idf base", "PS0", [(PS0, T.IDF[:], T.BASE[:], True, False)])
            act(16, "PG1", "i3", li(3), T.PG[:, 256:272])
            ts(16, "i3", "i4", li(4), li(3), 1, OP.bitwise_and)
            tt(32, "i4 ramp8", "rs7", T.RS7[:, 0::16], li(4), T.RAMP[:, 16:32], OP.add)
            saved_derived()
    spread("ss1", "PH0", lambda q: T.PH[:, 0, :, q], T.SS[:, 16:32], True)
    act(256, "yo", "PX1", T.PX[:, 256:512], T.YO[:], AF.Relu, bias=float(-B - 606239))
    tt(256, "PH0 eq", "nm", T.NM[:], T.PH[:, 0], T.EQ[:], OP.max)
    tt(256, "PX1 nm yo", "yo", T.YO[:], T.PX[:, 256:512], T.NM[:], OP.subtract)
    load("sync", T.yf[:], T.YO[:], "out", "yf", 1.9, "yo")

    ts(16, "i10", "i11", li(11), li(10), (1 << 19) - 1, OP.bitwise_and)
    for j, (key, src) in enumerate((("i11 i12", li(11, 2)), ("sav", T.SAV[:]))):
        if j:
            ts(32, key + " mu0", "fld%d0" % j, T.FLD[:, 2 * j:2 * j + 2, 0, :], src, T.MU[:, 0:1], OP.mult)
        else:
            act(32, key + " mu0", "fld%d0" % j, T.FLD[:, 2 * j:2 * j + 2, 0, :], src, AF.Identity, scale=T.MU[:, 0:1])
        act(32, key + " mu1", "fld%d1" % j, T.FLD[:, 2 * j:2 * j + 2, 1, :], src, AF.Identity, scale=T.MU[:, 1:2])
        run("v", V.transpose, "fld%d0 fld%d1" % (j, j), "flt%d" % j, us(64), T.FLT[:, 2 * j:2 * j + 2], T.FLD[:, 2 * j:2 * j + 2])
        tt(64, "flt%d" % j, "fo%d" % j, T.FO[:, 2 * j:2 * j + 2, :], T.FLT[:, 2 * j:2 * j + 2, 0, :], T.FLT[:, 2 * j:2 * j + 2, 1, :], OP.add)
    for j, y in enumerate((T.yc, T.yg, T.ysg, T.yk)):
        load("sync" if j % 2 else "s", y[:], T.FO[:, j, :], "out", "y%d" % j, 1.9, "fo%d" % (j // 2))
    def keep(line, lo, hi, kind="hint"):
        at = [[n for n in range(lo, hi) if nodes[n]["name"] == k][:1] for k in line.split()]
        at = [a[0] for a in at if a]
        for a, b in zip(at, at[1:]):
            if nodes[a]["q"] == nodes[b]["q"]:
                nodes[b][kind] |= set([a]) - nodes[b]["deps"] - nodes[b]["soft"]
    for line in FIRST:
        keep(line, 0, len(nodes), "soft")
    marks.append(len(nodes))
    for t in range(RO):
        if t:
            a = [n for n in range(marks[t], marks[t + 1]) if nodes[n]["name"] == "i1"][-1]
            [x for x in nodes[marks[t + 1]:] if x["name"] == "cg_0"][0]["hint"].add(a)
        for line in ("fl col f16", "col f%do" % (t + 1), "col i3"):
            keep(line, marks[t + 1], marks[t + 2], "soft")
        for line in EACH:
            keep(line.replace("#", str(t)).replace("+", str(t + 1)), marks[t + 1], marks[t + 2])
    cnt, seen = issue()
    g.sync.wait_ge(T.sem.out, cnt["out"])
    g.wait_ge(T.sem.sent, sent)
    for q in ("v", "s", "pe", "gq"):
        g.sync.wait_ge(T.sem[q], cnt[q])
    for sm in LOADS:
        if not any(k[1] == sm for k in seen):
            g.sync.wait_ge(T.sem[sm], 16)
